import numpy as np, ml_dtypes
CORES = [9,25,41,57]
N = 4
BF = ml_dtypes.bfloat16
def gentries(a):
    return np.ascontiguousarray(a.reshape(8, 16, -1).transpose(0, 2, 1)).reshape(8, -1)
def gtable(e):
    e = np.asarray(e); return np.ascontiguousarray(e.reshape(8, -1, 16).transpose(0, 2, 1)).reshape(128, -1).astype(np.int32)
V, NB, S0, T, RO = 2048, 3072, 512, 256, 4
def dist(b, c, v):
    pk = np.take_along_axis(b, c.reshape(N, 8, 1, 16 * T), 3).reshape(N, 8, 16, 16, T)
    return np.add.reduce(np.abs(pk - v[:, :, :, None, :]), axis=2)
def parts(rng):
    c = rng.integers(0, NB, (N, 8, 16, V)); p = rng.integers(0, V, (N, 8, 16, V)); sh = rng.integers(0, S0, (N, 8, V))
    b = rng.integers(0, 256, (N, 8, 16, NB)); h = rng.integers(600, 1150, (N, 8, 1, S0)) + rng.integers(-100, 101, (N, 8, 16, S0))
    v = rng.integers(0, 256, (N, 8, 16, T)); o = rng.integers(0, V, (N, 8, T)); dr = rng.integers(0, 256, (N, 8, 16, RO))
    return c, p, sh, b, h, v, o, dr
def apart(rng, sh):
    o = np.ascontiguousarray(np.argsort(rng.random((N, 8, V)), axis=-1)[..., :T]); lab = np.ascontiguousarray(np.argsort(rng.random((N, 8, S0)), axis=-1)[..., :T])
    np.put_along_axis(sh, o, lab, 2)
    return o, lab
def back(a):
    return np.swapaxes(a.reshape(N, N, T // N), 0, 1).reshape(N, T)
def trail(rng, g, c, p, sh, b, h, v, o):
    k = rng.integers(0, 3, (N, 1, V)); at = np.zeros((RO, N, T), np.int64); j = np.arange(RO * T); i = np.arange(T); m1 = min(S0, 2 * T)
    for q in range(N):
        u = rng.permutation(V)[:RO * T]; m = rng.permutation(S0)[:m1]
        at[:, q] = u.reshape(RO, T); sh[q, g, u] = m[j % m1]; k[q, 0, u] = j // m1
        if S0 == T and q % 2:
            x = u[T:2 * T]; sh[q, g, x] = m[i % (T // 2)]; k[q, 0, x] = 1 + i // (T // 2)
            at[2, q, :T // 2] = x[T // 2:]; k[q, 0, at[2, q, T // 2:]] = 1
    for t in range(RO - 1):
        to = back(at[t + 1])
        for q in range(N): p[q, g][:, at[t, q]] = to[q]
    b[:, g] = rng.integers(0, 64, (N, 16, NB)) + 32 + 80 * (np.arange(NB) % 3)
    c[:, g] = 3 * rng.integers(0, NB // 3, (N, 16, V)) + k
    v[:, g] = v[:, g] >> 4; h[:, g] = 0; o[:, g] = at[0]
def pack(c, p, sh, b, h, v, o, dr):
    def bf(x): return np.ascontiguousarray(x.reshape(N, 128, -1)).astype(np.float32).astype(BF)
    return {"rec": (p * 4096 + c).reshape(N, 128, V).astype(np.int32), "shp": sh.astype(np.int32), "box": bf(b), "bound": h.reshape(N, 128, S0).astype(np.int32),
            "tv": bf(v), "ob": np.stack([gtable(a) for a in o]), "dr": bf(dr)}
def setup_inputs(rng):
    return pack(*parts(rng))
def setup_inputs_ties(rng):
    c, p, sh, b, h, v, o, dr = parts(rng); o, lab = apart(rng, sh)
    c[:, :, 8:] = c[:, :, 7::-1].copy()
    v[..., :1] = np.take_along_axis(b, np.take_along_axis(c[:, :, 5], o[..., :1], 2)[:, :, None, :], 3)
    e = dist(b, np.take_along_axis(c, o[:, :, None, :], 3), v)
    m = rng.integers(0, 4, (N, 8, 1, T)); row = np.arange(16)[:, None]
    hit = np.where(m == 1, rng.random(e.shape) < 0.2, np.where(m == 2, row == 15, (m == 3) & (row == 0)))
    np.put_along_axis(h, lab[:, :, None, :] + np.zeros((1, 1, 16, 1), np.int64), np.maximum(e - 1 + hit, 0), 3)
    return pack(c, p, sh, b, h, v, o, dr)
def setup_inputs_crowd(rng):
    c, p, sh, b, h, v, o, dr = parts(rng); k = rng.permutation(V)[:12].reshape(4, 3); k[0] = k[0, 0]
    for j in range(4):
        o[:, 2 * j] = k[j][rng.integers(0, 3, (N, T))]; p[:, 2 * j] = k[j][rng.integers(0, 3, (N, 16, V))]
    sh[:, 1::2] = rng.choice(np.array([0, S0 - 1, S0 // 2]), (N, 4, V)); sh[:, 3] = rng.integers(0, S0, (N, 1))
    z = [1, 5, 7]
    b[:, z] = b[:, z] >> 3; v[:, z] = v[:, z] >> rng.integers(0, 4, (N, 3, 1, T)); h[:, z] = h[:, z] // 8
    return pack(c, p, sh, b, h, v, o, dr)
def setup_inputs_thin(rng):
    c, p, sh, b, h, v, o, dr = parts(rng); s2 = sh.copy(); o2, lab = apart(rng, s2)
    o[:, 3] = o2[:, 3]; sh[:, 3] = s2[:, 3]
    b[:, 3] = np.maximum(b[:, 3], 1); v[:, 3] = 0
    h[:, 0] = 0; h[:, 1] = 4080; h[:, 2, :, ::2] = 0; h[:, 2, :, 1::2] = 4080; h[:, 3] = 0
    h[:, 4] = 0; h[:, 4, 15] = 4080; h[:, 5] = 0; h[:, 5, 0] = 4080
    b[:, 6] = b[:, 6] >> (3 + np.arange(N) % 5)[:, None, None]; v[:, 6] = 255 - (v[:, 6] >> rng.integers(3, 8, (N, 1, T)))
    trail(rng, 7, c, p, sh, b, h, v, o)
    return pack(c, p, sh, b, h, v, o, dr)
def setup_inputs_ends(rng):
    c, p, sh, b, h, v, o, dr = parts(rng)
    c[:, ::3] = rng.choice(np.array([0, NB - 1]), (N, 3, 16, V)); p[:, 1:6:2] = rng.choice(np.array([0, V - 1]), (N, 3, 16, V))
    sh[:, 2:6:3] = rng.choice(np.array([0, S0 - 1]), (N, 2, V)); o[:, :3] = rng.choice(np.array([0, V - 1]), (N, 3, T))
    b[:, 4] = 0; v[:, 4] = 255; h[:, 4] = rng.choice(np.array([4079, 4080]), (N, 16, S0), p=np.array([0.96, 0.04]))
    b[:, 7] = rng.choice(np.array([0, 255]), (N, 16, NB)); v[:, 7] = rng.choice(np.array([0, 255]), (N, 16, T)); h[:, 7] = rng.integers(1000, 2100, (N, 16, S0))
    dr[:, ::2] = rng.choice(np.array([0, 255]), (N, 4, 16, RO))
    return pack(c, p, sh, b, h, v, o, dr)
def setup_inputs_spread(rng):
    c, p, sh, b, h, v, o, dr = parts(rng)
    b = b >> rng.integers(0, 8, (N, 8, 1, NB)); v = v >> rng.integers(0, 8, (N, 8, 1, T)); dr = dr >> rng.integers(0, 8, (N, 8, 1, RO))
    h = np.minimum(np.exp2(12 * rng.random((N, 8, 1, S0))) * (0.5 + rng.random((N, 8, 16, S0))), 4080).astype(np.int64)
    c = (NB * rng.random(c.shape) ** 2).astype(np.int64); p = (V * rng.random(p.shape) ** 3).astype(np.int64)
    sh = (S0 * rng.random(sh.shape) ** 2).astype(np.int64); o = (V * rng.random(o.shape) ** 3).astype(np.int64)
    return pack(c, p, sh, b, h, v, o, dr)
def check_inputs(d):
    bad = []
    for k, lo, hi in (("rec", 0, 4096 * V - 1), ("shp", 0, S0 - 1), ("box", 0, 255), ("bound", 0, 4080), ("tv", 0, 255), ("ob", 0, V - 1), ("dr", 0, 255)):
        x = np.asarray(d[k]).astype(np.float64)
        if not (np.min(x) >= lo and np.max(x) <= hi and np.all(np.floor(x) == x)): bad.append("range of " + k)
    if np.max(np.asarray(d["rec"]).astype(np.int64) & 4095) >= NB: bad.append("box numbers of rec")
    return bad
def reference(rec, shp, box, bound, tv, ob, dr):
    w = rec.astype(np.int64).reshape(N, 8, 16, V); sh = shp.astype(np.int64)
    b = np.zeros((N, 8, 16, NB + RO * T), np.int64); b[..., :NB] = box.astype(np.float32).astype(np.int64).reshape(N, 8, 16, NB)
    h = np.zeros((N, 8, 16, S0 + RO * T), np.int64); h[..., :S0] = bound.astype(np.int64).reshape(N, 8, 16, S0)
    nx = np.tile(np.arange(S0 + RO * T), (N, 8, 1))
    v = tv.astype(np.float32).astype(np.int64).reshape(N, 8, 16, T); o = np.stack([gentries(a) for a in ob]).astype(np.int64)
    drift = dr.astype(np.float32).astype(np.int64).reshape(N, 8, 16, RO)
    for t in range(RO):
        s = np.take_along_axis(sh, o, 2); n = np.take_along_axis(nx, s, 2)
        x = np.take_along_axis(w, o[:, :, None, :], 3)
        x = np.where((n != s)[:, :, None, :], np.roll(x, -1, axis=2), x)
        c = x & 4095; p = x >> 12; e = dist(b, c, v)
        hn = np.take_along_axis(h, n[:, :, None, :], 3); fit = e <= hn; has = np.any(fit, axis=2)
        a = np.where(has, np.argmax(fit, axis=2), np.argmin(e, axis=2))[:, :, None, :]
        ba = np.take_along_axis(b, np.take_along_axis(c, a, 2), 3); go = np.take_along_axis(p, a, 2)[:, :, 0]; hs = has[:, :, None, :]
        y = np.where((np.arange(16)[:, None] == a) & hs, p * 4096 + NB + T * t + np.arange(T), x)
        b[..., NB + T * t:NB + T * (t + 1)] = np.where(hs, (ba + v) >> 1, 0)
        makes = ~has & (np.take_along_axis(nx, n, 2) == n); wider = np.maximum(hn, e)
        for q in range(N):
            for g in range(8):
                i = np.unique(o[q, g], return_index=True)[1]
                w[q, g][:, o[q, g, i]] = y[q, g][:, i]; sh[q, g, o[q, g, i]] = n[q, g, i]
                j = np.flatnonzero(makes[q, g]); j = j[np.unique(n[q, g, j], return_index=True)[1]]
                h[q, g][:, S0 + T * t + j] = wider[q, g][:, j]; nx[q, g, n[q, g, j]] = S0 + T * t + j
        v = np.where(hs, (ba + drift[..., t:t + 1]) & 255, v); o = go
        if t < RO - 1:
            v = np.swapaxes(v.reshape(N, 8, 16, N, T // N), 0, 3).reshape(N, 8, 16, T)
            o = np.swapaxes(o.reshape(N, 8, N, T // N), 0, 2).reshape(N, 8, T)
    return {"yr": w.reshape(N, 128, V).astype(np.float32), "yh": h[..., S0:].reshape(N, 128, RO * T).astype(np.float32), "yv": v.reshape(N, 128, T).astype(np.float32).astype(BF)}

@@ -1,0 +1,584 @@
+import math
+from concourse.bass import DstId, RemoteDMATransfer
+from concourse.mybir import AluOpType, ActivationFunctionType
+
+ALU = AluOpType
+AF = ActivationFunctionType
+
+V, NB, S0, TH, RO = 2048, 3072, 512, 256, 4
+ND = [16, 16]
+NM = [0, 0]
+POOL = True
+SPLIT = False
+SPLIT2 = False
+DB = ["ps0", "ps1", "ps4"]
+GC, SC, LAT, PEC, CYC, REM, KB = 1.56, 3.8, 110.0, 0.52, 1.04, 3000.0, 4.0
+ROUNDS, NOISE, AHEAD = 1000, 1500.0, 0.5
+EQW = sum(256 - 16 * c for c in range(16))
+MAG = 12582912.0
+BIG = 2.0 ** 93
+LR, L0 = math.log(1.7), 63.0
+
+F32, BF, F16, I32, U16 = "float32", "bfloat16", "float16", "int32", "uint16"
+SCRATCH = {}
+
+
+def _sb(names, cols, dt):
+    for n in names.split():
+        SCRATCH[n] = ("sbuf", [128] + (list(cols) if isinstance(cols, (list, tuple)) else [cols]), dt)
+
+
+_sb("rect shpi", V, I32)
+_sb("shph", V, F16)
+_sb("recf shpt", V + TH, F32)
+_sb("boxt X", 4096, BF)
+_sb("Dab", [32, 128], BF)
+_sb("bnd", S0, I32)
+_sb("ht", 1536, F32)
+_sb("nxt", 1536 + TH, F32)
+_sb("ident", V, F32)
+_sb("obi pci", 16, I32)
+_sb("tvb", [4, 64], BF)
+_sb("drb", 8, BF)
+_sb("land0 land1 land2 land3 send0 send1 send2", [4, 72], F16)
+_sb("ol16 sl16 nl16 xl16 offo offn", 16, U16)
+_sb("cl16", TH, U16)
+_sb("ol32 nl32 xm of32 on32 askw wo wn il", 16, F32)
+_sb("kc", 96, F32)
+_sb("Wi c32 p32", TH, I32)
+_sb("c16 p16 s16 n16 orow Y16 m16 hn hr B1 hold sc", TH, F16)
+_sb("sel", 512, F16)
+_sb("rot nf OHT nhm q Da nfr Fo Fn yvb ones irow thr keep Ls", TH, BF)
+_sb("Hs W1 Ws d0f d0r tt fs Z a1", TH, F32)
+_sb("eqo eqn", EQW, BF)
+_sb("col", 64, F32)
+_sb("rowg rowr tm If5 RTI", 128, F32)
+_sb("Ib nIb I5 I12 nI13 I23 nI11 BIb nhI BO nBO nBO12 E8 RmI RTb Dc Vm0 Vm1", 128, BF)
+_sb("Mall", 144, BF)
+_sb("G32 G64 nG32 G13 S16", 8, BF)
+for _k in range(8):
+    SCRATCH["ps%d" % _k] = ("psum", [128, 512], F32)
+
+DMAS = ["d_ob", "d_tv", "d_dr", "d_rec", "d_shp", "d_box", "d_bnd", "d_yh0", "d_yh1", "d_yh2", "d_yh3", "d_yv", "d_yr0", "d_yr1"]
+SEMAPHORES = ["cv", "ca", "cp", "cg", "sent"] + ["arr%d%d" % (t, k) for t in range(1, RO) for k in range(2)] + DMAS
+ENG_SEM = {"v": "cv", "a": "ca", "p": "cp", "g": "cg"}
+
+
+def lanes(topo, cores, src, dst):
+    en = topo.engines(cores[src], cores[dst])
+    if src // 2 == dst // 2:
+        return en
+    m = len(en) // 2
+    return en[(dst % 2) * m:(dst % 2 + 1) * m]
+
+
+def build(g, core, T, topo, rank):
+    ops = []
+    cores = T.cores
+    Q = {"v": g.vector, "a": g.scalar, "p": g.tensor, "g": g, "s": g.sync}
+
+    def A(name, lo=None, hi=None, step=1):
+        if lo is None:
+            return (T[name][:], (name, 0, 1 << 20))
+        return (T[name][:, lo:hi:step] if step != 1 else T[name][:, lo:hi], (name, lo, hi))
+
+    def AR(name, lo, hi):
+        return (T[name][:, hi - 1::-1] if lo == 0 else T[name][:, hi - 1:lo - 1:-1], (name, lo, hi))
+
+    def M(name, q0, q1, lo, hi):
+        w = SCRATCH[name][1][2]
+        pat = T[name][:, q0, lo:hi] if q1 == q0 + 1 else T[name][:, q0:q1, lo:hi]
+        return (pat, (name, q0 * w + lo, (q1 - 1) * w + hi))
+
+    def P8(name, lo, hi):
+        return (T[name][0:8, lo:hi], (name, lo, hi))
+
+    def IND(win, off):
+        return (win[0].indirect(off[0]), win[1], off[1])
+
+    def op(eng, fn, rd, wr, dur, sem=None, inc=1, lat=0.0):
+        r = []
+        for x in rd:
+            if isinstance(x, tuple):
+                r.extend(x[1:])
+        w = []
+        for x in wr:
+            w.append(x[1])
+            r.extend(x[2:])
+        ops.append({"e": eng, "fn": fn, "r": r, "w": w, "dur": dur, "sem": sem, "inc": inc, "lat": lat})
+
+    def ap(x):
+        return x[0] if isinstance(x, tuple) else x
+
+    def two(x):
+        return SCRATCH[x[1][0]][2] in (BF, F16, U16)
+
+    def cost(eng, n, out, ins, k=None):
+        if len(out) == 3:
+            return 55.0 + n * SC * CYC
+        if len(ins[0]) == 3:
+            return (55.0 if eng == "v" else 70.0) + n * GC * CYC
+        if k is None:
+            k = 0.5 if (eng == "v" and two(out) and all(two(x) for x in ins)) else 1.0
+        return max(64.0, n * k) * CYC
+
+    def cp(out, in_, n):
+        op("v", lambda: g.vector.tensor_copy(out[0], in_[0]), [in_], [out], cost("v", n, out, [in_]))
+
+    def ts(out, in_, n, s1, o0, s2=None, o1=None):
+        if o1 is None:
+            fn = lambda: g.vector.tensor_scalar(out[0], in_[0], ap(s1), None, o0)
+        else:
+            fn = lambda: g.vector.tensor_scalar(out[0], in_[0], ap(s1), ap(s2), o0, o1)
+        op("v", fn, [in_, s1, s2], [out], cost("v", n, out, [in_]))
+
+    def tt(out, a, b, n, o):
+        ps = a[1][0].startswith("ps") or b[1][0].startswith("ps")
+        op("v", lambda: g.vector.tensor_tensor(out[0], a[0], b[0], o), [a, b], [out], cost("v", n, out, [a, b], 1.0 if ps else 2.0))
+
+    def scan(out, d0, d1, n, o0=ALU.add, o1=ALU.min):
+        op("v", lambda: g.vector.tensor_tensor_scan(out[0], d0[0], d1[0], 0.0, o0, o1), [d0, d1], [out], cost("v", n, out, [d0, d1]))
+
+    def act(out, in_, n, f, bias=0.0, scale=1.0, extra=0.0):
+        op("a", lambda: g.scalar.activation(out[0], in_[0], f, bias=bias, scale=ap(scale)), [in_, scale], [out], cost("a", n, out, [in_]) + extra)
+
+    def iota(out, pat, base, cm, n):
+        if SCRATCH[out[1][0]][2] == I32:
+            fn = lambda: g.iota(out[0], pat, base, cm)
+        else:
+            fn = lambda: g.iota(out[0], pat, base, cm, allow_small_or_imprecise_dtypes=True)
+        op("g", fn, [], [out], 160.0 + 2 * n * CYC)
+
+    def conv(out, in_, n):
+        if POOL:
+            op("g", lambda: g.affine_select(out[0], in_[0], [[0, n]], ALU.is_equal, 0.0, 0, 0), [in_], [out], 210.0 + 2 * n * CYC)
+        else:
+            cp(out, in_, n)
+
+    def mm(lst):
+        def fn():
+            h = None
+            for (o, l, r, n, st, sp) in lst:
+                h = g.tensor.matmul(o[0], l[0], r[0], st, sp)
+            return h
+        dur = sum(max(64, n) * (4 if SCRATCH[l[1][0]][2] == F32 else 1) for (o, l, r, n, st, sp) in lst) * PEC + 30.0
+        op("p", fn, [x[1] for x in lst] + [x[2] for x in lst], [x[0] for x in lst], dur)
+
+    def grp(out, terms, n, start=True, stop=True):
+        return [(out, l, r, n, start and k == 0, stop and k == len(terms) - 1) for k, (l, r) in enumerate(terms)]
+
+    def dma(eng, sem, out, in_, kb):
+        op(eng, lambda: Q[eng].dma_start(out[0], in_[0]), [in_], [out], 60.0, sem=sem, inc=16, lat=2000.0 + kb * KB)
+
+    def H(t):
+        return (t, ("hbm", 0, 0))
+
+    for eng, sem, dst, src, kb in (("s", "d_ob", A("obi"), T.ob[:], 8), ("a", "d_shp", P8("shpi", 0, V), T.shp[:], 128), ("s", "d_rec", A("rect"), T.rec[:], 1100),
+                                   ("a", "d_tv", A("tvb"), T.tv[:], 64), ("a", "d_dr", A("drb", 0, 4), T.dr[:], 1),
+                                   ("s", "d_box", A("boxt", 0, NB), T.box[:], 1900), ("s", "d_bnd", A("bnd"), T.bound[:], 2150)):
+        dma(eng, sem, dst, H(src), kb)
+        ops[-1]["w"].append(("turn" + eng, 0, 1))
+
+    iota(A("pci", 0, 1), [[1, 1]], 0, 1, 1)
+    iota(A("ident", 0, TH), [[1, TH]], 0, 0, TH)
+    iota(A("rowg"), [[16, 8], [0, 16]], 0, 0, 128)
+    for k in range(3):
+        iota(A("nxt", 512 * k, 512 * k + 512), [[1, 512]], 512 * k, 0, 512)
+    for k in range(4):
+        lo, hi = TH + 448 * k, TH + 448 * (k + 1)
+        iota(A("ident", lo, hi), [[1, hi - lo]], lo, 0, hi - lo)
+    C = {n: A("col", 4 * k, 4 * k + 1) for k, n in enumerate("pc rc gc nc pvc dc gm p16 hc r1".split())}
+    rowm, rowx, row8 = A("ident", 0, 128), A("ident", 0, 144), A("ident", 0, 128, 16)
+    ts(A("pci", 4, 5), A("pci", 0, 1), 1, 15, ALU.bitwise_and)
+    cp(C["pc"], A("pci", 0, 1), 1)
+    cp(C["rc"], A("pci", 4, 5), 1)
+    tt(C["gc"], C["pc"], C["rc"], 1, ALU.subtract)
+    ts(C["nc"], C["rc"], 1, 15.0, ALU.is_equal, -16.0, ALU.mult)
+    ts(C["nc"], C["nc"], 1, C["pc"], ALU.add, 1.0, ALU.add)
+    ts(C["pvc"], C["rc"], 1, 0.0, ALU.is_equal, 16.0, ALU.mult)
+    ts(C["dc"], C["pvc"], 1, -1.0, ALU.mult, 1.0, ALU.add)
+    ts(C["pvc"], C["pvc"], 1, C["pc"], ALU.add, -1.0, ALU.add)
+    ts(C["gm"], C["gc"], 1, 15.0, ALU.add)
+    ts(C["p16"], C["pc"], 1, 16.0, ALU.mult)
+    ts(C["r1"], C["rc"], 1, 1.0, ALU.add)
+    ts(C["hc"], C["rc"], 1, 15.0, ALU.not_equal, 2048.0, ALU.mult)
+    ts(A("Ib"), rowm, 128, C["pc"], ALU.is_equal)
+    for n, s in (("nIb", -1.0), ("If5", 1.0 / 32), ("I5", 32.0), ("I12", 4096.0), ("nI13", -8192.0), ("I23", 2.0 ** 23),
+                 ("nI11", -2048.0), ("BIb", BIG), ("nhI", -0.5), ("Dc", C["dc"])):
+        act(A(n), A("Ib"), 128, AF.Identity, scale=s)
+    ts(A("Mall"), rowx, 144, C["gm"], ALU.is_equal)
+    ts(A("BO"), A("rowg"), 128, C["gc"], ALU.is_equal)
+    act(A("nBO"), A("BO"), 128, AF.Identity, scale=-1.0)
+    act(A("nBO12"), A("BO"), 128, AF.Identity, scale=-4096.0)
+    ts(A("E8"), A("rowg"), 128, C["p16"], ALU.is_equal)
+    for k in range(4):
+        lo, hi = 512 * k, 512 * k + 512
+        cp(P8("shph", lo, hi), P8("shpi", lo, hi), 512)
+        mm([(A("ps%d" % k), P8("E8", 0, 128), P8("shph", lo, hi), 512, True, True)])
+        act(A("shpt", lo, hi), A("ps%d" % k), 512, AF.Copy)
+    tt(A("rowr"), rowm, A("rowg"), 128, ALU.subtract)
+    ts(A("G32"), row8, 8, C["gc"], ALU.is_equal, 32.0, ALU.mult)
+    ts(A("G13"), row8, 8, C["gc"], ALU.is_equal, 8192.0, ALU.mult)
+    ts(A("S16"), row8, 8, C["pc"], ALU.is_equal, 16.0, ALU.mult)
+    if max(NM):
+        ts(A("G64"), row8, 8, C["gc"], ALU.is_equal, 64.0, ALU.mult)
+        ts(A("nG32"), row8, 8, C["gc"], ALU.is_equal, -32.0, ALU.mult)
+    for k in range(2):
+        if NM[k]:
+            ts(A("Vm%d" % k), A("rowr"), 128, float(NM[k]), ALU.is_lt, 32.0, ALU.mult)
+            tt(A("Vm%d" % k), A("Vm%d" % k), A("nBO"), 128, ALU.mult)
+    ts(A("RmI"), rowm, 128, C["nc"], ALU.is_equal, 32.0, ALU.mult)
+    tt(A("RmI"), A("RmI"), A("I5"), 128, ALU.subtract)
+    ts(A("RTb"), rowm, 128, C["pvc"], ALU.is_equal)
+    tt(A("RTb"), A("RTb"), A("Ib"), 128, ALU.subtract)
+    act(A("RTI"), A("RTb"), 128, AF.Copy)
+    ts(A("tm"), A("rowr"), 128, C["rc"], ALU.not_equal, 1.0e7, ALU.mult)
+    act(A("Z", 0, 128), A("tm"), 128, AF.Identity, scale=64 * BIG / 1.0e7)
+    act(A("tm"), A("tm"), 128, AF.Identity, bias=16.0)
+    ts(A("Y16", 0, 128), A("rowr"), 128, C["rc"], ALU.is_equal, 8192.0, ALU.mult)
+    ts(A("m16", 0, 128), A("rowr"), 128, C["r1"], ALU.is_equal, -2048.0, ALU.mult)
+    ts(A("il"), A("ident", 0, TH, 16), 16, C["rc"], ALU.add)
+    for k, off in enumerate([NB - 2048 + TH * t for t in range(RO)] + [V, 1536]):
+        act(A("kc", 16 * k, 16 * k + 16), A("il"), 16, AF.Identity, bias=float(off))
+    act(A("ones"), A("ident", 0, TH), TH, AF.Identity, bias=1.0, scale=0.0)
+    act(A("irow"), A("ident", 0, TH), TH, AF.Copy)
+    act(A("a1"), A("ident", 0, TH), TH, AF.Exp, bias=L0 + math.log(2.56), scale=-LR, extra=1400.0)
+    act(A("wo"), A("il"), 16, AF.Exp, bias=L0, scale=-LR)
+    act(A("wn"), A("il"), 16, AF.Exp, bias=L0 - math.log(8192.0), scale=-LR)
+    for h in range(2):
+        tt(A("hold", 128 * h, 128 * h + 128), A("Y16", 0, 128), A("m16", 0, 128), 128, ALU.add)
+        tt(A("thr", 128 * h, 128 * h + 128), A("a1", 128 * h, 128 * h + 128), A("Z", 0, 128), 128, ALU.add)
+        act(A("keep", 128 * h, 128 * h + 128), A("rowr"), 128, AF.Sign)
+    act(A("d0f"), A("ident", 0, TH), TH, AF.Identity, bias=-1.0, scale=0.0)
+    act(A("d0f", 0, TH, 16), A("il"), 16, AF.Identity, bias=1.0e6, scale=0.0)
+    act(A("d0r"), A("ident", 0, TH), TH, AF.Identity, bias=1.0, scale=0.0)
+    act(A("d0r", 15, TH, 16), A("il"), 16, AF.Identity, bias=1.0e6, scale=0.0)
+    cp(M("land0", 0, 4, 0, 64), A("tvb"), TH)
+    conv(A("ht", 0, S0), A("bnd"), S0)
+    for k in range(4):
+        conv(A("recf", 512 * k, 512 * k + 512), A("rect", 512 * k, 512 * k + 512), 512)
+
+    def tolist(out, buf, lo, hi):
+        n = (hi - lo) // 16
+        return [(out, A("Mall", 15 - r, 143 - r), A(buf, lo + r, hi, 16), n, r == 0, False) for r in range(16)]
+
+    eoff = [sum(256 - 16 * k for k in range(c)) for c in range(17)]
+
+    def pairs(buf, row, keys, wts, cs, last):
+        for c0 in range(0, len(cs), 4):
+            part = cs[c0:c0 + 4]
+            for c in part:
+                ts(A(buf, eoff[c], eoff[c + 1]), A(row, 16 * c, TH), TH - 16 * c, A(keys, c, c + 1), ALU.is_equal, A(wts, c, c + 1), ALU.mult)
+            mm([(A("ps6", 16 * c, TH), A("BO"), A(buf, eoff[c], eoff[c + 1]), TH - 16 * c, False, last and c == cs[-1]) for c in part])
+
+    def places(out, flags, keys, spare):
+        scan(A("Ls"), A("keep"), A(flags), TH, ALU.mult, ALU.max)
+        tt(A("of32"), A("Ls", 15, TH, 16), spare, 16, ALU.mult)
+        tt(A("on32"), A("of32"), A(keys), 16, ALU.max)
+        cp(A(out), A("on32"), 16)
+
+    own = rank // 2
+    horder = [1 - own, own]
+    halves = [(128 * h, 128) for h in horder]
+    for t in range(RO):
+        last = t == RO - 1
+        land, nb, ns = "land%d" % t, NB + TH * t, S0 + TH * t
+        drc = A("drb", t, t + 1)
+        hs = lambda n, h, w=128: A(n, w * h, w * h + w)
+        EB = lambda h, k: A("ps%d" % (2 + h), 128 * k, 128 * k + 128)
+        DA = lambda h, a0, a1, lo, hi: M("Dab", 16 * h + a0, 16 * h + a1, lo, hi)
+        for h in horder:
+            if t == 0:
+                cp(hs("ol16", h, 8), hs("obi", h, 8), 8)
+                ts(hs("c32", h), IND(A("rect"), hs("ol16", h, 8)), 128, 4095, ALU.bitwise_and)
+            else:
+                cp(hs("ol16", h, 8), M(land, 2 * h, 2 * h + 2, 64, 68), 8)
+                cp(hs("Wi", h), IND(A("recf", 0, V), hs("ol16", h, 8)), 128)
+                ts(hs("c32", h), hs("Wi", h), 128, 4095, ALU.bitwise_and)
+            cp(hs("cl16", h), hs("c32", h), 128)
+        for lo, n in (halves if SPLIT else [(0, TH)]):
+            R = lambda name: A(name, lo, lo + n)
+            Lc = lambda name: A(name, lo // 16, (lo + n) // 16)
+            hh = range(lo // 128, (lo + n) // 128)
+            cp(R("s16"), IND(A("shpt", 0, V), Lc("ol16")), n)
+            scan(R("sc"), R("hold"), R("s16"), n)
+            ts(Lc("sl16"), A("sc", lo + 15, lo + n, 16), n // 16, C["hc"], ALU.add)
+            cp(R("n16"), IND(A("nxt", 0, 1536), Lc("sl16")), n)
+            scan(R("sc"), R("hold"), R("n16"), n)
+            ts(Lc("nl16"), A("sc", lo + 15, lo + n, 16), n // 16, C["hc"], ALU.add)
+            mm(grp(A("ps7", lo, lo + n), [(A("Ib"), R("n16")), (A("nIb"), R("s16"))], n))
+            act(R("rot"), A("ps7", lo, lo + n), n, AF.Sign)
+            ts(R("hn"), IND(A("ht", 0, ns), Lc("nl16")), n, -2048.0, ALU.add)
+            tt(R("hr"), R("hn"), R("rot"), n, ALU.mult)
+            mm([(A("ps5", 32 + 8 * h, 40 + 8 * h), hs("rot", h), A("S16"), 8, True, True) for h in hh])
+            rt = A("ps5", 32 + lo // 16, 32 + (lo + n) // 16)
+            act(A("d0f", lo + 1, lo + n, 16), rt, n // 16, AF.Identity, bias=-1.0)
+            act(A("d0r", lo, lo + n, 16), rt, n // 16, AF.Identity, bias=1.0, scale=-1.0)
+            mm(sum([grp(A("ps7", 256 + 128 * h, 384 + 128 * h), [(hs("hn", h), A("I5")), (hs("hr", h), A("RmI"))], 128) for h in hh], []))
+            act(R("Hs"), A("ps7", 256 + lo, 256 + lo + n), n, AF.Identity, bias=65536.0)
+        cp(A("nl32"), A("nl16"), 16)
+        for lo, n in (halves if SPLIT2 else [(0, TH)]):
+            R = lambda name: A(name, lo, lo + n)
+            Lc = lambda name: A(name, lo // 16, (lo + n) // 16)
+            ts(R("c16"), R("cl16"), n, -2048.0, ALU.add)
+            if t == 0:
+                ts(R("p32"), IND(A("rect"), Lc("ol16")), n, 12, ALU.arith_shift_right)
+            else:
+                ts(R("p32"), R("Wi"), n, 12, ALU.arith_shift_right)
+            conv(R("p16"), R("p32"), n)
+            ts(A("boxt", nb + lo, nb + lo + n), M(land, lo // 64, (lo + n) // 64, 0, 64), n, drc, ALU.subtract)
+            mm(grp(A("ps7", lo, lo + n), [(A("I23"), R("rot")), (A("I12"), R("p16")), (A("Ib"), R("c16"))], n))
+            act(R("W1"), A("ps7", lo, lo + n), n, AF.Relu, bias=2048.0 - 2.0 ** 23)
+            mm(grp(A("ps7", 256 + lo, 256 + lo + n), [(A("I12"), R("p16")), (A("Ib"), R("c16")), (A("RTI"), R("W1"))], n))
+            act(R("Ws"), A("ps7", 256 + lo, 256 + lo + n), n, AF.Identity, bias=2048.0)
+            cp(Lc("ol32"), Lc("ol16"), n // 16)
+            cp(R("orow"), IND(A("ident"), Lc("ol16")), n)
+        mm(grp(A("ps6", 0, TH), [(A("nIb"), A("thr"))], TH, stop=False))
+        pairs("eqo", "orow", "ol32", "wo", [8 * h + c for h in horder for c in range(8)], True)
+        act(A("Fo"), A("ps6", 0, TH), TH, AF.Sign)
+        places("offo", "Fo", "ol32", A("kc", 64, 80))
+        tt(A("nfr"), IND(A("nxt", 0, 1536), A("nl16")), A("n16"), TH, ALU.not_equal)
+        mm(grp(A("ps6", 0, TH), [(A("nIb"), A("thr")), (A("BIb"), A("nfr"))], TH, stop=False))
+        if not last:
+            cp(IND(A("shpt"), A("offo")), A("n16"), TH)
+        for k, h in enumerate(horder):
+            nm, na = NM[k], 128 - ND[k]
+            for lo, hi in ((128 * h, 128 * h + 64), (128 * h + 64, 128 * h + na)):
+                act(A("X", 16 * lo, 16 * hi), IND(A("boxt", 0, nb), A("cl16", lo, hi)), 16 * (hi - lo), AF.Copy)
+                ops[-1]["w"].append(("turn", 0, 1))
+            if ND[k]:
+                lo, hi = 128 * h + na, 128 * h + 128
+                cp(A("X", 16 * lo, 16 * hi), IND(A("boxt", 0, nb), A("cl16", lo, hi)), 16 * ND[k])
+            if nm:
+                mm([(A("ps5", 384 + 64 * b, 448 + 64 * b), A("Ib"), M(land, 2 * h + b, 2 * h + b + 1, 0, 64), 64, True, True) for b in range(2)])
+                mm([(EB(h, 0), M(land, 2 * h, 2 * h + 2, 0, 64), A("Vm%d" % k), 128, True, False)])
+            for a in range(nm):
+                tt(DA(h, a, a + 1, 0, 128), A("X", 2048 * h + a, 2048 * h + 2048, 16), A("ps5", 384, 512), 128, ALU.max)
+            aa = list(range(nm, 16))
+            tiles = [(b, aa[j:j + 8]) for b in range(2) for j in range(0, len(aa), 8)]
+            for j, (b, part) in enumerate(tiles):
+                bank = DB[(4 * k + j) % len(DB)]
+                x0 = 2048 * h + 1024 * b
+                mm(sum([grp(A(bank, 64 * m, 64 * m + 64), [(A("Ib"), A("X", x0 + a, x0 + 1024, 16)), (A("nIb"), M(land, 2 * h + b, 2 * h + b + 1, 0, 64))], 64)
+                        for m, a in enumerate(part)], []))
+                act(DA(h, part[0], part[-1] + 1, 64 * b, 64 * b + 64), A(bank, 0, 64 * len(part)), 64 * len(part), AF.Abs)
+                ops[-1]["r"].append(("turn", 0, 1))
+                if b == 1:
+                    mm([(A("ps%d" % (2 + h), a, 128, 16), DA(h, a, a + 1, 0, 128), A("G32"), 8, not nm, not nm) for a in part])
+            for j in range(nm // 4):
+                lst = []
+                for a in range(4 * j, 4 * j + 4):
+                    eo = A("ps%d" % (2 + h), a, 128, 16)
+                    lst += [(eo, A("X", 2048 * h + a, 2048 * h + 2048, 16), A("nG32"), 8, False, False), (eo, DA(h, a, a + 1, 0, 128), A("G64"), 8, False, a == nm - 1)]
+                mm(lst)
+            tt(hs("nf", h), EB(h, 0), hs("Hs", h), 128, ALU.is_gt)
+            tt(hs("tt", h), EB(h, 0), hs("nf", h), 128, ALU.mult)
+            scan(hs("fs", h), hs("d0f", h), hs("tt", h), 128)
+            scan(AR("ps%d" % (2 + h), 128, 256), AR("d0r", 128 * h, 128 * h + 128), AR("fs", 128 * h, 128 * h + 128), 128)
+            rs = EB(h, 1)
+            tt(hs("OHT", h), rs, hs("tt", h), 128, ALU.is_equal)
+            tt(hs("nhm", h), rs, A("tm"), 128, ALU.is_ge)
+            act(hs("q", h), rs, 128, AF.Relu, bias=16.0, scale=-1.0)
+            mm(grp(A("ps5", 128, 256), [(hs("OHT", h), A("Ib"))], 128))
+            sl = 256 * h
+            tt(A("sel", sl, sl + 128), A("ps5", 128, 256), hs("c16", h), 128, ALU.mult)
+            w = 8 if last else 16
+            if not last:
+                tt(A("sel", sl + 128, sl + 256), A("ps5", 128, 256), hs("p16", h), 128, ALU.mult)
+            mm(grp(EB(h, 2), [(hs("q", h), A("Ib")), (A("Dc"), hs("rot", h))], 128))
+            act(hs("Da", h), EB(h, 2), 128, AF.Abs, bias=-16.0)
+            mm(grp(EB(h, 2), [(A("Ib"), hs("irow", h)), (A("nBO"), A("sel", sl, sl + 128)), (A("nI13"), hs("Da", h))], 128))
+            act(hs("Z", h), EB(h, 2), 128, AF.Relu, bias=float(nb - 2048))
+            tt(IND(A("recf"), hs("offo", h, 8)), hs("Ws", h), hs("Z", h), 128, ALU.add)
+            mm(tolist(A("ps5", 64, 64 + w), "sel", sl, sl + 16 * w) + [(A("ps5", 64, 72), hs("nhm", h), A("G13"), 8, False, True),
+                                                                      (A("ps5", 80, 88), hs("nhm", h), A("G13"), 8, True, True)])
+            tt(hs("xm", h, 8), A("ps5", 64, 72), A("kc", 16 * t + 8 * h, 16 * t + 8 * h + 8), 8, ALU.min)
+            ts(hs("xl16", h, 8), hs("xm", h, 8), 8, 2048.0, ALU.add)
+            ts(hs("Y16", h), IND(A("boxt", 0, nb + TH), hs("xl16", h, 8)), 128, drc, ALU.add)
+            ts(hs("m16", h), hs("Y16", h), 128, 256.0, ALU.is_ge, 256.0, ALU.mult)
+            if last:
+                tt(hs("yvb", h), hs("Y16", h), hs("m16", h), 128, ALU.subtract)
+            else:
+                snd, nxl = "send%d" % t, "land%d" % (t + 1)
+                qs = [q for q in (2 * h, 2 * h + 1) if q != rank]
+                if h != own:
+                    cp(M(snd, 2 * h, 2 * h + 2, 64, 68), A("ps5", 72, 80), 8)
+                    tt(M(snd, 2 * h, 2 * h + 2, 0, 64), hs("Y16", h), hs("m16", h), 128, ALU.subtract)
+                else:
+                    for q in qs + [rank]:
+                        dst = nxl if q == rank else snd
+                        cp(M(dst, q, q + 1, 64, 68), A("ps5", 72 + 4 * (q % 2), 76 + 4 * (q % 2)), 4)
+                        tt(M(dst, q, q + 1, 0, 64), A("Y16", 64 * q, 64 * q + 64), A("m16", 64 * q, 64 * q + 64), 64, ALU.subtract)
+
+                def send(qs=qs, snd=snd, nxl=nxl, sem="arr%d%d" % (t + 1, k)):
+                    trs = []
+                    for q in qs:
+                        rid, pid, _se = topo.addr(cores[q])
+                        trs.append(RemoteDMATransfer(dst_ids=[DstId(rid=rid, pnc=pid)], dma_engine_mask=sum(1 << e for e in lanes(topo, cores, rank, q)),
+                                                     remote_sem=T.sem[sem], src=T[snd][:, q, 0:68], dst=T[nxl][:, rank, 0:68]))
+                    g.remote_dma_fused(trs, local_sem=T.sem.sent)
+                    return None
+                op("g", send, [M(snd, q, q + 1, 0, 68) for q in qs], [(None, ("net%d" % t, k, k + 1))], 300.0, sem="none")
+                op("r", None, [(None, ("net%d" % t, k, k + 1))], [M(nxl, q, q + 1, 0, 72) for q in qs], 0.0,
+                   sem="arr%d%d" % (t + 1, k), inc=sum(len(lanes(topo, cores, q, rank)) for q in qs), lat=REM)
+            tt(hs("askw", h, 8), A("ps5", 80, 88), hs("wn", h, 8), 8, ALU.mult)
+            mm(grp(EB(h, 3), [(A("nI11"), hs("ones", h)), (hs("tt", h), A("If5"))], 128))
+            tt(hs("B1", h), EB(h, 3), hs("rot", h), 128, ALU.mult)
+            mm([(A("ps6", 128 * h, 128 * h + 128), hs("q", h), A("BIb"), 128, False, False)])
+            pairs("eqn", "n16", "nl32", "askw", list(range(8 * h, 8 * h + 8)), h == own)
+        if last:
+            dma("s", "d_yr0", H(T.yr[:, 0:V // 2]), A("recf", 0, V // 2), 1024)
+            dma("a", "d_yr1", H(T.yr[:, V // 2:V]), A("recf", V // 2, V), 1024)
+            dma("s", "d_yv", H(T.yv[:]), A("yvb"), 64)
+        else:
+            mm(grp(A("ps7", 0, TH), [(A("Ib"), A("Y16")), (A("Ib"), A("boxt", nb, nb + TH)), (A("nhI"), A("ones"))], TH))
+            act(A("a1"), A("ps7", 0, TH), TH, AF.Identity, bias=MAG, scale=0.5)
+            act(A("boxt", nb, nb + TH), A("a1"), TH, AF.Identity, bias=-MAG)
+        act(A("Fn"), A("ps6", 0, TH), TH, AF.Sign)
+        if not last:
+            places("offn", "Fn", "nl32", A("kc", 80, 96))
+            ts(IND(A("nxt"), A("offn")), A("ident", 0, TH), TH, 1.0, ALU.mult, float(ns), ALU.add)
+        for h in horder:
+            mm(grp(EB(h, 3), [(hs("tt", h), A("If5")), (A("RTb"), hs("B1", h)), (A("nBO12"), hs("Fn", h))], 128))
+            act(A("ht", ns + 128 * h, ns + 128 * h + 128), EB(h, 3), 128, AF.Relu, bias=-65536.0)
+        dma("s", "d_yh%d" % t, H(T.yh[:, TH * t:TH * t + TH]), A("ht", ns, ns + TH), 128)
+    return ops, Q
+
+
+def depend(ops):
+    hist = {}
+    bank = {}
+    deps = []
+    for i, o in enumerate(ops):
+        d = {}
+        acc = [(r, False) for r in o["r"]] + [(r, True) for r in o["w"]]
+        for (name, lo, hi), wr in acc:
+            if name == "hbm":
+                continue
+            psum = name.startswith("ps")
+            if psum and name in bank and bank[name] != i:
+                j = bank[name]
+                d[j] = d.get(j, False) or ops[j]["e"] != o["e"]
+            for (j, l2, h2, w2) in hist.get(name, []):
+                same = ops[j]["e"] == o["e"] and ops[j]["sem"] is None
+                if name.startswith("turn"):
+                    if wr or w2:
+                        d[j] = d.get(j, False)
+                elif lo < h2 and l2 < hi and (wr or w2) and (same or not psum):
+                    d[j] = d.get(j, False) or (not same) or (w2 and o["e"] != "p")
+        for (name, lo, hi), wr in acc:
+            if name.startswith("ps"):
+                if name in bank and ops[bank[name]]["e"] != o["e"]:
+                    hist[name] = []
+                bank[name] = i
+            hist.setdefault(name, []).append((i, lo, hi, wr))
+        deps.append(d)
+    for i in range(len(ops)):
+        d = deps[i]
+        for j in sorted(d, reverse=True):
+            if j in d and d[j]:
+                for k, w in deps[j].items():
+                    if k in d and (w or not d[k]):
+                        del d[k]
+    return deps
+
+
+def passes(ops, pre, post, prio, back):
+    n = len(ops)
+    left = [len(p) for p in pre]
+    est = [0.0] * n
+    start = [0.0] * n
+    ready, free, order = {}, {}, []
+    for i in range(n):
+        ready.setdefault(ops[i]["e"], [])
+        if left[i] == 0:
+            ready[ops[i]["e"]].append(i)
+            est[i] = ops[i]["lat"] if back else 0.0
+    while len(order) < n:
+        t0, e = min((max(free.get(e, 0.0), min(est[i] for i in lst)), e) for e, lst in ready.items() if lst)
+        i = max((k for k in ready[e] if est[k] <= t0 + 1e-6), key=lambda k: prio[k])
+        for k in ready[e]:
+            if est[k] > t0 and est[k] - t0 < AHEAD * ops[i]["dur"] and prio[k] > prio[i] + ops[i]["dur"]:
+                i = k
+        ready[e].remove(i)
+        start[i] = max(t0, est[i])
+        free[e] = start[i] + ops[i]["dur"]
+        order.append(i)
+        for k, gap in post[i]:
+            est[k] = max(est[k], start[i] + gap)
+            left[k] -= 1
+            if left[k] == 0:
+                ready[ops[k]["e"]].append(k)
+    fin = [start[i] + ops[i]["dur"] + (0.0 if back else ops[i]["lat"]) for i in range(n)]
+    return order, start, fin
+
+
+def schedule(ops, deps):
+    n = len(ops)
+    fpre, fpost, bpre, bpost = [[[] for _ in range(n)] for _ in range(4)]
+    for i in range(n):
+        for j, w in deps[i].items():
+            gap = ops[j]["lat"] + LAT if w else 0.0
+            fpre[i].append(j)
+            fpost[j].append((i, gap + ops[j]["dur"]))
+            bpre[j].append(i)
+            bpost[i].append((j, gap + ops[i]["dur"]))
+    prio = [0.0] * n
+    for i in range(n - 1, -1, -1):
+        prio[i] = max([prio[k] + gap for k, gap in fpost[i]] + [ops[i]["dur"] + ops[i]["lat"]])
+    seed = [12345]
+
+    def rnd():
+        seed[0] = (seed[0] * 1103515245 + 12345) % 2147483648
+        return seed[0] / 2147483648.0
+    best = None
+    for it in range(30):
+        res = passes(ops, fpre, fpost, prio, False)
+        if best is None or max(res[2]) < max(best[2]):
+            best, base = res, prio
+        prio = passes(ops, bpre, bpost, [x + 300.0 * rnd() for x in res[2]], True)[2]
+    kinds = {}
+    kind = [kinds.setdefault((o["e"], o["w"][0][0] if o["e"] == "p" else o["w"][0][0].rstrip("0123456789"), o["w"][0][1] // 128), len(kinds)) for o in ops]
+    shift = [0.0] * len(kinds)
+    for it in range(ROUNDS):
+        new = list(shift)
+        for _ in range(1 + int(4 * rnd())):
+            new[int(rnd() * len(kinds))] += NOISE * (2 * rnd() - 1)
+        res = passes(ops, fpre, fpost, [base[i] + new[kind[i]] for i in range(n)], False)
+        if max(res[2]) <= max(best[2]):
+            best, shift = res, new
+    return best
+
+
+def rank_program(g, core, T, topo):
+    rank = T.rank_of(core)
+    if rank is None:
+        return
+    ops, Q = build(g, core, T, topo, rank)
+    deps = depend(ops)
+    order, start, fin = schedule(ops, deps)
+    count = {}
+    mark = {}
+    seen = {}
+    for i in order:
+        o = ops[i]
+        e = o["e"]
+        sem = o["sem"] or ENG_SEM[e]
+        if e != "r":
+            need = {}
+            for j, w in deps[i].items():
+                if w and mark[j][0] != "none":
+                    need[mark[j][0]] = max(need.get(mark[j][0], 0), mark[j][1])
+            for s, c in need.items():
+                if seen.get((e, s), 0) < c:
+                    Q[e].wait_ge(T.sem[s], c)
+                    seen[(e, s)] = c
+            h = o["fn"]()
+            if sem != "none":
+                h.then_inc(T.sem[sem], o["inc"])
+        count[sem] = count.get(sem, 0) + o["inc"]
+        mark[i] = (sem, count[sem])
+    count["sent"] = (RO - 1) * sum(len(lanes(topo, T.cores, rank, q)) for q in range(4) if q != rank)
+    for s, c in count.items():
+        if s != "none":
+            g.wait_ge(T.sem[s], c)

@@ -6,17 +6,20 @@ ALU = AluOpType
 AF = ActivationFunctionType
 
 V, NB, S0, TH, RO = 2048, 3072, 512, 256, 4
-ND = [16, 16]
-NM = [0, 0]
-POOL = True
-SPLIT = False
-SPLIT2 = False
-DB = ["ps0", "ps1", "ps4"]
-GC, SC, LAT, PEC, CYC, REM, KB = 1.56, 3.8, 110.0, 0.52, 1.04, 3000.0, 4.0
+ND = [[48, 48], [48, 48], [48, 48], [48, 48]]
+NM = [[8, 8], [8, 8], [8, 8], [8, 8]]
+MB = 64
+XC = [64, 16]
+ENG = {"s": "a", "n": "a", "hn": "a", "nn": "a", "Y": "v"}
+DB, CB = ["ps0", "ps1"], ["ps5", "ps5"]
+TURN = True
+GC, SC, LAT, PEC, CYC, REM, KB, DM0 = 1.56, 3.8, 230.0, 0.45, 0.9, 1800.0, 4.0, 1200.0
 ROUNDS, NOISE, AHEAD = 1000, 1500.0, 0.5
-EQW = sum(256 - 16 * c for c in range(16))
+CASES = [(130.0, 0.95, 0.9, 1300.0), (200.0, 0.92, 1.0, 1500.0), (300.0, 1.0, 1.0, 2400.0), (200.0, 1.35, 1.25, 1800.0)]
+MW = 136
 MAG = 12582912.0
 BIG = 2.0 ** 93
+U = 2.0 ** -16
 LR, L0 = math.log(1.7), 63.0
 
 F32, BF, F16, I32, U16 = "float32", "bfloat16", "float16", "int32", "uint16"
@@ -40,22 +43,28 @@ _sb("ident", V, F32)
 _sb("obi pci", 16, I32)
 _sb("tvb", [4, 64], BF)
 _sb("drb", 8, BF)
-_sb("land0 land1 land2 land3 send0 send1 send2", [4, 72], F16)
+_sb("land1 land2 land3", [8, MW], F16)
 _sb("ol16 sl16 nl16 xl16 offo offn", 16, U16)
 _sb("cl16", TH, U16)
-_sb("ol32 nl32 xm of32 on32 askw wo wn il", 16, F32)
-_sb("kc", 96, F32)
+_sb("ol32 nl32 xm of32 on32 il spn", 16, F32)
+_sb("olh", 16, F16)
+_sb("kc", 64, F32)
 _sb("Wi c32 p32", TH, I32)
-_sb("c16 p16 s16 n16 orow Y16 m16 hn hr B1 hold sc", TH, F16)
+_sb("cpb", [8, 64], F16)
+_sb("s16 n16 nn16 orow Y16 m16 hn hr B1 hold scs scn key", TH, F16)
 _sb("sel", 512, F16)
-_sb("rot nf OHT nhm q Da nfr Fo Fn yvb ones irow thr keep Ls", TH, BF)
-_sb("Hs W1 Ws d0f d0r tt fs Z a1", TH, F32)
-_sb("eqo eqn", EQW, BF)
+_sb("Kt", RO * TH, F16)
+_sb("rot Sg OHT nhm OHs nfr Fo Fn yvb ones irow Kc Vm", TH, BF)
+_sb("W1 Ws d0f d0r dl fs Z", TH, F32)
+_sb("eqo eqn", 2560, BF)
 _sb("col", 64, F32)
-_sb("rowg rowr tm If5 RTI", 128, F32)
-_sb("Ib nIb I5 I12 nI13 I23 nI11 BIb nhI BO nBO nBO12 E8 RmI RTb Dc Vm0 Vm1", 128, BF)
-_sb("Mall", 144, BF)
-_sb("G32 G64 nG32 G13 S16", 8, BF)
+_sb("rowg rowr tm RTI wx", 128, F32)
+_sb("Ib nIb I11 I12 nI12 I13 I23 nI11 BO nBO E8 E8n nRm RTb Dc WG AW", 128, BF)
+_sb("Hw", 128, F16)
+_sb("Mall M8", 144, BF)
+_sb("K8", 64, BF)
+_sb("GG GG2 nGG Dg", 16, BF)
+_sb("G13 SB nSB Z8", 8, BF)
 for _k in range(8):
     SCRATCH["ps%d" % _k] = ("psum", [128, 512], F32)
 
@@ -79,45 +88,48 @@ def build(g, core, T, topo, rank):
 
     def A(name, lo=None, hi=None, step=1):
         if lo is None:
-            return (T[name][:], (name, 0, 1 << 20))
-        return (T[name][:, lo:hi:step] if step != 1 else T[name][:, lo:hi], (name, lo, hi))
+            return (T[name][:], [(name, 0, 1 << 20)], [])
+        return (T[name][:, lo:hi:step] if step != 1 else T[name][:, lo:hi], [(name, lo, hi)], [])
 
     def AR(name, lo, hi):
-        return (T[name][:, hi - 1::-1] if lo == 0 else T[name][:, hi - 1:lo - 1:-1], (name, lo, hi))
+        return (T[name][:, hi - 1::-1] if lo == 0 else T[name][:, hi - 1:lo - 1:-1], [(name, lo, hi)], [])
 
-    def M(name, q0, q1, lo, hi):
+    def M(name, q0, q1, lo, hi, step=1):
         w = SCRATCH[name][1][2]
-        pat = T[name][:, q0, lo:hi] if q1 == q0 + 1 else T[name][:, q0:q1, lo:hi]
-        return (pat, (name, q0 * w + lo, (q1 - 1) * w + hi))
+        pat = T[name][:, q0, lo:hi] if q1 == q0 + 1 else (T[name][:, q0:q1, lo:hi] if step == 1 else T[name][:, q0:q1:step, lo:hi])
+        return (pat, [(name, q * w + lo, q * w + hi) for q in range(q0, q1, step)], [])
 
-    def P8(name, lo, hi):
-        return (T[name][0:8, lo:hi], (name, lo, hi))
+    def P8(name, lo, hi, step=1):
+        return (T[name][0:8, lo:hi:step] if step != 1 else T[name][0:8, lo:hi], [(name, lo, hi)], [])
 
     def IND(win, off):
         return (win[0].indirect(off[0]), win[1], off[1])
 
     def op(eng, fn, rd, wr, dur, sem=None, inc=1, lat=0.0):
-        r = []
+        r, w = [], []
         for x in rd:
             if isinstance(x, tuple):
-                r.extend(x[1:])
-        w = []
+                r.extend(x[1] + x[2])
         for x in wr:
-            w.append(x[1])
-            r.extend(x[2:])
-        ops.append({"e": eng, "fn": fn, "r": r, "w": w, "dur": dur, "sem": sem, "inc": inc, "lat": lat})
+            w.extend(x[1])
+            r.extend(x[2])
+        x = dur - 60.0 if any(isinstance(y, tuple) and y[2] for y in rd + wr) else 0.0
+        ops.append({"e": eng, "fn": fn, "r": r, "w": w, "dur": dur, "sem": sem, "inc": inc, "lat": lat, "x": x})
 
     def ap(x):
         return x[0] if isinstance(x, tuple) else x
 
+    def dtype(x):
+        return SCRATCH[x[1][0][0]][2]
+
     def two(x):
-        return SCRATCH[x[1][0]][2] in (BF, F16, U16)
+        return dtype(x) in (BF, F16, U16)
 
     def cost(eng, n, out, ins, k=None):
-        if len(out) == 3:
-            return 55.0 + n * SC * CYC
-        if len(ins[0]) == 3:
-            return (55.0 if eng == "v" else 70.0) + n * GC * CYC
+        if out[2]:
+            return 50.0 + n * SC * CYC
+        if ins[0][2]:
+            return (50.0 if eng == "v" else 65.0) + n * GC * CYC
         if k is None:
             k = 0.5 if (eng == "v" and two(out) and all(two(x) for x in ins)) else 1.0
         return max(64.0, n * k) * CYC
@@ -133,27 +145,35 @@ def build(g, core, T, topo, rank):
         op("v", fn, [in_, s1, s2], [out], cost("v", n, out, [in_]))
 
     def tt(out, a, b, n, o):
-        ps = a[1][0].startswith("ps") or b[1][0].startswith("ps")
+        ps = a[1][0][0].startswith("ps") or b[1][0][0].startswith("ps")
         op("v", lambda: g.vector.tensor_tensor(out[0], a[0], b[0], o), [a, b], [out], cost("v", n, out, [a, b], 1.0 if ps else 2.0))
 
     def scan(out, d0, d1, n, o0=ALU.add, o1=ALU.min):
         op("v", lambda: g.vector.tensor_tensor_scan(out[0], d0[0], d1[0], 0.0, o0, o1), [d0, d1], [out], cost("v", n, out, [d0, d1]))
 
     def act(out, in_, n, f, bias=0.0, scale=1.0, extra=0.0):
-        op("a", lambda: g.scalar.activation(out[0], in_[0], f, bias=bias, scale=ap(scale)), [in_, scale], [out], cost("a", n, out, [in_]) + extra)
+        op("a", lambda: g.scalar.activation(out[0], in_[0], f, bias=ap(bias), scale=ap(scale)), [in_, scale, bias], [out], cost("a", n, out, [in_]) + extra)
+
+    def plus(eng, out, in_, n, add=None):
+        if eng == "a":
+            if add is None:
+                act(out, in_, n, AF.Copy)
+            else:
+                act(out, in_, n, AF.Identity, bias=add)
+        elif add is None:
+            cp(out, in_, n)
+        else:
+            ts(out, in_, n, add, ALU.add)
 
     def iota(out, pat, base, cm, n):
-        if SCRATCH[out[1][0]][2] == I32:
+        if dtype(out) == I32:
             fn = lambda: g.iota(out[0], pat, base, cm)
         else:
             fn = lambda: g.iota(out[0], pat, base, cm, allow_small_or_imprecise_dtypes=True)
-        op("g", fn, [], [out], 160.0 + 2 * n * CYC)
+        op("g", fn, [], [out], 130.0 + 2 * n * CYC)
 
     def conv(out, in_, n):
-        if POOL:
-            op("g", lambda: g.affine_select(out[0], in_[0], [[0, n]], ALU.is_equal, 0.0, 0, 0), [in_], [out], 210.0 + 2 * n * CYC)
-        else:
-            cp(out, in_, n)
+        op("g", lambda: g.affine_select(out[0], in_[0], [[0, n]], ALU.is_equal, 0.0, 0, 0), [in_], [out], 170.0 + 2 * n * CYC)
 
     def mm(lst):
         def fn():
@@ -161,17 +181,17 @@ def build(g, core, T, topo, rank):
             for (o, l, r, n, st, sp) in lst:
                 h = g.tensor.matmul(o[0], l[0], r[0], st, sp)
             return h
-        dur = sum(max(64, n) * (4 if SCRATCH[l[1][0]][2] == F32 else 1) for (o, l, r, n, st, sp) in lst) * PEC + 30.0
+        dur = sum(n * (4 if dtype(l) == F32 else 1) for (o, l, r, n, st, sp) in lst) * PEC + 20.0
         op("p", fn, [x[1] for x in lst] + [x[2] for x in lst], [x[0] for x in lst], dur)
 
     def grp(out, terms, n, start=True, stop=True):
         return [(out, l, r, n, start and k == 0, stop and k == len(terms) - 1) for k, (l, r) in enumerate(terms)]
 
     def dma(eng, sem, out, in_, kb):
-        op(eng, lambda: Q[eng].dma_start(out[0], in_[0]), [in_], [out], 60.0, sem=sem, inc=16, lat=2000.0 + kb * KB)
+        op(eng, lambda: Q[eng].dma_start(out[0], in_[0]), [in_], [out], 60.0, sem=sem, inc=16, lat=DM0 + kb * KB)
 
     def H(t):
-        return (t, ("hbm", 0, 0))
+        return (t, [("hbm", 0, 0)], [])
 
     for eng, sem, dst, src, kb in (("s", "d_ob", A("obi"), T.ob[:], 8), ("a", "d_shp", P8("shpi", 0, V), T.shp[:], 128), ("s", "d_rec", A("rect"), T.rec[:], 1100),
                                    ("a", "d_tv", A("tvb"), T.tv[:], 64), ("a", "d_dr", A("drb", 0, 4), T.dr[:], 1),
@@ -182,12 +202,13 @@ def build(g, core, T, topo, rank):
     iota(A("pci", 0, 1), [[1, 1]], 0, 1, 1)
     iota(A("ident", 0, TH), [[1, TH]], 0, 0, TH)
     iota(A("rowg"), [[16, 8], [0, 16]], 0, 0, 128)
-    for k in range(3):
-        iota(A("nxt", 512 * k, 512 * k + 512), [[1, 512]], 512 * k, 0, 512)
+    iota(A("wx"), [[0, 16], [16, 8]], 0, 0, 128)
     for k in range(4):
         lo, hi = TH + 448 * k, TH + 448 * (k + 1)
         iota(A("ident", lo, hi), [[1, hi - lo]], lo, 0, hi - lo)
-    C = {n: A("col", 4 * k, 4 * k + 1) for k, n in enumerate("pc rc gc nc pvc dc gm p16 hc r1".split())}
+    for k in range(3):
+        iota(A("nxt", 512 * k, 512 * k + 512), [[1, 512]], 512 * k, 0, 512)
+    C = {n: A("col", 4 * k, 4 * k + 1) for k, n in enumerate("pc rc gc nc pvc dc gm p16 hc r1 h2 p15 wb".split())}
     rowm, rowx, row8 = A("ident", 0, 128), A("ident", 0, 144), A("ident", 0, 128, 16)
     ts(A("pci", 4, 5), A("pci", 0, 1), 1, 15, ALU.bitwise_and)
     cp(C["pc"], A("pci", 0, 1), 1)
@@ -200,247 +221,300 @@ def build(g, core, T, topo, rank):
     ts(C["pvc"], C["pvc"], 1, C["pc"], ALU.add, -1.0, ALU.add)
     ts(C["gm"], C["gc"], 1, 15.0, ALU.add)
     ts(C["p16"], C["pc"], 1, 16.0, ALU.mult)
+    ts(C["p15"], C["pc"], 1, 16.0, ALU.mult, 15.0, ALU.add)
     ts(C["r1"], C["rc"], 1, 1.0, ALU.add)
     ts(C["hc"], C["rc"], 1, 15.0, ALU.not_equal, 2048.0, ALU.mult)
+    ts(C["h2"], C["hc"], 1, 2048.0, ALU.add)
+    ts(C["wb"], C["rc"], 1, -LR, ALU.mult, L0, ALU.add)
     ts(A("Ib"), rowm, 128, C["pc"], ALU.is_equal)
-    for n, s in (("nIb", -1.0), ("If5", 1.0 / 32), ("I5", 32.0), ("I12", 4096.0), ("nI13", -8192.0), ("I23", 2.0 ** 23),
-                 ("nI11", -2048.0), ("BIb", BIG), ("nhI", -0.5), ("Dc", C["dc"])):
+    for n, s in (("nIb", -1.0), ("I11", 2048.0), ("I12", 4096.0), ("nI12", -4096.0), ("I13", 8192.0), ("I23", 2.0 ** 23),
+                 ("nI11", -2048.0), ("Dc", C["dc"])):
         act(A(n), A("Ib"), 128, AF.Identity, scale=s)
+    ts(A("Hw"), A("Ib"), 128, 0.5 - 2.0 ** -11, ALU.mult)
     ts(A("Mall"), rowx, 144, C["gm"], ALU.is_equal)
+    ts(A("M8"), rowx, 144, C["p15"], ALU.is_equal, 2048.0, ALU.mult)
     ts(A("BO"), A("rowg"), 128, C["gc"], ALU.is_equal)
     act(A("nBO"), A("BO"), 128, AF.Identity, scale=-1.0)
-    act(A("nBO12"), A("BO"), 128, AF.Identity, scale=-4096.0)
     ts(A("E8"), A("rowg"), 128, C["p16"], ALU.is_equal)
+    act(A("E8n"), A("E8"), 128, AF.Identity, scale=-4096.0)
     for k in range(4):
         lo, hi = 512 * k, 512 * k + 512
         cp(P8("shph", lo, hi), P8("shpi", lo, hi), 512)
         mm([(A("ps%d" % k), P8("E8", 0, 128), P8("shph", lo, hi), 512, True, True)])
         act(A("shpt", lo, hi), A("ps%d" % k), 512, AF.Copy)
     tt(A("rowr"), rowm, A("rowg"), 128, ALU.subtract)
-    ts(A("G32"), row8, 8, C["gc"], ALU.is_equal, 32.0, ALU.mult)
+    for n, s in (("GG", 1.0), ("GG2", 2.0), ("nGG", -1.0)):
+        ts(A(n, 0, 8), row8, 8, C["gc"], ALU.is_equal, s / 2048, ALU.mult)
+        ts(A(n, 8, 16), row8, 8, C["gc"], ALU.is_equal, s, ALU.mult)
     ts(A("G13"), row8, 8, C["gc"], ALU.is_equal, 8192.0, ALU.mult)
-    ts(A("S16"), row8, 8, C["pc"], ALU.is_equal, 16.0, ALU.mult)
-    if max(NM):
-        ts(A("G64"), row8, 8, C["gc"], ALU.is_equal, 64.0, ALU.mult)
-        ts(A("nG32"), row8, 8, C["gc"], ALU.is_equal, -32.0, ALU.mult)
-    for k in range(2):
-        if NM[k]:
-            ts(A("Vm%d" % k), A("rowr"), 128, float(NM[k]), ALU.is_lt, 32.0, ALU.mult)
-            tt(A("Vm%d" % k), A("Vm%d" % k), A("nBO"), 128, ALU.mult)
-    ts(A("RmI"), rowm, 128, C["nc"], ALU.is_equal, 32.0, ALU.mult)
-    tt(A("RmI"), A("RmI"), A("I5"), 128, ALU.subtract)
+    ts(A("SB"), row8, 8, C["pc"], ALU.is_equal, BIG, ALU.mult)
+    ts(A("nSB"), row8, 8, C["pc"], ALU.is_equal, -BIG, ALU.mult)
+    ts(A("Z8"), row8, 8, 0.0, ALU.mult)
+    ts(A("Dg"), A("ident", 0, 16), 16, C["rc"], ALU.is_equal, -2.56, ALU.mult)
+    ts(A("K8"), A("rowg", 0, 128, 2), 64, C["gc"], ALU.is_equal)
+    nms = sorted(set(x for y in NM for x in y if x))
+    assert len(nms) <= 1
+    for nm in nms:
+        ts(A("Vm", 128, 256), A("rowr"), 128, float(nm), ALU.is_lt)
+        tt(A("Vm", 128, 256), A("Vm", 128, 256), A("nBO"), 128, ALU.mult)
+        ts(A("Vm", 0, 128), A("Vm", 128, 256), 128, 1.0 / 2048, ALU.mult)
+        for t in range(RO):
+            ts(A("Kt", TH * t, TH * t + 128), A("Vm", 0, 128), 128, A("drb", t, t + 1), ALU.mult, -1.0 / 128, ALU.add)
+            ts(A("Kt", TH * t + 128, TH * t + TH), A("Vm", 128, 256), 128, A("drb", t, t + 1), ALU.mult)
+    ts(A("nRm"), rowm, 128, C["nc"], ALU.is_equal)
+    tt(A("nRm"), A("Ib"), A("nRm"), 128, ALU.subtract)
     ts(A("RTb"), rowm, 128, C["pvc"], ALU.is_equal)
     tt(A("RTb"), A("RTb"), A("Ib"), 128, ALU.subtract)
     act(A("RTI"), A("RTb"), 128, AF.Copy)
     ts(A("tm"), A("rowr"), 128, C["rc"], ALU.not_equal, 1.0e7, ALU.mult)
-    act(A("Z", 0, 128), A("tm"), 128, AF.Identity, scale=64 * BIG / 1.0e7)
-    act(A("tm"), A("tm"), 128, AF.Identity, bias=16.0)
+    act(A("tm"), A("tm"), 128, AF.Identity, bias=-1.0 + 16 * U)
     ts(A("Y16", 0, 128), A("rowr"), 128, C["rc"], ALU.is_equal, 8192.0, ALU.mult)
     ts(A("m16", 0, 128), A("rowr"), 128, C["r1"], ALU.is_equal, -2048.0, ALU.mult)
     ts(A("il"), A("ident", 0, TH, 16), 16, C["rc"], ALU.add)
-    for k, off in enumerate([NB - 2048 + TH * t for t in range(RO)] + [V, 1536]):
-        act(A("kc", 16 * k, 16 * k + 16), A("il"), 16, AF.Identity, bias=float(off))
+    ts(A("spn"), A("il"), 16, C["h2"], ALU.subtract, 1536.0, ALU.add)
+    for k in range(RO):
+        act(A("kc", 16 * k, 16 * k + 16), A("il"), 16, AF.Identity, bias=float(NB - 2048 + TH * k))
     act(A("ones"), A("ident", 0, TH), TH, AF.Identity, bias=1.0, scale=0.0)
+    act(A("Kc", 0, 128), rowm, 128, AF.Identity, bias=-1.0 / 128, scale=0.0)
+    act(A("Kc", 128, 256), rowm, 128, AF.Identity, scale=0.0)
     act(A("irow"), A("ident", 0, TH), TH, AF.Copy)
-    act(A("a1"), A("ident", 0, TH), TH, AF.Exp, bias=L0 + math.log(2.56), scale=-LR, extra=1400.0)
-    act(A("wo"), A("il"), 16, AF.Exp, bias=L0, scale=-LR)
-    act(A("wn"), A("il"), 16, AF.Exp, bias=L0 - math.log(8192.0), scale=-LR)
+    ts(A("AW"), A("wx"), 128, C["gc"], ALU.is_equal)
+    iota(A("wx"), [[16, 16], [0, 8]], 0, 0, 128)
+    act(A("wx"), A("wx"), 128, AF.Exp, bias=C["wb"], scale=-LR, extra=1300.0)
+    tt(A("WG"), A("wx"), A("AW"), 128, ALU.mult)
     for h in range(2):
         tt(A("hold", 128 * h, 128 * h + 128), A("Y16", 0, 128), A("m16", 0, 128), 128, ALU.add)
-        tt(A("thr", 128 * h, 128 * h + 128), A("a1", 128 * h, 128 * h + 128), A("Z", 0, 128), 128, ALU.add)
-        act(A("keep", 128 * h, 128 * h + 128), A("rowr"), 128, AF.Sign)
-    act(A("d0f"), A("ident", 0, TH), TH, AF.Identity, bias=-1.0, scale=0.0)
+    act(A("d0f"), A("ident", 0, TH), TH, AF.Identity, bias=-U, scale=0.0)
     act(A("d0f", 0, TH, 16), A("il"), 16, AF.Identity, bias=1.0e6, scale=0.0)
-    act(A("d0r"), A("ident", 0, TH), TH, AF.Identity, bias=1.0, scale=0.0)
+    act(A("d0r"), A("ident", 0, TH), TH, AF.Identity, bias=U, scale=0.0)
     act(A("d0r", 15, TH, 16), A("il"), 16, AF.Identity, bias=1.0e6, scale=0.0)
-    cp(M("land0", 0, 4, 0, 64), A("tvb"), TH)
     conv(A("ht", 0, S0), A("bnd"), S0)
     for k in range(4):
         conv(A("recf", 512 * k, 512 * k + 512), A("rect", 512 * k, 512 * k + 512), 512)
 
-    def tolist(out, buf, lo, hi):
-        n = (hi - lo) // 16
-        return [(out, A("Mall", 15 - r, 143 - r), A(buf, lo + r, hi, 16), n, r == 0, False) for r in range(16)]
+    def pairs(buf, row, keys, cs, blocks):
+        for c in cs:
+            lo = 64 * (c // 4) if blocks else 16 * c
+            ts(A(buf, eoff[c] + lo % 64, eoff[c + 1]), row(lo), TH - lo, A(keys, c, c + 1), ALU.is_equal)
 
-    eoff = [sum(256 - 16 * k for k in range(c)) for c in range(17)]
+    eoff = [sum(256 - 64 * (k // 4) for k in range(c)) for c in range(17)]
 
-    def pairs(buf, row, keys, wts, cs, last):
+    def sums(lo, buf, wts, cs, last):
         for c0 in range(0, len(cs), 4):
-            part = cs[c0:c0 + 4]
-            for c in part:
-                ts(A(buf, eoff[c], eoff[c + 1]), A(row, 16 * c, TH), TH - 16 * c, A(keys, c, c + 1), ALU.is_equal, A(wts, c, c + 1), ALU.mult)
-            mm([(A("ps6", 16 * c, TH), A("BO"), A(buf, eoff[c], eoff[c + 1]), TH - 16 * c, False, last and c == cs[-1]) for c in part])
+            lst = []
+            for c in cs[c0:c0 + 4]:
+                w = A(wts, 8 * c, 8 * c + 8)
+                lst.append((P8("ps6", lo + 16 * c, lo + TH), w, A(buf, eoff[c] + 16 * c % 64, eoff[c + 1]), TH - 16 * c, False, False))
+                lst.append((P8("ps6", lo + 16 * c, lo + 16 * c + 16), w, A("Dg"), 16, False, last and c == cs[-1]))
+            mm(lst)
 
-    def places(out, flags, keys, spare):
-        scan(A("Ls"), A("keep"), A(flags), TH, ALU.mult, ALU.max)
-        tt(A("of32"), A("Ls", 15, TH, 16), spare, 16, ALU.mult)
-        tt(A("on32"), A("of32"), A(keys), 16, ALU.max)
-        cp(A(out), A("on32"), 16)
+    def places(flags, keys):
+        out = A("ps6", 256, 272)
+        return [(out, P8("M8", 15 - r, 143 - r), P8(flags, r, TH, 16), 64, r == 0, False) for r in range(16)] + [(out, A("Ib"), keys, 64, False, True)]
 
-    own = rank // 2
+    own, par = rank // 2, rank % 2
     horder = [1 - own, own]
-    halves = [(128 * h, 128) for h in horder]
+    vo, oo, po = 8 * par, 64 + 8 * par, 128 - 124 * par
     for t in range(RO):
-        last = t == RO - 1
+        first, last = t == 0, t == RO - 1
         land, nb, ns = "land%d" % t, NB + TH * t, S0 + TH * t
         drc = A("drb", t, t + 1)
         hs = lambda n, h, w=128: A(n, w * h, w * h + w)
-        EB = lambda h, k: A("ps%d" % (2 + h), 128 * k, 128 * k + 128)
         DA = lambda h, a0, a1, lo, hi: M("Dab", 16 * h + a0, 16 * h + a1, lo, hi)
+        vv = lambda q0, q1: M("tvb", q0, q1, 0, 64) if first else M(land, 3 + q0, 3 + q1, vo, vo + 64)
+        cc = lambda h: M("cpb", 4 * h + 1, 4 * h + 3, 0, 64)
+        pp = lambda h: M("cpb", 4 * h, 4 * h + 4, 0, 64, 3)
+        if first:
+            cp(A("ol16"), A("obi"), 16)
+            cp(A("olh"), A("obi"), 16)
+            cp(A("ol32"), A("obi"), 16)
+            cp(A("orow"), IND(A("ident"), A("ol16")), TH)
         for h in horder:
-            if t == 0:
-                cp(hs("ol16", h, 8), hs("obi", h, 8), 8)
-                ts(hs("c32", h), IND(A("rect"), hs("ol16", h, 8)), 128, 4095, ALU.bitwise_and)
+            h8 = lambda n: hs(n, h, 8)
+            if first:
+                ts(hs("c32", h), IND(A("rect"), h8("ol16")), 128, 4095, ALU.bitwise_and)
+                cp(hs("cl16", h), hs("c32", h), 128)
+                ts(hs("p32", h), IND(A("rect"), h8("ol16")), 128, 12, ALU.arith_shift_right)
             else:
-                cp(hs("ol16", h, 8), M(land, 2 * h, 2 * h + 2, 64, 68), 8)
-                cp(hs("Wi", h), IND(A("recf", 0, V), hs("ol16", h, 8)), 128)
+                cp(h8("ol16"), M(land, 3 + 2 * h, 5 + 2 * h, po, po + 4), 8)
+                conv(h8("ol32"), M(land, 3 + 2 * h, 5 + 2 * h, po, po + 4), 8)
+                cp(hs("Wi", h), IND(A("recf", 0, V), h8("ol16")), 128)
                 ts(hs("c32", h), hs("Wi", h), 128, 4095, ALU.bitwise_and)
-            cp(hs("cl16", h), hs("c32", h), 128)
-        for lo, n in (halves if SPLIT else [(0, TH)]):
-            R = lambda name: A(name, lo, lo + n)
-            Lc = lambda name: A(name, lo // 16, (lo + n) // 16)
-            hh = range(lo // 128, (lo + n) // 128)
-            cp(R("s16"), IND(A("shpt", 0, V), Lc("ol16")), n)
-            scan(R("sc"), R("hold"), R("s16"), n)
-            ts(Lc("sl16"), A("sc", lo + 15, lo + n, 16), n // 16, C["hc"], ALU.add)
-            cp(R("n16"), IND(A("nxt", 0, 1536), Lc("sl16")), n)
-            scan(R("sc"), R("hold"), R("n16"), n)
-            ts(Lc("nl16"), A("sc", lo + 15, lo + n, 16), n // 16, C["hc"], ALU.add)
-            mm(grp(A("ps7", lo, lo + n), [(A("Ib"), R("n16")), (A("nIb"), R("s16"))], n))
-            act(R("rot"), A("ps7", lo, lo + n), n, AF.Sign)
-            ts(R("hn"), IND(A("ht", 0, ns), Lc("nl16")), n, -2048.0, ALU.add)
-            tt(R("hr"), R("hn"), R("rot"), n, ALU.mult)
-            mm([(A("ps5", 32 + 8 * h, 40 + 8 * h), hs("rot", h), A("S16"), 8, True, True) for h in hh])
-            rt = A("ps5", 32 + lo // 16, 32 + (lo + n) // 16)
-            act(A("d0f", lo + 1, lo + n, 16), rt, n // 16, AF.Identity, bias=-1.0)
-            act(A("d0r", lo, lo + n, 16), rt, n // 16, AF.Identity, bias=1.0, scale=-1.0)
-            mm(sum([grp(A("ps7", 256 + 128 * h, 384 + 128 * h), [(hs("hn", h), A("I5")), (hs("hr", h), A("RmI"))], 128) for h in hh], []))
-            act(R("Hs"), A("ps7", 256 + lo, 256 + lo + n), n, AF.Identity, bias=65536.0)
-        cp(A("nl32"), A("nl16"), 16)
-        for lo, n in (halves if SPLIT2 else [(0, TH)]):
-            R = lambda name: A(name, lo, lo + n)
-            Lc = lambda name: A(name, lo // 16, (lo + n) // 16)
-            ts(R("c16"), R("cl16"), n, -2048.0, ALU.add)
-            if t == 0:
-                ts(R("p32"), IND(A("rect"), Lc("ol16")), n, 12, ALU.arith_shift_right)
+                cp(hs("cl16", h), hs("c32", h), 128)
+                ts(hs("p32", h), hs("Wi", h), 128, 12, ALU.arith_shift_right)
+            ts(cc(h), hs("cl16", h), 128, -2048.0, ALU.add)
+            conv(pp(h), hs("p32", h), 128)
+            ts(A("boxt", nb + 128 * h, nb + 128 * h + 128), vv(2 * h, 2 * h + 2), 128, drc, ALU.subtract)
+            if not first:
+                plus(ENG["s"], hs("s16", h), IND(A("shpt", 0, V), h8("ol16")), 128)
+                scan(hs("scs", h), hs("hold", h), hs("s16", h), 128)
+                ts(h8("sl16"), A("scs", 128 * h + 15, 128 * h + 128, 16), 8, C["hc"], ALU.add)
+                plus(ENG["n"], hs("n16", h), IND(A("nxt", 0, 1536), h8("sl16")), 128)
             else:
-                ts(R("p32"), R("Wi"), n, 12, ALU.arith_shift_right)
-            conv(R("p16"), R("p32"), n)
-            ts(A("boxt", nb + lo, nb + lo + n), M(land, lo // 64, (lo + n) // 64, 0, 64), n, drc, ALU.subtract)
-            mm(grp(A("ps7", lo, lo + n), [(A("I23"), R("rot")), (A("I12"), R("p16")), (A("Ib"), R("c16"))], n))
-            act(R("W1"), A("ps7", lo, lo + n), n, AF.Relu, bias=2048.0 - 2.0 ** 23)
-            mm(grp(A("ps7", 256 + lo, 256 + lo + n), [(A("I12"), R("p16")), (A("Ib"), R("c16")), (A("RTI"), R("W1"))], n))
-            act(R("Ws"), A("ps7", 256 + lo, 256 + lo + n), n, AF.Identity, bias=2048.0)
-            cp(Lc("ol32"), Lc("ol16"), n // 16)
-            cp(R("orow"), IND(A("ident"), Lc("ol16")), n)
-        mm(grp(A("ps6", 0, TH), [(A("nIb"), A("thr"))], TH, stop=False))
-        pairs("eqo", "orow", "ol32", "wo", [8 * h + c for h in horder for c in range(8)], True)
-        act(A("Fo"), A("ps6", 0, TH), TH, AF.Sign)
-        places("offo", "Fo", "ol32", A("kc", 64, 80))
-        tt(A("nfr"), IND(A("nxt", 0, 1536), A("nl16")), A("n16"), TH, ALU.not_equal)
-        mm(grp(A("ps6", 0, TH), [(A("nIb"), A("thr")), (A("BIb"), A("nfr"))], TH, stop=False))
+                plus(ENG["n"], hs("n16", h), IND(A("shpt", 0, V), h8("ol16")), 128)
+            scan(hs("scn", h), hs("hold", h), hs("n16", h), 128)
+            ts(h8("nl16"), A("scn", 128 * h + 15, 128 * h + 128, 16), 8, C["hc"], ALU.add)
+            ts(h8("nl32"), A("scn", 128 * h + 15, 128 * h + 128, 16), 8, C["hc"], ALU.add)
+            plus(ENG["hn"], hs("hn", h), IND(A("ht", 0, ns), h8("nl16")), 128, -2048.0)
+            S7 = lambda k: A("ps7", 128 * k, 128 * k + 128)
+            if not first:
+                if ENG["nn"] == "a":
+                    plus("a", hs("nn16", h), IND(A("nxt", 0, 1536), h8("nl16")), 128)
+                else:
+                    tt(hs("nfr", h), IND(A("nxt", 0, 1536), h8("nl16")), hs("n16", h), 128, ALU.not_equal)
+                mm(grp(S7(0), [(A("I12"), hs("n16", h)), (A("nI12"), hs("s16", h)), (A("nI11"), hs("ones", h))], 128))
+                act(hs("rot", h), S7(0), 128, AF.Sign, bias=2048.0)
+                tt(hs("hr", h), hs("hn", h), S7(0), 128, ALU.min)
+                mm(grp(S7(1), [(hs("rot", h), A("Dc"))], 128) + grp(S7(2), [(A("I23"), hs("rot", h)), (A("I12"), pp(h)), (A("Ib"), cc(h))], 128))
+                act(A("d0f", 128 * h + 1, 128 * h + 128, 16), A("ps7", 129, 256, 16), 8, AF.Identity, bias=-U, scale=16 * U)
+                act(A("d0r", 128 * h, 128 * h + 128, 16), A("ps7", 129, 256, 16), 8, AF.Identity, bias=U, scale=-16 * U)
+                act(hs("dl", h), S7(1), 128, AF.Identity, bias=-1.0, scale=U)
+                act(hs("W1", h), S7(2), 128, AF.Relu, bias=2048.0 - 2.0 ** 23)
+                mm(grp(S7(3), [(A("I12"), pp(h)), (A("Ib"), cc(h)), (A("RTI"), hs("W1", h))], 128))
+            else:
+                mm(grp(S7(3), [(A("I12"), pp(h)), (A("Ib"), cc(h))], 128))
+            act(hs("Ws", h), S7(3), 128, AF.Identity, bias=2048.0)
+        chunks = [8 * h + c for h in horder for c in range(8)]
+        if first:
+            pairs("eqo", lambda lo: A("orow", lo, TH), "ol32", chunks, False)
+        else:
+            pairs("eqo", lambda lo: M(land, 3 + lo // 64, 7, oo, oo + 64), "ol32", chunks, True)
+        mm([(P8("ps6", 0, TH), A("Z8"), A("irow"), TH, True, False)])
+        sums(0, "eqo", "WG", chunks, True)
+        act(P8("Fo", 0, TH), P8("ps6", 0, TH), TH, AF.Sign)
+        mm(places("Fo", A("olh") if first else M(land, 3, 7, po, po + 4)))
+        tt(A("of32"), A("ps6", 256, 272), A("il"), 16, ALU.min)
+        ts(A("offo"), A("of32"), 16, 2048.0, ALU.add)
         if not last:
             cp(IND(A("shpt"), A("offo")), A("n16"), TH)
+        pairs("eqn", lambda lo: A("n16", lo, TH), "nl32", chunks, False)
+        out = P8("ps6", TH, 2 * TH)
+        if first:
+            mm(grp(out, [(A("Z8"), A("irow"))], TH, stop=False))
+        elif ENG["nn"] == "a":
+            mm(grp(out, [(A("SB"), A("nn16")), (A("nSB"), A("n16"))], TH, stop=False))
+        else:
+            mm(grp(out, [(A("SB"), A("nfr"))], TH, stop=False))
         for k, h in enumerate(horder):
-            nm, na = NM[k], 128 - ND[k]
-            for lo, hi in ((128 * h, 128 * h + 64), (128 * h + 64, 128 * h + na)):
-                act(A("X", 16 * lo, 16 * hi), IND(A("boxt", 0, nb), A("cl16", lo, hi)), 16 * (hi - lo), AF.Copy)
-                ops[-1]["w"].append(("turn", 0, 1))
-            if ND[k]:
-                lo, hi = 128 * h + na, 128 * h + 128
-                cp(A("X", 16 * lo, 16 * hi), IND(A("boxt", 0, nb), A("cl16", lo, hi)), 16 * ND[k])
+            h8 = lambda n: hs(n, h, 8)
+            E, cb = "ps%d" % (2 + h), CB[k]
+            nm, nd = NM[t][k], ND[t][k]
+            lo = 128 * h
+            for n in XC:
+                n = min(n, 128 * h + 128 - nd - lo)
+                if n > 0:
+                    act(A("X", 16 * lo, 16 * (lo + n)), IND(A("boxt", 0, nb), A("cl16", lo, lo + n)), 16 * n, AF.Copy)
+                    if TURN:
+                        ops[-1]["w"].append(("turn", 0, 1))
+                    lo += n
+            if nd:
+                cp(A("X", 16 * lo, 16 * (lo + nd)), IND(A("boxt", 0, nb), A("cl16", lo, lo + nd)), 16 * nd)
             if nm:
-                mm([(A("ps5", 384 + 64 * b, 448 + 64 * b), A("Ib"), M(land, 2 * h + b, 2 * h + b + 1, 0, 64), 64, True, True) for b in range(2)])
-                mm([(EB(h, 0), M(land, 2 * h, 2 * h + 2, 0, 64), A("Vm%d" % k), 128, True, False)])
-            for a in range(nm):
-                tt(DA(h, a, a + 1, 0, 128), A("X", 2048 * h + a, 2048 * h + 2048, 16), A("ps5", 384, 512), 128, ALU.max)
+                terms = [(hs("ones", 0), A("Kt", TH * t, TH * t + TH)), (A("boxt", nb + 128 * h, nb + 128 * h + 128), A("Vm"))]
+            else:
+                terms = [(hs("ones", 0), A("Kc"))]
+            mm(grp(A(E, 0, 256), terms, 256, stop=False))
+            if nm:
+                mm([(hs("ps4", h), A("Ib"), vv(2 * h, 2 * h + 2), 128, True, True)])
+            eo = lambda a: A(E, a, 256, 16)
             aa = list(range(nm, 16))
             tiles = [(b, aa[j:j + 8]) for b in range(2) for j in range(0, len(aa), 8)]
             for j, (b, part) in enumerate(tiles):
-                bank = DB[(4 * k + j) % len(DB)]
+                bank = DB[(len(tiles) * k + j) % len(DB)]
                 x0 = 2048 * h + 1024 * b
-                mm(sum([grp(A(bank, 64 * m, 64 * m + 64), [(A("Ib"), A("X", x0 + a, x0 + 1024, 16)), (A("nIb"), M(land, 2 * h + b, 2 * h + b + 1, 0, 64))], 64)
+                mm(sum([grp(A(bank, 64 * m, 64 * m + 64), [(A("Ib"), A("X", x0 + a, x0 + 1024, 16)), (A("nIb"), vv(2 * h + b, 2 * h + b + 1))], 64)
                         for m, a in enumerate(part)], []))
                 act(DA(h, part[0], part[-1] + 1, 64 * b, 64 * b + 64), A(bank, 0, 64 * len(part)), 64 * len(part), AF.Abs)
-                ops[-1]["r"].append(("turn", 0, 1))
-                if b == 1:
-                    mm([(A("ps%d" % (2 + h), a, 128, 16), DA(h, a, a + 1, 0, 128), A("G32"), 8, not nm, not nm) for a in part])
-            for j in range(nm // 4):
-                lst = []
-                for a in range(4 * j, 4 * j + 4):
-                    eo = A("ps%d" % (2 + h), a, 128, 16)
-                    lst += [(eo, A("X", 2048 * h + a, 2048 * h + 2048, 16), A("nG32"), 8, False, False), (eo, DA(h, a, a + 1, 0, 128), A("G64"), 8, False, a == nm - 1)]
-                mm(lst)
-            tt(hs("nf", h), EB(h, 0), hs("Hs", h), 128, ALU.is_gt)
-            tt(hs("tt", h), EB(h, 0), hs("nf", h), 128, ALU.mult)
-            scan(hs("fs", h), hs("d0f", h), hs("tt", h), 128)
-            scan(AR("ps%d" % (2 + h), 128, 256), AR("d0r", 128 * h, 128 * h + 128), AR("fs", 128 * h, 128 * h + 128), 128)
-            rs = EB(h, 1)
-            tt(hs("OHT", h), rs, hs("tt", h), 128, ALU.is_equal)
+                if TURN:
+                    ops[-1]["r"].append(("turn", 0, 1))
+            if nm:
+                mm([(eo(a), A("X", 2048 * h + a, 2048 * h + 2048, 16), A("nGG"), 64, False, False) for a in range(nm)])
+            for lo in range(0, 128, MB):
+                x0 = 2048 * h + 16 * lo
+                for a in range(nm):
+                    tt(DA(h, a, a + 1, lo, lo + MB), A("X", x0 + a, x0 + 16 * MB, 16), A("ps4", 128 * h + lo, 128 * h + lo + MB), MB, ALU.max)
+            he = A(E, 128, 256)
+            mm([(he, hs("hn", h), A("nIb"), 128, False, False)] + ([] if first else [(he, hs("hr", h), A("nRm"), 128, False, False)]))
+            for j in range(0, nm, 4):
+                mm([(eo(a), DA(h, a, a + 1, 0, 128), A("GG2"), 64, False, a == 15) for a in range(j, min(nm, j + 4))])
+            for j in range(nm, 16, 8):
+                mm([(eo(a), DA(h, a, a + 1, 0, 128), A("GG"), 64, False, a == 15) for a in range(j, min(16, j + 8))])
+            act(hs("Sg", h), he, 128, AF.Sign, bias=-2048.5)
+            tt(hs("key", h), A(E, 0, 128), hs("Sg", h), 128, ALU.min)
+            scan(hs("fs", h), hs("d0f", h), hs("key", h), 128)
+            scan(AR(E, 384, 512), AR("d0r", 128 * h, 128 * h + 128), AR("fs", 128 * h, 128 * h + 128), 128)
+            rs = A(E, 384, 512)
+            tt(hs("OHT", h), rs, hs("key", h), 128, ALU.is_equal)
             tt(hs("nhm", h), rs, A("tm"), 128, ALU.is_ge)
-            act(hs("q", h), rs, 128, AF.Relu, bias=16.0, scale=-1.0)
-            mm(grp(A("ps5", 128, 256), [(hs("OHT", h), A("Ib"))], 128))
+            if first:
+                ts(hs("OHs", h), rs, 128, -1.0, ALU.is_equal)
+            else:
+                tt(hs("OHs", h), rs, hs("dl", h), 128, ALU.is_equal)
             sl = 256 * h
-            tt(A("sel", sl, sl + 128), A("ps5", 128, 256), hs("c16", h), 128, ALU.mult)
-            w = 8 if last else 16
+            q0, q1 = (1, 3) if last else (0, 4)
+            mm([(A(cb, 64 * q, 64 * q + 64), hs("OHT", h), A("Ib", 64 * (q // 2), 64 * (q // 2) + 64), 64, True, True) for q in range(q0, q1)]
+               + [(A(cb, 256, 320), hs("nhm", h), A("K8"), 64, True, True)])
+            tt(A("sel", sl + 64 * q0, sl + 64 * q1), A(cb, 64 * q0, 64 * q1), M("cpb", 4 * h + q0, 4 * h + q1, 0, 64), 64 * (q1 - q0), ALU.mult)
+            tt(hs("AW", h, 64), A(cb, 256, 320), hs("WG", h, 64), 64, ALU.mult)
+            lists = A(E, 128 + 4 * q0, 128 + 4 * q1)
+            mm([(lists, A("Mall", 15 - r, 143 - r), A("sel", sl + 64 * q0 + r, sl + 64 * q1, 16), 64, r == 0, False) for r in range(16)]
+               + [(A(E, 132, 140), hs("nhm", h), A("G13"), 64, False, True)])
+            tt(h8("xm"), A(E, 132, 140), A("kc", 16 * t + 8 * h, 16 * t + 8 * h + 8), 8, ALU.min)
+            ts(h8("xl16"), h8("xm"), 8, 2048.0, ALU.add)
+            mm(grp(A(cb, 384, 512), [(A("Ib"), hs("irow", h)), (A("nBO"), A("sel", sl + 64, sl + 192)), (hs("OHs", h), A("I13"))], 128))
+            act(hs("Z", h), A(cb, 384, 512), 128, AF.Relu, bias=float(nb - 2048 - 8192))
+            tt(IND(A("recf"), h8("offo")), hs("Ws", h), hs("Z", h), 128, ALU.add)
+            plus(ENG["Y"], hs("Y16", h), IND(A("boxt", 0, nb + TH), h8("xl16")), 128, drc)
             if not last:
-                tt(A("sel", sl + 128, sl + 256), A("ps5", 128, 256), hs("p16", h), 128, ALU.mult)
-            mm(grp(EB(h, 2), [(hs("q", h), A("Ib")), (A("Dc"), hs("rot", h))], 128))
-            act(hs("Da", h), EB(h, 2), 128, AF.Abs, bias=-16.0)
-            mm(grp(EB(h, 2), [(A("Ib"), hs("irow", h)), (A("nBO"), A("sel", sl, sl + 128)), (A("nI13"), hs("Da", h))], 128))
-            act(hs("Z", h), EB(h, 2), 128, AF.Relu, bias=float(nb - 2048))
-            tt(IND(A("recf"), hs("offo", h, 8)), hs("Ws", h), hs("Z", h), 128, ALU.add)
-            mm(tolist(A("ps5", 64, 64 + w), "sel", sl, sl + 16 * w) + [(A("ps5", 64, 72), hs("nhm", h), A("G13"), 8, False, True),
-                                                                      (A("ps5", 80, 88), hs("nhm", h), A("G13"), 8, True, True)])
-            tt(hs("xm", h, 8), A("ps5", 64, 72), A("kc", 16 * t + 8 * h, 16 * t + 8 * h + 8), 8, ALU.min)
-            ts(hs("xl16", h, 8), hs("xm", h, 8), 8, 2048.0, ALU.add)
-            ts(hs("Y16", h), IND(A("boxt", 0, nb + TH), hs("xl16", h, 8)), 128, drc, ALU.add)
+                nbx = A("boxt", nb + 128 * h, nb + 128 * h + 128)
+                mm(grp(A(cb, 256, 384), [(A("Hw"), hs("Y16", h)), (A("Hw"), nbx)], 128))
+                ts(nbx, A(cb, 256, 384), 128, MAG, ALU.add, -MAG, ALU.add)
             ts(hs("m16", h), hs("Y16", h), 128, 256.0, ALU.is_ge, 256.0, ALU.mult)
             if last:
-                tt(hs("yvb", h), hs("Y16", h), hs("m16", h), 128, ALU.subtract)
+                mm(grp(A(E, 0, 128), [(A("Ib"), hs("Y16", h)), (A("nIb"), hs("m16", h))], 128))
+                act(hs("yvb", h), A(E, 0, 128), 128, AF.Copy)
             else:
-                snd, nxl = "send%d" % t, "land%d" % (t + 1)
+                nxl = "land%d" % (t + 1)
+                lst = []
+                for b in range(2):
+                    lst += grp(A(E, 64 + 144 * b, 128 + 144 * b), [(A("BO"), A("sel", sl + 192 * b, sl + 192 * b + 64))], 64)
+                for b in range(2):
+                    x0 = 128 * h + 64 * b
+                    lst += grp(A(E, 144 * b, 144 * b + 64), [(A("Ib"), A("Y16", x0, x0 + 64)), (A("nIb"), A("m16", x0, x0 + 64))], 64)
+                mm(lst)
                 qs = [q for q in (2 * h, 2 * h + 1) if q != rank]
-                if h != own:
-                    cp(M(snd, 2 * h, 2 * h + 2, 64, 68), A("ps5", 72, 80), 8)
-                    tt(M(snd, 2 * h, 2 * h + 2, 0, 64), hs("Y16", h), hs("m16", h), 128, ALU.subtract)
-                else:
-                    for q in qs + [rank]:
-                        dst = nxl if q == rank else snd
-                        cp(M(dst, q, q + 1, 64, 68), A("ps5", 72 + 4 * (q % 2), 76 + 4 * (q % 2)), 4)
-                        tt(M(dst, q, q + 1, 0, 64), A("Y16", 64 * q, 64 * q + 64), A("m16", 64 * q, 64 * q + 64), 64, ALU.subtract)
+                slot = {q: (3 + q if q == rank else (q % 2 if h != own else (2 if par else 7))) for q in (2 * h, 2 * h + 1)}
+                act(M(nxl, slot[2 * h], slot[2 * h + 1] + 1, 0, MW, slot[2 * h + 1] - slot[2 * h]), A(E, 0, 2 * MW), 2 * MW, AF.Copy)
 
-                def send(qs=qs, snd=snd, nxl=nxl, sem="arr%d%d" % (t + 1, k)):
+                def send(qs=qs, slot=slot, nxl=nxl, sem="arr%d%d" % (t + 1, k)):
                     trs = []
                     for q in qs:
                         rid, pid, _se = topo.addr(cores[q])
                         trs.append(RemoteDMATransfer(dst_ids=[DstId(rid=rid, pnc=pid)], dma_engine_mask=sum(1 << e for e in lanes(topo, cores, rank, q)),
-                                                     remote_sem=T.sem[sem], src=T[snd][:, q, 0:68], dst=T[nxl][:, rank, 0:68]))
+                                                     remote_sem=T.sem[sem], src=T[nxl][:, slot[q], :], dst=T[nxl][:, 3 + rank, :]))
                     g.remote_dma_fused(trs, local_sem=T.sem.sent)
                     return None
-                op("g", send, [M(snd, q, q + 1, 0, 68) for q in qs], [(None, ("net%d" % t, k, k + 1))], 300.0, sem="none")
-                op("r", None, [(None, ("net%d" % t, k, k + 1))], [M(nxl, q, q + 1, 0, 72) for q in qs], 0.0,
+                net = (None, [("net%d" % t, k, k + 1)], [])
+                op("g", send, [M(nxl, slot[q], slot[q] + 1, 0, MW) for q in qs], [net], 300.0, sem="none")
+                op("r", None, [net], [M(nxl, 3 + q, 4 + q, 0, MW) for q in qs], 0.0,
                    sem="arr%d%d" % (t + 1, k), inc=sum(len(lanes(topo, cores, q, rank)) for q in qs), lat=REM)
-            tt(hs("askw", h, 8), A("ps5", 80, 88), hs("wn", h, 8), 8, ALU.mult)
-            mm(grp(EB(h, 3), [(A("nI11"), hs("ones", h)), (hs("tt", h), A("If5"))], 128))
-            tt(hs("B1", h), EB(h, 3), hs("rot", h), 128, ALU.mult)
-            mm([(A("ps6", 128 * h, 128 * h + 128), hs("q", h), A("BIb"), 128, False, False)])
-            pairs("eqn", "n16", "nl32", "askw", list(range(8 * h, 8 * h + 8)), h == own)
+            sums(TH, "eqn", "AW", list(range(8 * h, 8 * h + 8)), k == 1)
+            if not first:
+                mm(grp(rs, [(hs("key", h), A("I11"))], 128))
+                tt(hs("B1", h), rs, hs("rot", h), 128, ALU.mult)
         if last:
             dma("s", "d_yr0", H(T.yr[:, 0:V // 2]), A("recf", 0, V // 2), 1024)
             dma("a", "d_yr1", H(T.yr[:, V // 2:V]), A("recf", V // 2, V), 1024)
             dma("s", "d_yv", H(T.yv[:]), A("yvb"), 64)
-        else:
-            mm(grp(A("ps7", 0, TH), [(A("Ib"), A("Y16")), (A("Ib"), A("boxt", nb, nb + TH)), (A("nhI"), A("ones"))], TH))
-            act(A("a1"), A("ps7", 0, TH), TH, AF.Identity, bias=MAG, scale=0.5)
-            act(A("boxt", nb, nb + TH), A("a1"), TH, AF.Identity, bias=-MAG)
-        act(A("Fn"), A("ps6", 0, TH), TH, AF.Sign)
+        act(P8("Fn", 0, TH), P8("ps6", TH, 2 * TH), TH, AF.Sign, bias=2.0 ** -115)
         if not last:
-            places("offn", "Fn", "nl32", A("kc", 80, 96))
+            mm(places("Fn", A("scn", 15, TH, 16)))
+            tt(A("on32"), A("ps6", 256, 272), A("spn"), 16, ALU.min)
+            ts(A("offn"), A("on32"), 16, C["h2"], ALU.add)
             ts(IND(A("nxt"), A("offn")), A("ident", 0, TH), TH, 1.0, ALU.mult, float(ns), ALU.add)
-        for h in horder:
-            mm(grp(EB(h, 3), [(hs("tt", h), A("If5")), (A("RTb"), hs("B1", h)), (A("nBO12"), hs("Fn", h))], 128))
-            act(A("ht", ns + 128 * h, ns + 128 * h + 128), EB(h, 3), 128, AF.Relu, bias=-65536.0)
+        mm(sum([grp(hs("ps6", h), [(hs("key", h), A("I11")), (P8("E8n", 0, 128), P8("Fn", 128 * h, 128 * h + 128))]
+                    + ([] if first else [(A("RTb"), hs("B1", h))]), 128) for h in horder], []))
+        act(A("ht", ns, ns + TH), A("ps6", 0, TH), TH, AF.Relu, bias=-2048.0)
         dma("s", "d_yh%d" % t, H(T.yh[:, TH * t:TH * t + TH]), A("ht", ns, ns + TH), 128)
     return ops, Q
 
@@ -524,30 +598,77 @@ def schedule(ops, deps):
             bpre[j].append(i)
             bpost[i].append((j, gap + ops[i]["dur"]))
     prio = [0.0] * n
-    for i in range(n - 1, -1, -1):
+    for i in reversed(passes(ops, fpre, fpost, prio, False)[0]):
         prio[i] = max([prio[k] + gap for k, gap in fpost[i]] + [ops[i]["dur"] + ops[i]["lat"]])
     seed = [12345]
 
     def rnd():
         seed[0] = (seed[0] * 1103515245 + 12345) % 2147483648
         return seed[0] / 2147483648.0
+    cases = []
+    for lat, f, fx, rem in CASES:
+        dur = [f * (o["dur"] + (fx - 1.0) * o["x"]) for o in ops]
+        cases.append((dur, [[(j, dur[j] + ((rem if ops[j]["e"][0] == "r" else ops[j]["lat"]) + lat if w else 0.0)) for j, w in deps[i].items()] for i in range(n)]))
+
+    def length(order):
+        tot = 0.0
+        for dur, pre in cases:
+            start, free, end = [0.0] * n, {}, 0.0
+            for i in order:
+                e = ops[i]["e"]
+                t = free.get(e, 0.0)
+                for j, gap in pre[i]:
+                    if start[j] + gap > t:
+                        t = start[j] + gap
+                start[i] = t
+                free[e] = t + dur[i]
+                if t + dur[i] + ops[i]["lat"] > end:
+                    end = t + dur[i] + ops[i]["lat"]
+            tot += end
+        return tot / len(cases)
     best = None
-    for it in range(30):
+    for it in range(20):
         res = passes(ops, fpre, fpost, prio, False)
-        if best is None or max(res[2]) < max(best[2]):
-            best, base = res, prio
+        val = length(res[0])
+        if best is None or val < low:
+            best, base, low = res, prio, val
         prio = passes(ops, bpre, bpost, [x + 300.0 * rnd() for x in res[2]], True)[2]
     kinds = {}
-    kind = [kinds.setdefault((o["e"], o["w"][0][0] if o["e"] == "p" else o["w"][0][0].rstrip("0123456789"), o["w"][0][1] // 128), len(kinds)) for o in ops]
+    kind = [kinds.setdefault((o["e"], o["w"][0][0] if o["e"][0] == "p" else o["w"][0][0].rstrip("0123456789"), o["w"][0][1] // 128), len(kinds)) for o in ops]
     shift = [0.0] * len(kinds)
     for it in range(ROUNDS):
         new = list(shift)
         for _ in range(1 + int(4 * rnd())):
             new[int(rnd() * len(kinds))] += NOISE * (2 * rnd() - 1)
         res = passes(ops, fpre, fpost, [base[i] + new[kind[i]] for i in range(n)], False)
-        if max(res[2]) <= max(best[2]):
-            best, shift = res, new
+        val = length(res[0])
+        if val <= low:
+            best, shift, low = res, new, val
     return best
+
+
+ORDERS = {}
+
+
+def orders(g, core, T, topo):
+    if not ORDERS:
+        ops, deps, sends = [], [], {}
+        for rank in (0, 2):
+            part = build(g, core, T, topo, rank)[0]
+            base = len(ops)
+            deps += [{j + base: w for j, w in d.items()} for d in depend(part)]
+            ops += [dict(o, e=o["e"] + str(rank)) for o in part]
+        n = len(ops) // 2
+        for i, o in enumerate(ops):
+            if o["e"][0] == "r" and o["sem"][-1] == "0":
+                for j in list(deps[i]):
+                    if ops[j]["sem"] == "none":
+                        deps[i][(j + n) % (2 * n)] = True
+        res = schedule(ops, deps)
+        ORDERS["all"] = (ops, deps, res)
+        for own in range(2):
+            ORDERS[own] = [i - own * n for i in res[0] if i // n == own]
+    return ORDERS
 
 
 def rank_program(g, core, T, topo):
@@ -556,7 +677,7 @@ def rank_program(g, core, T, topo):
         return
     ops, Q = build(g, core, T, topo, rank)
     deps = depend(ops)
-    order, start, fin = schedule(ops, deps)
+    order = orders(g, core, T, topo)[rank // 2]
     count = {}
     mark = {}
     seen = {}

@@ -9,12 +9,16 @@ V, NB, S0, TH, RO = 2048, 3072, 512, 256, 4
 ND = [[48, 48], [48, 48], [48, 48], [48, 48]]
 NM = [[8, 8], [8, 8], [8, 8], [8, 8]]
 MB = 64
-XC = [64, 16]
-ENG = {"s": "a", "n": "a", "hn": "a", "nn": "a", "Y": "v"}
-DB, CB = ["ps0", "ps1"], ["ps5", "ps5"]
+XC, XV = [64, 64], [64, 64]
+ENG = {"s": "a", "n": "a", "hn": "a", "nn": "a", "Y": "v", "shpt": "a", "nxt": "a"}
+OF = 64
+DB, CB = ["ps0", "ps1"], ["ps4", "ps5"]
 TURN = True
-GC, SC, LAT, PEC, CYC, REM, KB, DM0 = 1.56, 3.8, 230.0, 0.45, 0.9, 1800.0, 4.0, 1200.0
-ROUNDS, NOISE, AHEAD = 1000, 1500.0, 0.5
+SHORT, EXACT, SEEN, ZB = [False, True], [False, True], True, "ps7"
+PT, PS = 4, 2
+GC, SC, LAT, PEC, CYC, REM, KB, DM0 = 1.56, 3.8, 260.0, 0.45, 0.9, 1800.0, 4.0, 1200.0
+FIRST, PAIR, MOVES, WIDE = 1500.0, 0.0, [0.3, 0.35, 0.7], 4000.0
+ROUNDS, NOISE, AHEAD, SWAPS, HEAT, SEED = 3000, 1300.0, 0.5, 5000, 300.0, 3
 CASES = [(130.0, 0.95, 0.9, 1300.0), (200.0, 0.92, 1.0, 1500.0), (300.0, 1.0, 1.0, 2400.0), (200.0, 1.35, 1.25, 1800.0)]
 MW = 136
 MAG = 12582912.0
@@ -46,20 +50,23 @@ _sb("drb", 8, BF)
 _sb("land1 land2 land3", [8, MW], F16)
 _sb("ol16 sl16 nl16 xl16 offo offn", 16, U16)
 _sb("cl16", TH, U16)
+_sb("ol1 ol2 ol3", 48, U16)
 _sb("ol32 nl32 xm of32 on32 il spn", 16, F32)
 _sb("olh", 16, F16)
 _sb("kc", 64, F32)
 _sb("Wi c32 p32", TH, I32)
-_sb("cpb", [8, 64], F16)
+_sb("cpb cp1", [8, 64], F16)
+_sb("KF", 64, F16)
+_sb("kf", 8, F32)
 _sb("s16 n16 nn16 orow Y16 m16 hn hr B1 hold scs scn key", TH, F16)
 _sb("sel", 512, F16)
 _sb("Kt", RO * TH, F16)
-_sb("rot Sg OHT nhm OHs nfr Fo Fn yvb ones irow Kc Vm", TH, BF)
-_sb("W1 Ws d0f d0r dl fs Z", TH, F32)
+_sb("rot Sg OHT nhm OHs OHf Fo Fn yvb ones irow Kc Vm", TH, BF)
+_sb("W1 Ws d0f d0r dl fs Z n32", TH, F32)
 _sb("eqo eqn", 2560, BF)
 _sb("col", 64, F32)
 _sb("rowg rowr tm RTI wx", 128, F32)
-_sb("Ib nIb I11 I12 nI12 I13 I23 nI11 BO nBO E8 E8n nRm RTb Dc WG AW", 128, BF)
+_sb("Ib nIb I11 I12 nI12 I13 I23 nI11 BO nBO E8 E8n nRm RTb R12 Dc WG AW", 128, BF)
 _sb("Hw", 128, F16)
 _sb("Mall M8", 144, BF)
 _sb("K8", 64, BF)
@@ -69,7 +76,7 @@ for _k in range(8):
     SCRATCH["ps%d" % _k] = ("psum", [128, 512], F32)
 
 DMAS = ["d_ob", "d_tv", "d_dr", "d_rec", "d_shp", "d_box", "d_bnd", "d_yh0", "d_yh1", "d_yh2", "d_yh3", "d_yv", "d_yr0", "d_yr1"]
-SEMAPHORES = ["cv", "ca", "cp", "cg", "sent"] + ["arr%d%d" % (t, k) for t in range(1, RO) for k in range(2)] + DMAS
+SEMAPHORES = ["cv", "ca", "cp", "cg", "sent"] + ["%s%d%d" % (s, t, k) for s in ("arr", "lst") for t in range(1, RO) for k in range(2)] + DMAS
 ENG_SEM = {"v": "cv", "a": "ca", "p": "cp", "g": "cg"}
 
 
@@ -82,7 +89,7 @@ def lanes(topo, cores, src, dst):
 
 
 def build(g, core, T, topo, rank):
-    ops = []
+    ops, tally, stage = [], {}, [-1]
     cores = T.cores
     Q = {"v": g.vector, "a": g.scalar, "p": g.tensor, "g": g, "s": g.sync}
 
@@ -115,6 +122,10 @@ def build(g, core, T, topo, rank):
             r.extend(x[2])
         x = dur - 60.0 if any(isinstance(y, tuple) and y[2] for y in rd + wr) else 0.0
         ops.append({"e": eng, "fn": fn, "r": r, "w": w, "dur": dur, "sem": sem, "inc": inc, "lat": lat, "x": x})
+        name = (eng, w[0][0] if eng == "p" else w[0][0].rstrip("0123456789"))
+        name = (eng, "E") if name[1] in ("ps2", "ps3") else name
+        tally[name] = tally.get(name, 0) + 1
+        ops[-1]["like"], ops[-1]["t"] = (name, tally[name], min(stage[0], 1)), stage[0]
 
     def ap(x):
         return x[0] if isinstance(x, tuple) else x
@@ -153,6 +164,9 @@ def build(g, core, T, topo, rank):
 
     def act(out, in_, n, f, bias=0.0, scale=1.0, extra=0.0):
         op("a", lambda: g.scalar.activation(out[0], in_[0], f, bias=ap(bias), scale=ap(scale)), [in_, scale, bias], [out], cost("a", n, out, [in_]) + extra)
+
+    def silu(out, in_, n, new):
+        op("a", lambda: g.scalar.activation(out[0], in_[0], AF.Silu), [in_], [out], cost("a", n, out, [in_]) + (1500.0 if new else 0.0))
 
     def plus(eng, out, in_, n, add=None):
         if eng == "a":
@@ -207,8 +221,8 @@ def build(g, core, T, topo, rank):
         lo, hi = TH + 448 * k, TH + 448 * (k + 1)
         iota(A("ident", lo, hi), [[1, hi - lo]], lo, 0, hi - lo)
     for k in range(3):
-        iota(A("nxt", 512 * k, 512 * k + 512), [[1, 512]], 512 * k, 0, 512)
-    C = {n: A("col", 4 * k, 4 * k + 1) for k, n in enumerate("pc rc gc nc pvc dc gm p16 hc r1 h2 p15 wb".split())}
+        iota(A("nxt", 512 * k, 512 * k + 512), [[1, 512]], 512 * k + OF, 0, 512)
+    C = {n: A("col", 4 * k, 4 * k + 1) for k, n in enumerate("pc rc gc nc pvc dc gm p16 hc r1 h2 p15 wb hk".split())}
     rowm, rowx, row8 = A("ident", 0, 128), A("ident", 0, 144), A("ident", 0, 128, 16)
     ts(A("pci", 4, 5), A("pci", 0, 1), 1, 15, ALU.bitwise_and)
     cp(C["pc"], A("pci", 0, 1), 1)
@@ -223,7 +237,8 @@ def build(g, core, T, topo, rank):
     ts(C["p16"], C["pc"], 1, 16.0, ALU.mult)
     ts(C["p15"], C["pc"], 1, 16.0, ALU.mult, 15.0, ALU.add)
     ts(C["r1"], C["rc"], 1, 1.0, ALU.add)
-    ts(C["hc"], C["rc"], 1, 15.0, ALU.not_equal, 2048.0, ALU.mult)
+    ts(C["hk"], C["rc"], 1, 15.0, ALU.not_equal, 2048.0, ALU.mult)
+    ts(C["hc"], C["hk"], 1, -float(OF), ALU.add)
     ts(C["h2"], C["hc"], 1, 2048.0, ALU.add)
     ts(C["wb"], C["rc"], 1, -LR, ALU.mult, L0, ALU.add)
     ts(A("Ib"), rowm, 128, C["pc"], ALU.is_equal)
@@ -241,7 +256,7 @@ def build(g, core, T, topo, rank):
         lo, hi = 512 * k, 512 * k + 512
         cp(P8("shph", lo, hi), P8("shpi", lo, hi), 512)
         mm([(A("ps%d" % k), P8("E8", 0, 128), P8("shph", lo, hi), 512, True, True)])
-        act(A("shpt", lo, hi), A("ps%d" % k), 512, AF.Copy)
+        act(A("shpt", lo, hi), A("ps%d" % k), 512, AF.Identity, bias=float(OF))
     tt(A("rowr"), rowm, A("rowg"), 128, ALU.subtract)
     for n, s in (("GG", 1.0), ("GG2", 2.0), ("nGG", -1.0)):
         ts(A(n, 0, 8), row8, 8, C["gc"], ALU.is_equal, s / 2048, ALU.mult)
@@ -266,6 +281,10 @@ def build(g, core, T, topo, rank):
     ts(A("RTb"), rowm, 128, C["pvc"], ALU.is_equal)
     tt(A("RTb"), A("RTb"), A("Ib"), 128, ALU.subtract)
     act(A("RTI"), A("RTb"), 128, AF.Copy)
+    act(A("R12"), A("RTb"), 128, AF.Identity, scale=4096.0)
+    iota(A("kf"), [[128, 8]], NB - 2048, 1, 8)
+    for j in range(2 * RO):
+        ts(A("KF", 8 * j, 8 * j + 8), row8, 8, C["gc"], ALU.is_equal, A("kf", j, j + 1), ALU.mult)
     ts(A("tm"), A("rowr"), 128, C["rc"], ALU.not_equal, 1.0e7, ALU.mult)
     act(A("tm"), A("tm"), 128, AF.Identity, bias=-1.0 + 16 * U)
     ts(A("Y16", 0, 128), A("rowr"), 128, C["rc"], ALU.is_equal, 8192.0, ALU.mult)
@@ -292,17 +311,21 @@ def build(g, core, T, topo, rank):
     for k in range(4):
         conv(A("recf", 512 * k, 512 * k + 512), A("rect", 512 * k, 512 * k + 512), 512)
 
-    def pairs(buf, row, keys, cs, blocks):
+    def pairs(buf, row, keys, cs, blocks, less=None):
         for c in cs:
             lo = 64 * (c // 4) if blocks else 16 * c
-            ts(A(buf, eoff[c] + lo % 64, eoff[c + 1]), row(lo), TH - lo, A(keys, c, c + 1), ALU.is_equal)
+            out = A(buf, eoff[c] + lo % 64, eoff[c + 1])
+            if less is None:
+                ts(out, row(lo), TH - lo, A(keys, c, c + 1), ALU.is_equal)
+            else:
+                ts(out, row(lo), TH - lo, A(keys, c, c + 1), ALU.subtract, less, ALU.is_equal)
 
     eoff = [sum(256 - 64 * (k // 4) for k in range(c)) for c in range(17)]
 
     def sums(lo, buf, wts, cs, last):
-        for c0 in range(0, len(cs), 4):
+        for c0 in range(0, len(cs), PS):
             lst = []
-            for c in cs[c0:c0 + 4]:
+            for c in cs[c0:c0 + PS]:
                 w = A(wts, 8 * c, 8 * c + 8)
                 lst.append((P8("ps6", lo + 16 * c, lo + TH), w, A(buf, eoff[c] + 16 * c % 64, eoff[c + 1]), TH - 16 * c, False, False))
                 lst.append((P8("ps6", lo + 16 * c, lo + 16 * c + 16), w, A("Dg"), 16, False, last and c == cs[-1]))
@@ -315,8 +338,29 @@ def build(g, core, T, topo, rank):
     own, par = rank // 2, rank % 2
     horder = [1 - own, own]
     vo, oo, po = 8 * par, 64 + 8 * par, 128 - 124 * par
+
+    def pieces(t, h):
+        if h != own:
+            return [(128 * h, 128, A("ol%d" % t, 32, 40))]
+        return [(64 * rank, 64, A("ol%d" % t, 16 + 12 * par, 20 + 12 * par)), (64 * (rank ^ 1), 64, A("ol%d" % t, 40, 44))]
+
+    def send(t, k, sem, parts, extra):
+        def fn():
+            trs = []
+            for q, src, dst, _here in parts:
+                rid, pid, _se = topo.addr(cores[q])
+                trs.append(RemoteDMATransfer(dst_ids=[DstId(rid=rid, pnc=pid)], dma_engine_mask=sum(1 << e for e in lanes(topo, cores, rank, q)),
+                                             remote_sem=T.sem[sem], src=src[0], dst=dst[0]))
+            g.remote_dma_fused(trs, local_sem=T.sem.sent)
+            return None
+        net = (None, [("net" + sem, 0, 1)], [])
+        op("g", fn, [x[1] for x in parts], [net], 300.0, sem="none", lat=extra)
+        op("r", None, [net], [x[3] for x in parts], 0.0, sem=sem, inc=sum(len(lanes(topo, cores, x[0], rank)) for x in parts), lat=REM)
+
     for t in range(RO):
         first, last = t == 0, t == RO - 1
+        tally.clear()
+        stage[0] = t
         land, nb, ns = "land%d" % t, NB + TH * t, S0 + TH * t
         drc = A("drb", t, t + 1)
         hs = lambda n, h, w=128: A(n, w * h, w * h + w)
@@ -336,17 +380,18 @@ def build(g, core, T, topo, rank):
                 cp(hs("cl16", h), hs("c32", h), 128)
                 ts(hs("p32", h), IND(A("rect"), h8("ol16")), 128, 12, ALU.arith_shift_right)
             else:
-                cp(h8("ol16"), M(land, 3 + 2 * h, 5 + 2 * h, po, po + 4), 8)
                 conv(h8("ol32"), M(land, 3 + 2 * h, 5 + 2 * h, po, po + 4), 8)
-                cp(hs("Wi", h), IND(A("recf", 0, V), h8("ol16")), 128)
-                ts(hs("c32", h), hs("Wi", h), 128, 4095, ALU.bitwise_and)
-                cp(hs("cl16", h), hs("c32", h), 128)
+                for lo, n, ol in pieces(t, h):
+                    cp(A("Wi", lo, lo + n), IND(A("recf", 0, V), ol), n)
+                    ts(A("c32", lo, lo + n), A("Wi", lo, lo + n), n, 4095, ALU.bitwise_and)
+                    cp(A("cl16", lo, lo + n), A("c32", lo, lo + n), n)
                 ts(hs("p32", h), hs("Wi", h), 128, 12, ALU.arith_shift_right)
             ts(cc(h), hs("cl16", h), 128, -2048.0, ALU.add)
             conv(pp(h), hs("p32", h), 128)
             ts(A("boxt", nb + 128 * h, nb + 128 * h + 128), vv(2 * h, 2 * h + 2), 128, drc, ALU.subtract)
             if not first:
-                plus(ENG["s"], hs("s16", h), IND(A("shpt", 0, V), h8("ol16")), 128)
+                for lo, n, ol in pieces(t, h):
+                    plus(ENG["s"], A("s16", lo, lo + n), IND(A("shpt", 0, V), ol), n)
                 scan(hs("scs", h), hs("hold", h), hs("s16", h), 128)
                 ts(h8("sl16"), A("scs", 128 * h + 15, 128 * h + 128, 16), 8, C["hc"], ALU.add)
                 plus(ENG["n"], hs("n16", h), IND(A("nxt", 0, 1536), h8("sl16")), 128)
@@ -354,27 +399,34 @@ def build(g, core, T, topo, rank):
                 plus(ENG["n"], hs("n16", h), IND(A("shpt", 0, V), h8("ol16")), 128)
             scan(hs("scn", h), hs("hold", h), hs("n16", h), 128)
             ts(h8("nl16"), A("scn", 128 * h + 15, 128 * h + 128, 16), 8, C["hc"], ALU.add)
-            ts(h8("nl32"), A("scn", 128 * h + 15, 128 * h + 128, 16), 8, C["hc"], ALU.add)
-            plus(ENG["hn"], hs("hn", h), IND(A("ht", 0, ns), h8("nl16")), 128, -2048.0)
+            conv(h8("nl32"), A("scn", 128 * h + 15, 128 * h + 128, 16), 8)
+            if not last and ENG["shpt"] == "a":
+                conv(hs("n32", h), hs("n16", h), 128)
+            plus("v" if first else ENG["hn"], hs("hn", h), IND(A("bnd") if first else A("ht", 0, ns), h8("nl16")), 128, -2048.0)
             S7 = lambda k: A("ps7", 128 * k, 128 * k + 128)
+            short = SHORT[horder.index(h)]
             if not first:
-                if ENG["nn"] == "a":
-                    plus("a", hs("nn16", h), IND(A("nxt", 0, 1536), h8("nl16")), 128)
-                else:
-                    tt(hs("nfr", h), IND(A("nxt", 0, 1536), h8("nl16")), hs("n16", h), 128, ALU.not_equal)
-                mm(grp(S7(0), [(A("I12"), hs("n16", h)), (A("nI12"), hs("s16", h)), (A("nI11"), hs("ones", h))], 128))
-                act(hs("rot", h), S7(0), 128, AF.Sign, bias=2048.0)
-                tt(hs("hr", h), hs("hn", h), S7(0), 128, ALU.min)
-                mm(grp(S7(1), [(hs("rot", h), A("Dc"))], 128) + grp(S7(2), [(A("I23"), hs("rot", h)), (A("I12"), pp(h)), (A("Ib"), cc(h))], 128))
-                act(A("d0f", 128 * h + 1, 128 * h + 128, 16), A("ps7", 129, 256, 16), 8, AF.Identity, bias=-U, scale=16 * U)
-                act(A("d0r", 128 * h, 128 * h + 128, 16), A("ps7", 129, 256, 16), 8, AF.Identity, bias=U, scale=-16 * U)
-                act(hs("dl", h), S7(1), 128, AF.Identity, bias=-1.0, scale=U)
-                act(hs("W1", h), S7(2), 128, AF.Relu, bias=2048.0 - 2.0 ** 23)
-                mm(grp(S7(3), [(A("I12"), pp(h)), (A("Ib"), cc(h)), (A("RTI"), hs("W1", h))], 128))
-            else:
-                mm(grp(S7(3), [(A("I12"), pp(h)), (A("Ib"), cc(h))], 128))
-            act(hs("Ws", h), S7(3), 128, AF.Identity, bias=2048.0)
-        chunks = [8 * h + c for h in horder for c in range(8)]
+                plus(ENG["nn"], hs("nn16", h), IND(A("nxt", 0, 1536), h8("nl16")), 128)
+                zz = lambda out, lo, n: grp(out, [(A("I12"), A("n16", lo, lo + n)), (A("nI12"), A("s16", lo, lo + n)), (A("nI11"), A("ones", 0, n))], n)
+                E = "ps%d" % (2 + h)
+                z = A(E, 320, 448)
+                mm(zz(z, 128 * h, 128) + (zz(A(E, 256, 320), 128 * h, 64) + zz(A(E, 448, 512), 128 * h + 64, 64) if short else []))
+                act(hs("rot", h), z, 128, AF.Sign, bias=2048.0)
+                if short:
+                    tt(M("cp1", 4 * h, 4 * h + 4, 0, 64), M("cpb", 4 * h, 4 * h + 4, 0, 64), A(E, 256, 512), 256, ALU.min)
+                tt(hs("hr", h), hs("hn", h), z, 128, ALU.min)
+                mm(grp(S7(0), [(hs("rot", h), A("Dc"))], 128))
+                act(A("d0f", 128 * h + 1, 128 * h + 128, 16), A("ps7", 1, 128, 16), 8, AF.Identity, bias=-U, scale=16 * U)
+                act(A("d0r", 128 * h, 128 * h + 128, 16), A("ps7", 1, 128, 16), 8, AF.Identity, bias=U, scale=-16 * U)
+                act(hs("dl", h), S7(0), 128, AF.Identity, bias=-1.0, scale=U)
+        long = [h for h in horder if not (first or SHORT[horder.index(h)])]
+        for h in long:
+            mm(grp(S7(1), [(A("I23"), hs("rot", h)), (A("I12"), pp(h)), (A("Ib"), cc(h))], 128))
+            act(hs("W1", h), S7(1), 128, AF.Relu, bias=2048.0 - 2.0 ** 23)
+        turned = lambda h: [(A("R12"), M("cp1", 4 * h, 4 * h + 4, 0, 64, 3)), (A("RTb"), M("cp1", 4 * h + 1, 4 * h + 3, 0, 64))]
+        mm(sum([grp(S7(2 + h), [(A("I12"), pp(h)), (A("Ib"), cc(h))] + ([] if first else [(A("RTI"), hs("W1", h))] if h in long else turned(h)), 128) for h in horder], []))
+        act(A("Ws"), A("ps7", 256, 512), TH, AF.Identity, bias=2048.0)
+        chunks = list(range(8, 16)) + list(range(8))
         if first:
             pairs("eqo", lambda lo: A("orow", lo, TH), "ol32", chunks, False)
         else:
@@ -386,53 +438,56 @@ def build(g, core, T, topo, rank):
         tt(A("of32"), A("ps6", 256, 272), A("il"), 16, ALU.min)
         ts(A("offo"), A("of32"), 16, 2048.0, ALU.add)
         if not last:
-            cp(IND(A("shpt"), A("offo")), A("n16"), TH)
-        pairs("eqn", lambda lo: A("n16", lo, TH), "nl32", chunks, False)
+            if ENG["shpt"] == "a":
+                silu(IND(A("shpt"), A("offo")), A("n32"), TH, first)
+            else:
+                cp(IND(A("shpt"), A("offo")), A("n16"), TH)
+        pairs("eqn", lambda lo: A("n16", lo, TH), "nl32", chunks, False, C["hk"])
         out = P8("ps6", TH, 2 * TH)
         if first:
             mm(grp(out, [(A("Z8"), A("irow"))], TH, stop=False))
-        elif ENG["nn"] == "a":
-            mm(grp(out, [(A("SB"), A("nn16")), (A("nSB"), A("n16"))], TH, stop=False))
         else:
-            mm(grp(out, [(A("SB"), A("nfr"))], TH, stop=False))
+            mm(grp(out, [(A("SB"), A("nn16")), (A("nSB"), A("n16"))], TH, stop=False))
         for k, h in enumerate(horder):
             h8 = lambda n: hs(n, h, 8)
             E, cb = "ps%d" % (2 + h), CB[k]
             nm, nd = NM[t][k], ND[t][k]
-            lo = 128 * h
-            for n in XC:
-                n = min(n, 128 * h + 128 - nd - lo)
+            flip = par if k else 0
+            done = 0
+            for eng, n in [("a", n) for n in XC] + [("v", n) for n in XV]:
+                n = min(n, (128 - nd if eng == "a" else 128) - done)
                 if n > 0:
-                    act(A("X", 16 * lo, 16 * (lo + n)), IND(A("boxt", 0, nb), A("cl16", lo, lo + n)), 16 * n, AF.Copy)
-                    if TURN:
+                    lo = 128 * h + (128 - done - n if flip else done)
+                    plus(eng, A("X", 16 * lo, 16 * (lo + n)), IND(A("boxt", 0, nb), A("cl16", lo, lo + n)), 16 * n)
+                    if TURN and eng == "a":
                         ops[-1]["w"].append(("turn", 0, 1))
-                    lo += n
-            if nd:
-                cp(A("X", 16 * lo, 16 * (lo + nd)), IND(A("boxt", 0, nb), A("cl16", lo, lo + nd)), 16 * nd)
+                    done += n
+            assert done == 128
             if nm:
                 terms = [(hs("ones", 0), A("Kt", TH * t, TH * t + TH)), (A("boxt", nb + 128 * h, nb + 128 * h + 128), A("Vm"))]
             else:
                 terms = [(hs("ones", 0), A("Kc"))]
             mm(grp(A(E, 0, 256), terms, 256, stop=False))
             if nm:
-                mm([(hs("ps4", h), A("Ib"), vv(2 * h, 2 * h + 2), 128, True, True)])
+                mm([(A(cb, 0, 128), A("Ib"), vv(2 * h, 2 * h + 2), 128, True, True)])
             eo = lambda a: A(E, a, 256, 16)
             aa = list(range(nm, 16))
-            tiles = [(b, aa[j:j + 8]) for b in range(2) for j in range(0, len(aa), 8)]
+            tiles = [(b ^ flip, aa[j:j + 8]) for b in range(2) for j in range(0, len(aa), 8)]
             for j, (b, part) in enumerate(tiles):
                 bank = DB[(len(tiles) * k + j) % len(DB)]
                 x0 = 2048 * h + 1024 * b
-                mm(sum([grp(A(bank, 64 * m, 64 * m + 64), [(A("Ib"), A("X", x0 + a, x0 + 1024, 16)), (A("nIb"), vv(2 * h + b, 2 * h + b + 1))], 64)
-                        for m, a in enumerate(part)], []))
+                for m0 in range(0, len(part), PT):
+                    mm(sum([grp(A(bank, 64 * m, 64 * m + 64), [(A("Ib"), A("X", x0 + part[m], x0 + 1024, 16)), (A("nIb"), vv(2 * h + b, 2 * h + b + 1))], 64)
+                            for m in range(m0, min(len(part), m0 + PT))], []))
                 act(DA(h, part[0], part[-1] + 1, 64 * b, 64 * b + 64), A(bank, 0, 64 * len(part)), 64 * len(part), AF.Abs)
                 if TURN:
                     ops[-1]["r"].append(("turn", 0, 1))
             if nm:
                 mm([(eo(a), A("X", 2048 * h + a, 2048 * h + 2048, 16), A("nGG"), 64, False, False) for a in range(nm)])
-            for lo in range(0, 128, MB):
+            for lo in list(range(0, 128, MB))[::-1 if flip else 1]:
                 x0 = 2048 * h + 16 * lo
                 for a in range(nm):
-                    tt(DA(h, a, a + 1, lo, lo + MB), A("X", x0 + a, x0 + 16 * MB, 16), A("ps4", 128 * h + lo, 128 * h + lo + MB), MB, ALU.max)
+                    tt(DA(h, a, a + 1, lo, lo + MB), A("X", x0 + a, x0 + 16 * MB, 16), A(cb, lo, lo + MB), MB, ALU.max)
             he = A(E, 128, 256)
             mm([(he, hs("hn", h), A("nIb"), 128, False, False)] + ([] if first else [(he, hs("hr", h), A("nRm"), 128, False, False)]))
             for j in range(0, nm, 4):
@@ -444,26 +499,55 @@ def build(g, core, T, topo, rank):
             scan(hs("fs", h), hs("d0f", h), hs("key", h), 128)
             scan(AR(E, 384, 512), AR("d0r", 128 * h, 128 * h + 128), AR("fs", 128 * h, 128 * h + 128), 128)
             rs = A(E, 384, 512)
-            tt(hs("OHT", h), rs, hs("key", h), 128, ALU.is_equal)
+            short = SHORT[k] or first
+            exact = short and (first or last or EXACT[k])
+            seen = lambda: tt(hs("OHs", h), rs, hs("dl", h), 128, ALU.is_equal)
+            if short and not first and (SEEN or last):
+                seen()
+            if not (last and exact):
+                tt(hs("OHT", h), rs, hs("key", h), 128, ALU.is_equal)
+            fits = hs("OHs" if first else "OHf", h)
+            if exact:
+                ts(fits, rs, 128, -1.0, ALU.is_equal)
             tt(hs("nhm", h), rs, A("tm"), 128, ALU.is_ge)
-            if first:
-                ts(hs("OHs", h), rs, 128, -1.0, ALU.is_equal)
-            else:
-                tt(hs("OHs", h), rs, hs("dl", h), 128, ALU.is_equal)
+            if not first and not (short and (SEEN or last)):
+                seen()
             sl = 256 * h
             q0, q1 = (1, 3) if last else (0, 4)
-            mm([(A(cb, 64 * q, 64 * q + 64), hs("OHT", h), A("Ib", 64 * (q // 2), 64 * (q // 2) + 64), 64, True, True) for q in range(q0, q1)]
+
+            def change():
+                if short:
+                    terms = [(A("I12"), pp(h)), (A("Ib"), hs("irow", h))] + ([] if first else [(A("R12"), M("cp1", 4 * h, 4 * h + 4, 0, 64, 3))]) + [(hs("OHs", h), A("I23"))]
+                    mm(grp(A(cb, 384, 512), terms, 128))
+                    act(hs("Z", h), A(cb, 384, 512), 128, AF.Identity, bias=float(nb) - 2.0 ** 23)
+                else:
+                    mm(grp(A(cb, 384, 512), [(A("Ib"), hs("irow", h)), (A("nBO"), A("sel", sl + 64, sl + 192)), (hs("OHs", h), A("I13"))], 128))
+                    act(hs("Z", h), A(cb, 384, 512), 128, AF.Relu, bias=float(nb - 2048 - 8192))
+                tt(IND(A("recf"), h8("offo")), hs("Ws", h), hs("Z", h), 128, ALU.max if short else ALU.add)
+            cb, ob = (ZB if short and ZB else CB[k]), CB[k]
+            if short and (SEEN or last):
+                change()
+            cb = ob
+            mm([(A(cb, 64 * q, 64 * q + 64), fits if exact and q in (1, 2) else hs("OHT", h), A("Ib", 64 * (q // 2), 64 * (q // 2) + 64), 64, True, True) for q in range(q0, q1)]
                + [(A(cb, 256, 320), hs("nhm", h), A("K8"), 64, True, True)])
             tt(A("sel", sl + 64 * q0, sl + 64 * q1), A(cb, 64 * q0, 64 * q1), M("cpb", 4 * h + q0, 4 * h + q1, 0, 64), 64 * (q1 - q0), ALU.mult)
             tt(hs("AW", h, 64), A(cb, 256, 320), hs("WG", h, 64), 64, ALU.mult)
             lists = A(E, 128 + 4 * q0, 128 + 4 * q1)
             mm([(lists, A("Mall", 15 - r, 143 - r), A("sel", sl + 64 * q0 + r, sl + 64 * q1, 16), 64, r == 0, False) for r in range(16)]
-               + [(A(E, 132, 140), hs("nhm", h), A("G13"), 64, False, True)])
-            tt(h8("xm"), A(E, 132, 140), A("kc", 16 * t + 8 * h, 16 * t + 8 * h + 8), 8, ALU.min)
-            ts(h8("xl16"), h8("xm"), 8, 2048.0, ALU.add)
-            mm(grp(A(cb, 384, 512), [(A("Ib"), hs("irow", h)), (A("nBO"), A("sel", sl + 64, sl + 192)), (hs("OHs", h), A("I13"))], 128))
-            act(hs("Z", h), A(cb, 384, 512), 128, AF.Relu, bias=float(nb - 2048 - 8192))
-            tt(IND(A("recf"), h8("offo")), hs("Ws", h), hs("Z", h), 128, ALU.add)
+               + [(A(E, 132, 140), hs("nhm", h), A("KF", 16 * t + 8 * h, 16 * t + 8 * h + 8) if exact else A("G13"), 64, False, True)])
+            if exact:
+                ts(h8("xl16"), A(E, 132, 140), 8, 2048.0, ALU.add)
+            if not last:
+                nol, qs = "ol%d" % (t + 1), [q for q in (2 * h, 2 * h + 1) if q != rank]
+                cp(A(nol, 16 * k, 16 * k + 16), A(E, 128, 144), 16)
+                at = lambda q: A(nol, 40 if k else 32 + 4 * (q % 2), 44 if k else 36 + 4 * (q % 2))
+                send(t, k, "lst%d%d" % (t + 1, k), [(q, A(nol, 16 * k + 12 * (q % 2), 16 * k + 12 * (q % 2) + 4), at(rank), at(q)) for q in qs],
+                     FIRST if first and k == 0 else 0.0)
+            if not exact:
+                tt(h8("xm"), A(E, 132, 140), A("kc", 16 * t + 8 * h, 16 * t + 8 * h + 8), 8, ALU.min)
+                ts(h8("xl16"), h8("xm"), 8, 2048.0, ALU.add)
+            if not (short and (SEEN or last)):
+                change()
             plus(ENG["Y"], hs("Y16", h), IND(A("boxt", 0, nb + TH), h8("xl16")), 128, drc)
             if not last:
                 nbx = A("boxt", nb + 128 * h, nb + 128 * h + 128)
@@ -485,19 +569,7 @@ def build(g, core, T, topo, rank):
                 qs = [q for q in (2 * h, 2 * h + 1) if q != rank]
                 slot = {q: (3 + q if q == rank else (q % 2 if h != own else (2 if par else 7))) for q in (2 * h, 2 * h + 1)}
                 act(M(nxl, slot[2 * h], slot[2 * h + 1] + 1, 0, MW, slot[2 * h + 1] - slot[2 * h]), A(E, 0, 2 * MW), 2 * MW, AF.Copy)
-
-                def send(qs=qs, slot=slot, nxl=nxl, sem="arr%d%d" % (t + 1, k)):
-                    trs = []
-                    for q in qs:
-                        rid, pid, _se = topo.addr(cores[q])
-                        trs.append(RemoteDMATransfer(dst_ids=[DstId(rid=rid, pnc=pid)], dma_engine_mask=sum(1 << e for e in lanes(topo, cores, rank, q)),
-                                                     remote_sem=T.sem[sem], src=T[nxl][:, slot[q], :], dst=T[nxl][:, 3 + rank, :]))
-                    g.remote_dma_fused(trs, local_sem=T.sem.sent)
-                    return None
-                net = (None, [("net%d" % t, k, k + 1)], [])
-                op("g", send, [M(nxl, slot[q], slot[q] + 1, 0, MW) for q in qs], [net], 300.0, sem="none")
-                op("r", None, [net], [M(nxl, 3 + q, 4 + q, 0, MW) for q in qs], 0.0,
-                   sem="arr%d%d" % (t + 1, k), inc=sum(len(lanes(topo, cores, q, rank)) for q in qs), lat=REM)
+                send(t, k, "arr%d%d" % (t + 1, k), [(q, M(nxl, slot[q], slot[q] + 1, 0, MW), M(nxl, 3 + rank, 4 + rank, 0, MW), M(nxl, 3 + q, 4 + q, 0, MW)) for q in qs], 0.0)
             sums(TH, "eqn", "AW", list(range(8 * h, 8 * h + 8)), k == 1)
             if not first:
                 mm(grp(rs, [(hs("key", h), A("I11"))], 128))
@@ -511,7 +583,10 @@ def build(g, core, T, topo, rank):
             mm(places("Fn", A("scn", 15, TH, 16)))
             tt(A("on32"), A("ps6", 256, 272), A("spn"), 16, ALU.min)
             ts(A("offn"), A("on32"), 16, C["h2"], ALU.add)
-            ts(IND(A("nxt"), A("offn")), A("ident", 0, TH), TH, 1.0, ALU.mult, float(ns), ALU.add)
+            if ENG["nxt"] == "a":
+                silu(IND(A("nxt"), A("offn")), A("ident", ns + OF, ns + OF + TH), TH, first and ENG["shpt"] != "a")
+            else:
+                cp(IND(A("nxt"), A("offn")), A("ident", ns + OF, ns + OF + TH), TH)
         mm(sum([grp(hs("ps6", h), [(hs("key", h), A("I11")), (P8("E8n", 0, 128), P8("Fn", 128 * h, 128 * h + 128))]
                     + ([] if first else [(A("RTb"), hs("B1", h))]), 128) for h in horder], []))
         act(A("ht", ns, ns + TH), A("ps6", 0, TH), TH, AF.Relu, bias=-2048.0)
@@ -644,7 +719,225 @@ def schedule(ops, deps):
         val = length(res[0])
         if val <= low:
             best, shift, low = res, new, val
-    return best
+    order = list(best[0])
+    names = sorted(set(o["e"] for o in ops))
+    eng = [names.index(o["e"]) for o in ops]
+    tail = [o["lat"] for o in ops]
+
+    def run(order, case):
+        dur, pre = case
+        start, why, free, prev, end, top = [0.0] * n, [-1] * n, [0.0] * len(names), [-1] * len(names), 0.0, 0
+        for i in order:
+            e = eng[i]
+            t, b = free[e], prev[e]
+            for j, gap in pre[i]:
+                if start[j] + gap >= t:
+                    t, b = start[j] + gap, j
+            start[i], why[i], prev[e] = t, b, i
+            t += dur[i]
+            free[e] = t
+            if t + tail[i] > end:
+                end, top = t + tail[i], i
+        swaps = []
+        while why[top] >= 0:
+            if why[top] not in deps[top]:
+                swaps.append((why[top], top))
+            top = why[top]
+        return end, swaps
+
+    def every(order):
+        res = [run(order, c) for c in cases]
+        return sum(r[0] for r in res) / len(res), [s for r in res for s in r[1]]
+    low, swaps = every(order)
+    cur, keep = low, order
+    for it in range(SWAPS):
+        j, i = swaps[int(rnd() * len(swaps))]
+        a, b = order.index(j), order.index(i)
+        for _ in range(int(3 * rnd() * rnd())):
+            c = a - 1
+            while c >= 0 and eng[order[c]] != eng[i]:
+                c -= 1
+            if c >= 0:
+                a = c
+        need, engs, up, ok = set(deps[i]), set(), [i], True
+        for k in reversed(order[a:b]):
+            if k in need or eng[k] in engs:
+                if eng[k] == eng[i]:
+                    ok = False
+                    break
+                up.append(k)
+                need.update(deps[k])
+                engs.add(eng[k])
+        if not ok:
+            continue
+        moved = set(up)
+        new = order[:a] + up[::-1] + [k for k in order[a:b] if k not in moved] + order[b + 1:]
+        val, sw = every(new)
+        if val <= cur + HEAT * (1.0 - it / SWAPS) * rnd():
+            order, cur, swaps = new, val, sw
+            if val < low:
+                low, keep = val, new
+    return keep, low
+
+
+def place(seq, pre, dur, eng, ne, first):
+    start = [0.0] * len(dur)
+    begs, ends = [[] for _ in range(ne)], [[] for _ in range(ne)]
+    for i in seq:
+        t = first[i]
+        for j, gap in pre[i]:
+            if start[j] + gap > t:
+                t = start[j] + gap
+        b, e, d = begs[eng[i]], ends[eng[i]], dur[i]
+        lo, hi = 0, len(b)
+        while lo < hi:
+            m = (lo + hi) // 2
+            if e[m] <= t:
+                lo = m + 1
+            else:
+                hi = m
+        while lo < len(b) and b[lo] < t + d:
+            t = e[lo]
+            lo += 1
+        b.insert(lo, t)
+        e.insert(lo, t + d)
+        start[i] = t
+    return start
+
+
+def arrange(ops, deps):
+    n = len(ops)
+    names = sorted(set(o["e"] for o in ops))
+    eng, ne = [names.index(o["e"]) for o in ops], len(names)
+    dur = [o["dur"] + 1.0 for o in ops]
+    tail, zero = [o["lat"] for o in ops], [0.0] * n
+    fpre, bpre = [[] for _ in range(n)], [[] for _ in range(n)]
+    for i in range(n):
+        for j, w in deps[i].items():
+            gap = ops[j]["lat"] + LAT if w else 0.0
+            fpre[i].append((j, gap + dur[j]))
+            bpre[j].append((i, gap + dur[i]))
+    cases = []
+    for lat, f, fx, rem in CASES:
+        d = [f * (o["dur"] + (fx - 1.0) * o["x"]) for o in ops]
+        cases.append((d, [[(j, d[j] + ((rem if ops[j]["e"][0] == "r" else ops[j]["lat"]) + lat if w else 0.0)) for j, w in deps[i].items()] for i in range(n)]))
+
+    def length(order):
+        tot = 0.0
+        for d, pre in cases:
+            start, free, end = [0.0] * n, [0.0] * ne, 0.0
+            for i in order:
+                t = free[eng[i]]
+                for j, gap in pre[i]:
+                    if start[j] + gap > t:
+                        t = start[j] + gap
+                start[i] = t
+                t += d[i]
+                free[eng[i]] = t
+                if t + tail[i] > end:
+                    end = t + tail[i]
+            tot += end
+        return tot / len(cases)
+    seed = [SEED]
+
+    def rnd():
+        seed[0] = (seed[0] * 1103515245 + 12345) % 2147483648
+        return seed[0] / 2147483648.0
+
+    def ranked(key, pre):
+        k = list(key)
+        for i in sorted(range(n), key=lambda x: top[x], reverse=pre is bpre):
+            for j, _gap in pre[i]:
+                if k[j] >= k[i]:
+                    k[i] = k[j] + 1e-3
+        return sorted(range(n), key=lambda x: k[x])
+    top, left, post = [0] * n, [len(p) for p in fpre], [[] for _ in range(n)]
+    for i in range(n):
+        for j, _gap in fpre[i]:
+            post[j].append(i)
+    todo = [i for i in range(n) if not left[i]]
+    for m, i in enumerate(todo):
+        top[i] = m
+        for k in post[i]:
+            left[k] -= 1
+            if not left[k]:
+                todo.append(k)
+    kinds = {}
+    kind = [kinds.setdefault((o["e"], o["w"][0][0] if o["e"][0] == "p" else o["w"][0][0].rstrip("0123456789"), o["w"][0][1] // 128), len(kinds)) for o in ops]
+    cut = [1e9]
+
+    def both(key):
+        back = place(ranked([-x for x in key], bpre), bpre, dur, eng, ne, tail)
+        late = [-(back[i] + dur[i]) for i in range(n)]
+        return late, place(ranked(late, fpre), fpre, dur, eng, ne, zero)
+    def held(order, case):
+        d, pre = case
+        start, why, free, prev, end, last = [0.0] * n, [-1] * n, [0.0] * ne, [-1] * ne, 0.0, 0
+        for i in order:
+            t, b = free[eng[i]], prev[eng[i]]
+            for j, gap in pre[i]:
+                if start[j] + gap >= t:
+                    t, b = start[j] + gap, j
+            start[i], why[i], prev[eng[i]] = t, b, i
+            t += d[i]
+            free[eng[i]] = t
+            if t + tail[i] > end:
+                end, last = t + tail[i], i
+        res = []
+        while why[last] >= 0:
+            if why[last] not in deps[last]:
+                res.append((why[last], last))
+            last = why[last]
+        return res
+    like = {}
+    for i, o in enumerate(ops):
+        like.setdefault(o["like"], []).append(i)
+    heads = [like[(("a", "X"), 1, 0)][0]] + like[(("a", "X"), 1, 1)]
+    start = place(todo, fpre, dur, eng, ne, zero)
+    best, low, cur, pairs = None, 0.0, 0.0, []
+    for it in range(ROUNDS):
+        way = rnd() if it > 8 else 1.0
+        if way < PAIR:
+            j, i = pairs[int(rnd() * len(pairs))]
+            key = list(start)
+            by = start[i] - start[j] + 1.0 + (500.0 * rnd() if rnd() < 0.3 else 0.0)
+            m, by = (i, -by) if rnd() < 0.5 else (j, by)
+            for x in (like[ops[m]["like"]] if rnd() < 0.6 else [m]):
+                key[x] += by
+            new = place(ranked(key, fpre), fpre, dur, eng, ne, zero)
+        else:
+            key = [start[i] + dur[i] for i in range(n)]
+            if way < MOVES[0]:
+                pick, by = int(rnd() * len(kinds)), NOISE * (2 * rnd() - 1)
+                key = [x + by if kind[i] == pick else x for i, x in enumerate(key)]
+            elif way < MOVES[1]:
+                a, b = 1 + int(2 * rnd()), 1 + int(3 * rnd())
+                by = key[heads[b]] - key[heads[a]]
+                for grp in like.values():
+                    src = [i for i in grp if ops[i]["t"] == a]
+                    for i in grp:
+                        if src and ops[i]["t"] == b:
+                            key[i] = key[src[0]] + by
+            elif way < MOVES[2]:
+                mid, amp = 20000.0 * rnd() - 5000.0, NOISE * rnd()
+                for grp in like.values():
+                    by = amp * rnd()
+                    for i in grp:
+                        if ops[i]["t"] > 0 and abs(key[i] - key[heads[ops[i]["t"]]] - mid) < WIDE:
+                            key[i] += by
+            elif it > 8:
+                mid, amp = rnd() * max(key), NOISE * rnd()
+                key = [x + amp * rnd() if abs(x - mid) < WIDE else x for x in key]
+            late, new = both(key)
+        order = sorted(range(n), key=lambda x: (new[x], top[x]))
+        val = length(order)
+        if best is None or val <= cur + HEAT * (1.0 - it / ROUNDS) * rnd():
+            start, cur = new, val
+            if PAIR:
+                pairs = held(order, cases[1]) + held(order, cases[int(rnd() * len(cases))])
+            if best is None or val < low:
+                best, low = order, val
+    return best, low
 
 
 ORDERS = {}
@@ -652,23 +945,11 @@ ORDERS = {}
 
 def orders(g, core, T, topo):
     if not ORDERS:
-        ops, deps, sends = [], [], {}
-        for rank in (0, 2):
-            part = build(g, core, T, topo, rank)[0]
-            base = len(ops)
-            deps += [{j + base: w for j, w in d.items()} for d in depend(part)]
-            ops += [dict(o, e=o["e"] + str(rank)) for o in part]
-        n = len(ops) // 2
-        for i, o in enumerate(ops):
-            if o["e"][0] == "r" and o["sem"][-1] == "0":
-                for j in list(deps[i]):
-                    if ops[j]["sem"] == "none":
-                        deps[i][(j + n) % (2 * n)] = True
-        res = schedule(ops, deps)
-        ORDERS["all"] = (ops, deps, res)
-        for own in range(2):
-            ORDERS[own] = [i - own * n for i in res[0] if i // n == own]
-    return ORDERS
+        parts = [build(g, core, T, topo, rank)[0] for rank in range(len(T.cores))]
+        ops = [dict(x[0], dur=max(o["dur"] for o in x)) for x in zip(*parts)]
+        deps = [{j: any(d.get(j, False) for d in x) for j in set().union(*x)} for x in zip(*[depend(p) for p in parts])]
+        ORDERS["all"] = (ops, deps, arrange(ops, deps))
+    return ORDERS["all"][2][0]
 
 
 def rank_program(g, core, T, topo):
@@ -677,7 +958,7 @@ def rank_program(g, core, T, topo):
         return
     ops, Q = build(g, core, T, topo, rank)
     deps = depend(ops)
-    order = orders(g, core, T, topo)[rank // 2]
+    order = orders(g, core, T, topo)
     count = {}
     mark = {}
     seen = {}
@@ -699,7 +980,7 @@ def rank_program(g, core, T, topo):
                 h.then_inc(T.sem[sem], o["inc"])
         count[sem] = count.get(sem, 0) + o["inc"]
         mark[i] = (sem, count[sem])
-    count["sent"] = (RO - 1) * sum(len(lanes(topo, T.cores, rank, q)) for q in range(4) if q != rank)
+    count["sent"] = 2 * (RO - 1) * sum(len(lanes(topo, T.cores, rank, q)) for q in range(4) if q != rank)
     for s, c in count.items():
         if s != "none":
             g.wait_ge(T.sem[s], c)

@@ -6,20 +6,23 @@ ALU = AluOpType
 AF = ActivationFunctionType
 
 V, NB, S0, TH, RO = 2048, 3072, 512, 256, 4
-ND = [[48, 48], [48, 48], [48, 48], [48, 48]]
-NM = [[8, 8], [8, 8], [8, 8], [8, 8]]
+ND = [[48, 40], [48, 40], [48, 40], [48, 40]]
+NM = [[10, 10], [10, 10], [10, 10], [10, 10]]
 MB = 64
 XC, XV = [64, 64], [64, 64]
-ENG = {"s": "a", "n": "a", "hn": "a", "nn": "a", "Y": "v", "shpt": "a", "nxt": "a"}
+ENG = {"s": "a", "n": "a", "hn": "a", "nn": "a", "Y": "aa", "shpt": "a", "nxt": "a", "d0": "a", "dl": "a",
+       "cl16": "vvv", "c16": "av", "vdr": "av", "sl16": "vv", "off": "av", "xl": "vv"}
 OF = 64
 DB, CB = ["ps0", "ps1"], ["ps4", "ps5"]
-TURN = True
-SHORT, EXACT, SEEN, ZB = [False, True], [False, True], True, "ps7"
+TURN, TTK, GROW = True, 0.85, True
+SHORT, EXACT, SEEN, ZB = [True, True], [True, True], True, "ps7"
+FLAGS, AB = ["tnsf", "stfn"], [None, None]
 PT, PS = 4, 2
-GC, SC, LAT, PEC, CYC, REM, KB, DM0 = 1.56, 3.8, 260.0, 0.45, 0.9, 1800.0, 4.0, 1200.0
+GC, SC, LAT, PEC, CYC, REM, KB, DM0 = 1.56, 3.8, 260.0, 0.46, 0.9, 1800.0, 4.0, 1100.0
 FIRST, PAIR, MOVES, WIDE = 1500.0, 0.0, [0.3, 0.35, 0.7], 4000.0
-ROUNDS, NOISE, AHEAD, SWAPS, HEAT, SEED = 3000, 1300.0, 0.5, 5000, 300.0, 3
-CASES = [(130.0, 0.95, 0.9, 1300.0), (200.0, 0.92, 1.0, 1500.0), (300.0, 1.0, 1.0, 2400.0), (200.0, 1.35, 1.25, 1800.0)]
+ROUNDS, NOISE, AHEAD, SWAPS, HEAT, SEED = 3500, 1300.0, 0.5, 0, 300.0, 2
+OA, SOON, WARM, TRY, TRIES = 0.0, 0.0, 100.0, 400, 0
+CASES = [(200.0, 0.92, 1.0, 1500.0, 1.0, 1.0), (120.0, 1.05, 0.8, 1300.0, 1.0, 0.8), (300.0, 1.0, 1.0, 2500.0, 1.0, 1.0), (200.0, 1.3, 1.25, 1800.0, 1.0, 1.0)]
 MW = 136
 MAG = 12582912.0
 BIG = 2.0 ** 93
@@ -35,7 +38,9 @@ def _sb(names, cols, dt):
         SCRATCH[n] = ("sbuf", [128] + (list(cols) if isinstance(cols, (list, tuple)) else [cols]), dt)
 
 
-_sb("rect shpi", V, I32)
+_sb("shpi", V, I32)
+_sb("rect", V + TH, I32)
+_sb("nbr", 128 * RO, BF)
 _sb("shph", V, F16)
 _sb("recf shpt", V + TH, F32)
 _sb("boxt X", 4096, BF)
@@ -46,7 +51,7 @@ _sb("nxt", 1536 + TH, F32)
 _sb("ident", V, F32)
 _sb("obi pci", 16, I32)
 _sb("tvb", [4, 64], BF)
-_sb("drb", 8, BF)
+_sb("drb ndr", 8, BF)
 _sb("land1 land2 land3", [8, MW], F16)
 _sb("ol16 sl16 nl16 xl16 offo offn", 16, U16)
 _sb("cl16", TH, U16)
@@ -61,12 +66,12 @@ _sb("kf", 8, F32)
 _sb("s16 n16 nn16 orow Y16 m16 hn hr B1 hold scs scn key", TH, F16)
 _sb("sel", 512, F16)
 _sb("Kt", RO * TH, F16)
-_sb("rot Sg OHT nhm OHs OHf Fo Fn yvb ones irow Kc Vm", TH, BF)
+_sb("rot Sg OHT nhm OHs OHf Fo Fn ones irow Kc Vm yvb", TH, BF)
 _sb("W1 Ws d0f d0r dl fs Z n32", TH, F32)
 _sb("eqo eqn", 2560, BF)
 _sb("col", 64, F32)
-_sb("rowg rowr tm RTI wx", 128, F32)
-_sb("Ib nIb I11 I12 nI12 I13 I23 nI11 BO nBO E8 E8n nRm RTb R12 Dc WG AW", 128, BF)
+_sb("rowg rowr tm wy wx", 128, F32)
+_sb("Ib nIb I11 I12 I13 I23 BO nBO E8 E8n nRm RTb R12 Dc WG AW", 128, BF)
 _sb("Hw", 128, F16)
 _sb("Mall M8", 144, BF)
 _sb("K8", 64, BF)
@@ -143,7 +148,7 @@ def build(g, core, T, topo, rank):
             return (50.0 if eng == "v" else 65.0) + n * GC * CYC
         if k is None:
             k = 0.5 if (eng == "v" and two(out) and all(two(x) for x in ins)) else 1.0
-        return max(64.0, n * k) * CYC
+        return max(64.0, n * k) * CYC + (OA if eng == "a" else 0.0)
 
     def cp(out, in_, n):
         op("v", lambda: g.vector.tensor_copy(out[0], in_[0]), [in_], [out], cost("v", n, out, [in_]))
@@ -157,7 +162,7 @@ def build(g, core, T, topo, rank):
 
     def tt(out, a, b, n, o):
         ps = a[1][0][0].startswith("ps") or b[1][0][0].startswith("ps")
-        op("v", lambda: g.vector.tensor_tensor(out[0], a[0], b[0], o), [a, b], [out], cost("v", n, out, [a, b], 1.0 if ps else 2.0))
+        op("v", lambda: g.vector.tensor_tensor(out[0], a[0], b[0], o), [a, b], [out], cost("v", n, out, [a, b], TTK if out[1][0][0] == "Dab" else 1.0 if ps or (two(out) and two(a) and two(b)) else 2.0))
 
     def scan(out, d0, d1, n, o0=ALU.add, o1=ALU.min):
         op("v", lambda: g.vector.tensor_tensor_scan(out[0], d0[0], d1[0], 0.0, o0, o1), [d0, d1], [out], cost("v", n, out, [d0, d1]))
@@ -178,6 +183,12 @@ def build(g, core, T, topo, rank):
             cp(out, in_, n)
         else:
             ts(out, in_, n, add, ALU.add)
+
+    def line(eng, out, in_, n, scale, bias):
+        if eng == "a":
+            act(out, in_, n, AF.Identity, bias=bias, scale=scale)
+        else:
+            ts(out, in_, n, scale, ALU.mult, bias, ALU.add)
 
     def iota(out, pat, base, cm, n):
         if dtype(out) == I32:
@@ -207,8 +218,8 @@ def build(g, core, T, topo, rank):
     def H(t):
         return (t, [("hbm", 0, 0)], [])
 
-    for eng, sem, dst, src, kb in (("s", "d_ob", A("obi"), T.ob[:], 8), ("a", "d_shp", P8("shpi", 0, V), T.shp[:], 128), ("s", "d_rec", A("rect"), T.rec[:], 1100),
-                                   ("a", "d_tv", A("tvb"), T.tv[:], 64), ("a", "d_dr", A("drb", 0, 4), T.dr[:], 1),
+    for eng, sem, dst, src, kb in (("s", "d_ob", A("obi"), T.ob[:], 8), ("a", "d_shp", P8("shpi", 0, V), T.shp[:], 128), ("s", "d_dr", A("drb", 0, 4), T.dr[:], 130),
+                                   ("a", "d_tv", A("tvb"), T.tv[:], 190), ("s", "d_rec", A("rect", 0, V), T.rec[:], 1150),
                                    ("s", "d_box", A("boxt", 0, NB), T.box[:], 1900), ("s", "d_bnd", A("bnd"), T.bound[:], 2150)):
         dma(eng, sem, dst, H(src), kb)
         ops[-1]["w"].append(("turn" + eng, 0, 1))
@@ -241,9 +252,12 @@ def build(g, core, T, topo, rank):
     ts(C["hc"], C["hk"], 1, -float(OF), ALU.add)
     ts(C["h2"], C["hc"], 1, 2048.0, ALU.add)
     ts(C["wb"], C["rc"], 1, -LR, ALU.mult, L0, ALU.add)
+    iota(A("wy"), [[16, 16], [0, 8]], 0, 0, 128)
+    act(A("wy"), A("wy"), 128, AF.Exp, bias=C["wb"], scale=-LR, extra=1300.0)
+    ops[-1]["w"].append(("turnf", 0, 1))
+    ts(A("ndr", 0, RO), A("drb", 0, RO), RO, -1.0, ALU.mult)
     ts(A("Ib"), rowm, 128, C["pc"], ALU.is_equal)
-    for n, s in (("nIb", -1.0), ("I11", 2048.0), ("I12", 4096.0), ("nI12", -4096.0), ("I13", 8192.0), ("I23", 2.0 ** 23),
-                 ("nI11", -2048.0), ("Dc", C["dc"])):
+    for n, s in [("nIb", -1.0), ("I11", 2048.0), ("I12", 4096.0), ("I23", -2.0 ** 23), ("Dc", C["dc"])] + ([] if all(SHORT) else [("I13", 8192.0)]):
         act(A(n), A("Ib"), 128, AF.Identity, scale=s)
     ts(A("Hw"), A("Ib"), 128, 0.5 - 2.0 ** -11, ALU.mult)
     ts(A("Mall"), rowx, 144, C["gm"], ALU.is_equal)
@@ -255,8 +269,9 @@ def build(g, core, T, topo, rank):
     for k in range(4):
         lo, hi = 512 * k, 512 * k + 512
         cp(P8("shph", lo, hi), P8("shpi", lo, hi), 512)
-        mm([(A("ps%d" % k), P8("E8", 0, 128), P8("shph", lo, hi), 512, True, True)])
-        act(A("shpt", lo, hi), A("ps%d" % k), 512, AF.Identity, bias=float(OF))
+        mm([(A("ps%d" % (k + 2)), P8("E8", 0, 128), P8("shph", lo, hi), 512, True, True)])
+        act(A("shpt", lo, hi), A("ps%d" % (k + 2)), 512, AF.Silu, bias=float(OF), extra=0.0 if k else 1500.0)
+        ops[-1]["w"].append(("turnf", 0, 1))
     tt(A("rowr"), rowm, A("rowg"), 128, ALU.subtract)
     for n, s in (("GG", 1.0), ("GG2", 2.0), ("nGG", -1.0)):
         ts(A(n, 0, 8), row8, 8, C["gc"], ALU.is_equal, s / 2048, ALU.mult)
@@ -280,7 +295,8 @@ def build(g, core, T, topo, rank):
     tt(A("nRm"), A("Ib"), A("nRm"), 128, ALU.subtract)
     ts(A("RTb"), rowm, 128, C["pvc"], ALU.is_equal)
     tt(A("RTb"), A("RTb"), A("Ib"), 128, ALU.subtract)
-    act(A("RTI"), A("RTb"), 128, AF.Copy)
+    if not all(SHORT):
+        act(A("RTI"), A("RTb"), 128, AF.Copy)
     act(A("R12"), A("RTb"), 128, AF.Identity, scale=4096.0)
     iota(A("kf"), [[128, 8]], NB - 2048, 1, 8)
     for j in range(2 * RO):
@@ -291,16 +307,13 @@ def build(g, core, T, topo, rank):
     ts(A("m16", 0, 128), A("rowr"), 128, C["r1"], ALU.is_equal, -2048.0, ALU.mult)
     ts(A("il"), A("ident", 0, TH, 16), 16, C["rc"], ALU.add)
     ts(A("spn"), A("il"), 16, C["h2"], ALU.subtract, 1536.0, ALU.add)
-    for k in range(RO):
-        act(A("kc", 16 * k, 16 * k + 16), A("il"), 16, AF.Identity, bias=float(NB - 2048 + TH * k))
-    act(A("ones"), A("ident", 0, TH), TH, AF.Identity, bias=1.0, scale=0.0)
-    act(A("Kc", 0, 128), rowm, 128, AF.Identity, bias=-1.0 / 128, scale=0.0)
-    act(A("Kc", 128, 256), rowm, 128, AF.Identity, scale=0.0)
+    for k in range(RO - 1):
+        if not all(EXACT):
+            act(A("kc", 16 * k, 16 * k + 16), A("il"), 16, AF.Identity, bias=float(NB - 2048 + TH * k))
+    act(A("ones", 0, 128), rowm, 128, AF.Identity, bias=1.0, scale=0.0)
     act(A("irow"), A("ident", 0, TH), TH, AF.Copy)
     ts(A("AW"), A("wx"), 128, C["gc"], ALU.is_equal)
-    iota(A("wx"), [[16, 16], [0, 8]], 0, 0, 128)
-    act(A("wx"), A("wx"), 128, AF.Exp, bias=C["wb"], scale=-LR, extra=1300.0)
-    tt(A("WG"), A("wx"), A("AW"), 128, ALU.mult)
+    tt(A("WG"), A("wy"), A("AW"), 128, ALU.mult)
     for h in range(2):
         tt(A("hold", 128 * h, 128 * h + 128), A("Y16", 0, 128), A("m16", 0, 128), 128, ALU.add)
     act(A("d0f"), A("ident", 0, TH), TH, AF.Identity, bias=-U, scale=0.0)
@@ -308,8 +321,7 @@ def build(g, core, T, topo, rank):
     act(A("d0r"), A("ident", 0, TH), TH, AF.Identity, bias=U, scale=0.0)
     act(A("d0r", 15, TH, 16), A("il"), 16, AF.Identity, bias=1.0e6, scale=0.0)
     conv(A("ht", 0, S0), A("bnd"), S0)
-    for k in range(4):
-        conv(A("recf", 512 * k, 512 * k + 512), A("rect", 512 * k, 512 * k + 512), 512)
+    iota(A("nbr"), [[TH, RO], [0, 128]], NB, 0, 128 * RO)
 
     def pairs(buf, row, keys, cs, blocks, less=None):
         for c in cs:
@@ -322,12 +334,12 @@ def build(g, core, T, topo, rank):
 
     eoff = [sum(256 - 64 * (k // 4) for k in range(c)) for c in range(17)]
 
-    def sums(lo, buf, wts, cs, last):
+    def sums(lo, buf, wts, cs, last, start=False):
         for c0 in range(0, len(cs), PS):
             lst = []
             for c in cs[c0:c0 + PS]:
                 w = A(wts, 8 * c, 8 * c + 8)
-                lst.append((P8("ps6", lo + 16 * c, lo + TH), w, A(buf, eoff[c] + 16 * c % 64, eoff[c + 1]), TH - 16 * c, False, False))
+                lst.append((P8("ps6", lo + 16 * c, lo + TH), w, A(buf, eoff[c] + 16 * c % 64, eoff[c + 1]), TH - 16 * c, start and c == 0, False))
                 lst.append((P8("ps6", lo + 16 * c, lo + 16 * c + 16), w, A("Dg"), 16, False, last and c == cs[-1]))
             mm(lst)
 
@@ -368,32 +380,36 @@ def build(g, core, T, topo, rank):
         vv = lambda q0, q1: M("tvb", q0, q1, 0, 64) if first else M(land, 3 + q0, 3 + q1, vo, vo + 64)
         cc = lambda h: M("cpb", 4 * h + 1, 4 * h + 3, 0, 64)
         pp = lambda h: M("cpb", 4 * h, 4 * h + 4, 0, 64, 3)
+        for k in range(8 if last else 0):
+            conv(A("recf", TH * k, TH * k + TH), A("rect", TH * k, TH * k + TH), TH)
         if first:
             cp(A("ol16"), A("obi"), 16)
             cp(A("olh"), A("obi"), 16)
             cp(A("ol32"), A("obi"), 16)
             cp(A("orow"), IND(A("ident"), A("ol16")), TH)
-        for h in horder:
+        for k, h in enumerate(horder):
             h8 = lambda n: hs(n, h, 8)
             if first:
-                ts(hs("c32", h), IND(A("rect"), h8("ol16")), 128, 4095, ALU.bitwise_and)
+                ts(hs("c32", h), IND(A("rect", 0, V), h8("ol16")), 128, 4095, ALU.bitwise_and)
                 cp(hs("cl16", h), hs("c32", h), 128)
-                ts(hs("p32", h), IND(A("rect"), h8("ol16")), 128, 12, ALU.arith_shift_right)
+                ts(hs("p32", h), IND(A("rect", 0, V), h8("ol16")), 128, 12, ALU.arith_shift_right)
             else:
                 conv(h8("ol32"), M(land, 3 + 2 * h, 5 + 2 * h, po, po + 4), 8)
-                for lo, n, ol in pieces(t, h):
-                    cp(A("Wi", lo, lo + n), IND(A("recf", 0, V), ol), n)
-                    ts(A("c32", lo, lo + n), A("Wi", lo, lo + n), n, 4095, ALU.bitwise_and)
-                    cp(A("cl16", lo, lo + n), A("c32", lo, lo + n), n)
-                ts(hs("p32", h), hs("Wi", h), 128, 12, ALU.arith_shift_right)
-            ts(cc(h), hs("cl16", h), 128, -2048.0, ALU.add)
+                for j, (lo, n, ol) in enumerate(pieces(t, h)):
+                    ts(A("c32", lo, lo + n), IND(A("rect", 0, V), ol), n, 4095, ALU.bitwise_and)
+                    plus(ENG["cl16"][k + j], A("cl16", lo, lo + n), A("c32", lo, lo + n), n)
+                    ts(A("p32", lo, lo + n), IND(A("rect", 0, V), ol), n, 12, ALU.arith_shift_right)
+            if ENG["c16"][k] == "a":
+                plus("a", cc(h), hs("c32", h), 128, -2048.0)
+            else:
+                ts(cc(h), hs("cl16", h), 128, -2048.0, ALU.add)
             conv(pp(h), hs("p32", h), 128)
-            ts(A("boxt", nb + 128 * h, nb + 128 * h + 128), vv(2 * h, 2 * h + 2), 128, drc, ALU.subtract)
+            plus(ENG["vdr"][k], A("boxt", nb + 128 * h, nb + 128 * h + 128), vv(2 * h, 2 * h + 2), 128, A("ndr", t, t + 1))
             if not first:
                 for lo, n, ol in pieces(t, h):
                     plus(ENG["s"], A("s16", lo, lo + n), IND(A("shpt", 0, V), ol), n)
                 scan(hs("scs", h), hs("hold", h), hs("s16", h), 128)
-                ts(h8("sl16"), A("scs", 128 * h + 15, 128 * h + 128, 16), 8, C["hc"], ALU.add)
+                plus(ENG["sl16"][k], h8("sl16"), A("scs", 128 * h + 15, 128 * h + 128, 16), 8, C["hc"])
                 plus(ENG["n"], hs("n16", h), IND(A("nxt", 0, 1536), h8("sl16")), 128)
             else:
                 plus(ENG["n"], hs("n16", h), IND(A("shpt", 0, V), h8("ol16")), 128)
@@ -406,19 +422,17 @@ def build(g, core, T, topo, rank):
             S7 = lambda k: A("ps7", 128 * k, 128 * k + 128)
             short = SHORT[horder.index(h)]
             if not first:
-                plus(ENG["nn"], hs("nn16", h), IND(A("nxt", 0, 1536), h8("nl16")), 128)
-                zz = lambda out, lo, n: grp(out, [(A("I12"), A("n16", lo, lo + n)), (A("nI12"), A("s16", lo, lo + n)), (A("nI11"), A("ones", 0, n))], n)
-                E = "ps%d" % (2 + h)
-                z = A(E, 320, 448)
-                mm(zz(z, 128 * h, 128) + (zz(A(E, 256, 320), 128 * h, 64) + zz(A(E, 448, 512), 128 * h + 64, 64) if short else []))
-                act(hs("rot", h), z, 128, AF.Sign, bias=2048.0)
+                if h == own:
+                    plus(ENG["nn"], A("nn16"), IND(A("nxt", 0, 1536), A("nl16")), TH)
+                tt(hs("rot", h), hs("n16", h), hs("s16", h), 128, ALU.not_equal)
+                tt(hs("hr", h), hs("hn", h), hs("rot", h), 128, ALU.mult)
                 if short:
-                    tt(M("cp1", 4 * h, 4 * h + 4, 0, 64), M("cpb", 4 * h, 4 * h + 4, 0, 64), A(E, 256, 512), 256, ALU.min)
-                tt(hs("hr", h), hs("hn", h), z, 128, ALU.min)
+                    tt(M("cp1", 4 * h, 4 * h + 4, 0, 64, 3), pp(h), hs("rot", h), 128, ALU.mult)
+                    tt(M("cp1", 4 * h + 1, 4 * h + 3, 0, 64), cc(h), hs("rot", h), 128, ALU.mult)
                 mm(grp(S7(0), [(hs("rot", h), A("Dc"))], 128))
-                act(A("d0f", 128 * h + 1, 128 * h + 128, 16), A("ps7", 1, 128, 16), 8, AF.Identity, bias=-U, scale=16 * U)
-                act(A("d0r", 128 * h, 128 * h + 128, 16), A("ps7", 1, 128, 16), 8, AF.Identity, bias=U, scale=-16 * U)
-                act(hs("dl", h), S7(0), 128, AF.Identity, bias=-1.0, scale=U)
+                line(ENG["d0"], A("d0f", 128 * h + 1, 128 * h + 128, 16), A("ps7", 1, 128, 16), 8, 16 * U, -U)
+                line(ENG["d0"], A("d0r", 128 * h, 128 * h + 128, 16), A("ps7", 1, 128, 16), 8, -16 * U, U)
+                line(ENG["dl"], hs("dl", h), S7(0), 128, U, -1.0)
         long = [h for h in horder if not (first or SHORT[horder.index(h)])]
         for h in long:
             mm(grp(S7(1), [(A("I23"), hs("rot", h)), (A("I12"), pp(h)), (A("Ib"), cc(h))], 128))
@@ -426,20 +440,21 @@ def build(g, core, T, topo, rank):
         turned = lambda h: [(A("R12"), M("cp1", 4 * h, 4 * h + 4, 0, 64, 3)), (A("RTb"), M("cp1", 4 * h + 1, 4 * h + 3, 0, 64))]
         mm(sum([grp(S7(2 + h), [(A("I12"), pp(h)), (A("Ib"), cc(h))] + ([] if first else [(A("RTI"), hs("W1", h))] if h in long else turned(h)), 128) for h in horder], []))
         act(A("Ws"), A("ps7", 256, 512), TH, AF.Identity, bias=2048.0)
-        chunks = list(range(8, 16)) + list(range(8))
-        if first:
+        chunks = list(range(16))
+        if first or GROW:
+            for h in ([] if first else horder):
+                conv(hs("orow", h), M(land, 3 + 2 * h, 5 + 2 * h, oo, oo + 64), 128)
             pairs("eqo", lambda lo: A("orow", lo, TH), "ol32", chunks, False)
         else:
             pairs("eqo", lambda lo: M(land, 3 + lo // 64, 7, oo, oo + 64), "ol32", chunks, True)
-        mm([(P8("ps6", 0, TH), A("Z8"), A("irow"), TH, True, False)])
-        sums(0, "eqo", "WG", chunks, True)
+        sums(0, "eqo", "WG", chunks, True, True)
         act(P8("Fo", 0, TH), P8("ps6", 0, TH), TH, AF.Sign)
         mm(places("Fo", A("olh") if first else M(land, 3, 7, po, po + 4)))
         tt(A("of32"), A("ps6", 256, 272), A("il"), 16, ALU.min)
-        ts(A("offo"), A("of32"), 16, 2048.0, ALU.add)
+        plus(ENG["off"][0], A("offo"), A("of32"), 16, 2048.0)
         if not last:
             if ENG["shpt"] == "a":
-                silu(IND(A("shpt"), A("offo")), A("n32"), TH, first)
+                silu(IND(A("shpt"), A("offo")), A("n32"), TH, False)
             else:
                 cp(IND(A("shpt"), A("offo")), A("n16"), TH)
         pairs("eqn", lambda lo: A("n16", lo, TH), "nl32", chunks, False, C["hk"])
@@ -468,8 +483,6 @@ def build(g, core, T, topo, rank):
             else:
                 terms = [(hs("ones", 0), A("Kc"))]
             mm(grp(A(E, 0, 256), terms, 256, stop=False))
-            if nm:
-                mm([(A(cb, 0, 128), A("Ib"), vv(2 * h, 2 * h + 2), 128, True, True)])
             eo = lambda a: A(E, a, 256, 16)
             aa = list(range(nm, 16))
             tiles = [(b ^ flip, aa[j:j + 8]) for b in range(2) for j in range(0, len(aa), 8)]
@@ -487,7 +500,7 @@ def build(g, core, T, topo, rank):
             for lo in list(range(0, 128, MB))[::-1 if flip else 1]:
                 x0 = 2048 * h + 16 * lo
                 for a in range(nm):
-                    tt(DA(h, a, a + 1, lo, lo + MB), A("X", x0 + a, x0 + 16 * MB, 16), A(cb, lo, lo + MB), MB, ALU.max)
+                    tt(DA(h, a, a + 1, lo, lo + MB), A("X", x0 + a, x0 + 16 * MB, 16), vv(2 * h + lo // 64, 2 * h + (lo + MB) // 64), MB, ALU.max)
             he = A(E, 128, 256)
             mm([(he, hs("hn", h), A("nIb"), 128, False, False)] + ([] if first else [(he, hs("hr", h), A("nRm"), 128, False, False)]))
             for j in range(0, nm, 4):
@@ -500,46 +513,47 @@ def build(g, core, T, topo, rank):
             scan(AR(E, 384, 512), AR("d0r", 128 * h, 128 * h + 128), AR("fs", 128 * h, 128 * h + 128), 128)
             rs = A(E, 384, 512)
             short = SHORT[k] or first
-            exact = short and (first or last or EXACT[k])
-            seen = lambda: tt(hs("OHs", h), rs, hs("dl", h), 128, ALU.is_equal)
-            if short and not first and (SEEN or last):
-                seen()
-            if not (last and exact):
-                tt(hs("OHT", h), rs, hs("key", h), 128, ALU.is_equal)
-            fits = hs("OHs" if first else "OHf", h)
-            if exact:
-                ts(fits, rs, 128, -1.0, ALU.is_equal)
-            tt(hs("nhm", h), rs, A("tm"), 128, ALU.is_ge)
-            if not first and not (short and (SEEN or last)):
-                seen()
+            exact = last or EXACT[k]
+            fits = hs("OHf", h)
+            flags = {"s": lambda: ts(hs("OHs", h), rs, 128, -1.0, ALU.not_equal) if first else tt(hs("OHs", h), rs, hs("dl", h), 128, ALU.not_equal),
+                     "t": lambda: None if last and exact else tt(hs("OHT", h), rs, hs("key", h), 128, ALU.is_equal),
+                     "f": lambda: ts(fits, rs, 128, -1.0, ALU.is_equal) if exact else None,
+                     "n": lambda: tt(hs("nhm", h), rs, A("tm"), 128, ALU.is_ge)}
+            for x in ("stfn" if last else FLAGS[k]):
+                flags[x]()
             sl = 256 * h
             q0, q1 = (1, 3) if last else (0, 4)
 
             def change():
-                if short:
-                    terms = [(A("I12"), pp(h)), (A("Ib"), hs("irow", h))] + ([] if first else [(A("R12"), M("cp1", 4 * h, 4 * h + 4, 0, 64, 3))]) + [(hs("OHs", h), A("I23"))]
-                    mm(grp(A(cb, 384, 512), terms, 128))
-                    act(hs("Z", h), A(cb, 384, 512), 128, AF.Identity, bias=float(nb) - 2.0 ** 23)
+                terms = [(A("I12"), pp(h)), (A("Ib"), hs("irow", h))] + ([] if first else [(A("R12"), M("cp1", 4 * h, 4 * h + 4, 0, 64, 3))])
+                terms += ([] if last else [(A("Ib"), A("nbr", 128 * t, 128 * t + 128))]) + [(hs("OHs", h), A("I23"))]
+                mm(grp(A(cb, 384, 512), terms, 128))
+                if last:
+                    act(hs("Z", h), A(cb, 384, 512), 128, AF.Identity, bias=float(nb))
+                    tt(IND(A("recf"), h8("offo")), hs("Ws", h), hs("Z", h), 128, ALU.max)
                 else:
-                    mm(grp(A(cb, 384, 512), [(A("Ib"), hs("irow", h)), (A("nBO"), A("sel", sl + 64, sl + 192)), (hs("OHs", h), A("I13"))], 128))
-                    act(hs("Z", h), A(cb, 384, 512), 128, AF.Relu, bias=float(nb - 2048 - 8192))
-                tt(IND(A("recf"), h8("offo")), hs("Ws", h), hs("Z", h), 128, ALU.max if short else ALU.add)
+                    tt(hs("Wi", h), A(cb, 384, 512), hs("Ws", h), 128, ALU.max)
+                    cp(IND(A("rect"), h8("offo")), hs("Wi", h), 128)
             cb, ob = (ZB if short and ZB else CB[k]), CB[k]
             if short and (SEEN or last):
                 change()
             cb = ob
+            ab = AB[k] or cb
+            ask = [(A(ab, 256, 320), hs("nhm", h), A("K8"), 64, True, True)]
             mm([(A(cb, 64 * q, 64 * q + 64), fits if exact and q in (1, 2) else hs("OHT", h), A("Ib", 64 * (q // 2), 64 * (q // 2) + 64), 64, True, True) for q in range(q0, q1)]
-               + [(A(cb, 256, 320), hs("nhm", h), A("K8"), 64, True, True)])
+               + ([] if AB[k] else ask))
             tt(A("sel", sl + 64 * q0, sl + 64 * q1), A(cb, 64 * q0, 64 * q1), M("cpb", 4 * h + q0, 4 * h + q1, 0, 64), 64 * (q1 - q0), ALU.mult)
-            tt(hs("AW", h, 64), A(cb, 256, 320), hs("WG", h, 64), 64, ALU.mult)
+            if AB[k]:
+                mm(ask)
+            tt(hs("AW", h, 64), A(ab, 256, 320), hs("WG", h, 64), 64, ALU.mult)
             lists = A(E, 128 + 4 * q0, 128 + 4 * q1)
             mm([(lists, A("Mall", 15 - r, 143 - r), A("sel", sl + 64 * q0 + r, sl + 64 * q1, 16), 64, r == 0, False) for r in range(16)]
                + [(A(E, 132, 140), hs("nhm", h), A("KF", 16 * t + 8 * h, 16 * t + 8 * h + 8) if exact else A("G13"), 64, False, True)])
             if exact:
-                ts(h8("xl16"), A(E, 132, 140), 8, 2048.0, ALU.add)
+                plus(ENG["xl"][k], h8("xl16"), A(E, 132, 140), 8, 2048.0)
             if not last:
                 nol, qs = "ol%d" % (t + 1), [q for q in (2 * h, 2 * h + 1) if q != rank]
-                cp(A(nol, 16 * k, 16 * k + 16), A(E, 128, 144), 16)
+                plus(ENG["xl"][k], A(nol, 16 * k, 16 * k + 16), A(E, 128, 144), 16)
                 at = lambda q: A(nol, 40 if k else 32 + 4 * (q % 2), 44 if k else 36 + 4 * (q % 2))
                 send(t, k, "lst%d%d" % (t + 1, k), [(q, A(nol, 16 * k + 12 * (q % 2), 16 * k + 12 * (q % 2) + 4), at(rank), at(q)) for q in qs],
                      FIRST if first and k == 0 else 0.0)
@@ -548,7 +562,7 @@ def build(g, core, T, topo, rank):
                 ts(h8("xl16"), h8("xm"), 8, 2048.0, ALU.add)
             if not (short and (SEEN or last)):
                 change()
-            plus(ENG["Y"], hs("Y16", h), IND(A("boxt", 0, nb + TH), h8("xl16")), 128, drc)
+            plus(ENG["Y"][k], hs("Y16", h), IND(A("boxt", 0, nb + TH), h8("xl16")), 128, drc)
             if not last:
                 nbx = A("boxt", nb + 128 * h, nb + 128 * h + 128)
                 mm(grp(A(cb, 256, 384), [(A("Hw"), hs("Y16", h)), (A("Hw"), nbx)], 128))
@@ -582,9 +596,9 @@ def build(g, core, T, topo, rank):
         if not last:
             mm(places("Fn", A("scn", 15, TH, 16)))
             tt(A("on32"), A("ps6", 256, 272), A("spn"), 16, ALU.min)
-            ts(A("offn"), A("on32"), 16, C["h2"], ALU.add)
+            plus(ENG["off"][1], A("offn"), A("on32"), 16, C["h2"])
             if ENG["nxt"] == "a":
-                silu(IND(A("nxt"), A("offn")), A("ident", ns + OF, ns + OF + TH), TH, first and ENG["shpt"] != "a")
+                silu(IND(A("nxt"), A("offn")), A("ident", ns + OF, ns + OF + TH), TH, False)
             else:
                 cp(IND(A("nxt"), A("offn")), A("ident", ns + OF, ns + OF + TH), TH)
         mm(sum([grp(hs("ps6", h), [(hs("key", h), A("I11")), (P8("E8n", 0, 128), P8("Fn", 128 * h, 128 * h + 128))]
@@ -786,17 +800,14 @@ def place(seq, pre, dur, eng, ne, first):
     for i in seq:
         t = first[i]
         for j, gap in pre[i]:
-            if start[j] + gap > t:
-                t = start[j] + gap
+            gap += start[j]
+            if gap > t:
+                t = gap
         b, e, d = begs[eng[i]], ends[eng[i]], dur[i]
-        lo, hi = 0, len(b)
-        while lo < hi:
-            m = (lo + hi) // 2
-            if e[m] <= t:
-                lo = m + 1
-            else:
-                hi = m
-        while lo < len(b) and b[lo] < t + d:
+        lo = hi = len(b)
+        while lo and e[lo - 1] > t:
+            lo -= 1
+        while lo < hi and b[lo] < t + d:
             t = e[lo]
             lo += 1
         b.insert(lo, t)
@@ -818,26 +829,26 @@ def arrange(ops, deps):
             fpre[i].append((j, gap + dur[j]))
             bpre[j].append((i, gap + dur[i]))
     cases = []
-    for lat, f, fx, rem in CASES:
-        d = [f * (o["dur"] + (fx - 1.0) * o["x"]) for o in ops]
-        cases.append((d, [[(j, d[j] + ((rem if ops[j]["e"][0] == "r" else ops[j]["lat"]) + lat if w else 0.0)) for j, w in deps[i].items()] for i in range(n)]))
+    for lat, f, fx, rem, fp, fd in CASES:
+        d = [f * (o["dur"] * (fp if o["e"] == "p" else 1.0) + (fx - 1.0) * o["x"]) for o in ops]
+        cases.append((d, [[(j, d[j] + ((rem if ops[j]["e"][0] == "r" else fd * ops[j]["lat"]) + lat if w else 0.0)) for j, w in deps[i].items()] for i in range(n)]))
 
-    def length(order):
+    def length(order, some):
         tot = 0.0
-        for d, pre in cases:
-            start, free, end = [0.0] * n, [0.0] * ne, 0.0
+        for d, pre in some:
+            start, free = [0.0] * n, [0.0] * ne
             for i in order:
-                t = free[eng[i]]
+                e = eng[i]
+                t = free[e]
                 for j, gap in pre[i]:
-                    if start[j] + gap > t:
-                        t = start[j] + gap
+                    gap += start[j]
+                    if gap > t:
+                        t = gap
                 start[i] = t
-                t += d[i]
-                free[eng[i]] = t
-                if t + tail[i] > end:
-                    end = t + tail[i]
-            tot += end
-        return tot / len(cases)
+                free[e] = t + d[i]
+            tot += max(start[i] + d[i] + tail[i] for i in ends)
+        return tot
+    ends = [i for i in range(n) if not bpre[i]]
     seed = [SEED]
 
     def rnd():
@@ -846,11 +857,13 @@ def arrange(ops, deps):
 
     def ranked(key, pre):
         k = list(key)
-        for i in sorted(range(n), key=lambda x: top[x], reverse=pre is bpre):
+        for i in (todo[::-1] if pre is bpre else todo):
+            x = k[i]
             for j, _gap in pre[i]:
-                if k[j] >= k[i]:
-                    k[i] = k[j] + 1e-3
-        return sorted(range(n), key=lambda x: k[x])
+                if k[j] >= x:
+                    x = k[j] + 1e-3
+            k[i] = x
+        return [i for _x, i in sorted(zip(k, range(n)))]
     top, left, post = [0] * n, [len(p) for p in fpre], [[] for _ in range(n)]
     for i in range(n):
         for j, _gap in fpre[i]:
@@ -865,10 +878,11 @@ def arrange(ops, deps):
     kinds = {}
     kind = [kinds.setdefault((o["e"], o["w"][0][0] if o["e"][0] == "p" else o["w"][0][0].rstrip("0123456789"), o["w"][0][1] // 128), len(kinds)) for o in ops]
     cut = [1e9]
+    soon = [-SOON if o["t"] < 0 and o["w"][0][0] not in ("recf", "ht", "nxt") else 0.0 for o in ops]
 
     def both(key):
         back = place(ranked([-x for x in key], bpre), bpre, dur, eng, ne, tail)
-        late = [-(back[i] + dur[i]) for i in range(n)]
+        late = [soon[i] - back[i] - dur[i] for i in range(n)]
         return late, place(ranked(late, fpre), fpre, dur, eng, ne, zero)
     def held(order, case):
         d, pre = case
@@ -895,7 +909,10 @@ def arrange(ops, deps):
     heads = [like[(("a", "X"), 1, 0)][0]] + like[(("a", "X"), 1, 1)]
     start = place(todo, fpre, dur, eng, ne, zero)
     best, low, cur, pairs = None, 0.0, 0.0, []
+    fresh, kept = start, start
     for it in range(ROUNDS):
+        if it and it % TRY == 0 and it <= TRY * TRIES:
+            start, cur, cut[0] = (fresh, 1e9, 1e9) if it < TRY * TRIES else (kept, low, 1e9)
         way = rnd() if it > 8 else 1.0
         if way < PAIR:
             j, i = pairs[int(rnd() * len(pairs))]
@@ -929,13 +946,54 @@ def arrange(ops, deps):
                 mid, amp = rnd() * max(key), NOISE * rnd()
                 key = [x + amp * rnd() if abs(x - mid) < WIDE else x for x in key]
             late, new = both(key)
-        order = sorted(range(n), key=lambda x: (new[x], top[x]))
-        val = length(order)
+        order = [i for _x, _y, i in sorted(zip(new, top, range(n)))]
+        one = length(order, cases[:1])
+        if one > cut[0] + 1000.0:
+            continue
+        val = (one + length(order, cases[1:])) / len(cases)
         if best is None or val <= cur + HEAT * (1.0 - it / ROUNDS) * rnd():
-            start, cur = new, val
+            start, cur, cut[0] = new, val, one
             if PAIR:
                 pairs = held(order, cases[1]) + held(order, cases[int(rnd() * len(cases))])
             if best is None or val < low:
+                best, low, kept = order, val, new
+    after = [set(j for j, _gap in p) for p in bpre]
+
+    def swap(order, j, i, ahead):
+        a, b = order.index(j), order.index(i)
+        if a > b:
+            return order
+        part = order[a:b + 1] if ahead else order[a:b + 1][::-1]
+        tie = deps if ahead else after
+        need, engs, up = set(tie[part[-1]]), set(), [part[-1]]
+        for k in reversed(part[:-1]):
+            if k in need or eng[k] in engs:
+                if eng[k] == eng[i]:
+                    return order
+                up.append(k)
+                need.update(tie[k])
+                engs.add(eng[k])
+        moved = set(up)
+        part = up[::-1] + [k for k in part if k not in moved]
+        return order[:a] + (part if ahead else part[::-1]) + order[b + 1:]
+    order, cur, one = best, low, length(best, cases[:1])
+    pairs = held(order, cases[0]) + held(order, cases[2])
+    for it in range(SWAPS):
+        j, i = pairs[int(rnd() * len(pairs))]
+        ahead, new = rnd() < 0.5, order
+        twins = [(x, y) for x in like[ops[j]["like"]] for y in like[ops[i]["like"]] if ops[x]["t"] - ops[y]["t"] == ops[j]["t"] - ops[i]["t"]]
+        for x, y in (twins if rnd() < 0.5 else [(j, i)]):
+            new = swap(new, x, y, ahead)
+        if new is order:
+            continue
+        two = length(new, cases[:1])
+        if two > one + 500.0:
+            continue
+        val = (two + length(new, cases[1:])) / len(cases)
+        if val <= cur + WARM * (1.0 - it / SWAPS) * rnd():
+            order, cur, one = new, val, two
+            pairs = held(order, cases[0]) + held(order, cases[1 + int(rnd() * (len(cases) - 1))])
+            if val < low:
                 best, low = order, val
     return best, low
 

import math
from concourse.bass import DstId, RemoteDMATransfer
from concourse.mybir import AluOpType, ActivationFunctionType

ALU = AluOpType
AF = ActivationFunctionType

V, NB, S0, TH, RO = 2048, 3072, 512, 256, 4
ND = [[48, 40], [48, 40], [48, 40], [48, 40]]
NM = [[10, 10], [10, 10], [10, 10], [10, 10]]
MB = 64
XC, XV = [64, 64], [64, 64]
ENG = {"s": "a", "n": "a", "hn": "a", "nn": "a", "Y": "aa", "shpt": "a", "nxt": "a", "d0": "a", "dl": "a",
       "cl16": "vvv", "c16": "av", "vdr": "av", "sl16": "vv", "off": "av", "xl": "vv"}
OF = 64
DB, CB = ["ps0", "ps1"], ["ps4", "ps5"]
TURN, TTK, GROW = True, 0.85, True
SHORT, EXACT, SEEN, ZB = [True, True], [True, True], True, "ps7"
FLAGS, AB = ["tnsf", "stfn"], [None, None]
PT, PS = 4, 2
GC, SC, LAT, PEC, CYC, REM, KB, DM0 = 1.56, 3.8, 260.0, 0.46, 0.9, 1800.0, 4.0, 1100.0
FIRST, PAIR, MOVES, WIDE = 1500.0, 0.0, [0.3, 0.35, 0.7], 4000.0
ROUNDS, NOISE, AHEAD, SWAPS, HEAT, SEED = 3500, 1300.0, 0.5, 0, 300.0, 2
OA, SOON, WARM, TRY, TRIES = 0.0, 0.0, 100.0, 400, 0
CASES = [(200.0, 0.92, 1.0, 1500.0, 1.0, 1.0), (120.0, 1.05, 0.8, 1300.0, 1.0, 0.8), (300.0, 1.0, 1.0, 2500.0, 1.0, 1.0), (200.0, 1.3, 1.25, 1800.0, 1.0, 1.0)]
MW = 136
MAG = 12582912.0
BIG = 2.0 ** 93
U = 2.0 ** -16
LR, L0 = math.log(1.7), 63.0

F32, BF, F16, I32, U16 = "float32", "bfloat16", "float16", "int32", "uint16"
SCRATCH = {}


def _sb(names, cols, dt):
    for n in names.split():
        SCRATCH[n] = ("sbuf", [128] + (list(cols) if isinstance(cols, (list, tuple)) else [cols]), dt)


_sb("shpi", V, I32)
_sb("rect", V + TH, I32)
_sb("nbr", 128 * RO, BF)
_sb("shph", V, F16)
_sb("recf shpt", V + TH, F32)
_sb("boxt X", 4096, BF)
_sb("Dab", [32, 128], BF)
_sb("bnd", S0, I32)
_sb("ht", 1536, F32)
_sb("nxt", 1536 + TH, F32)
_sb("ident", V, F32)
_sb("obi pci", 16, I32)
_sb("tvb", [4, 64], BF)
_sb("drb ndr", 8, BF)
_sb("land1 land2 land3", [8, MW], F16)
_sb("ol16 sl16 nl16 xl16 offo offn", 16, U16)
_sb("cl16", TH, U16)
_sb("ol1 ol2 ol3", 48, U16)
_sb("ol32 nl32 xm of32 on32 il spn", 16, F32)
_sb("olh", 16, F16)
_sb("kc", 64, F32)
_sb("Wi c32 p32", TH, I32)
_sb("cpb cp1", [8, 64], F16)
_sb("KF", 64, F16)
_sb("kf", 8, F32)
_sb("s16 n16 nn16 orow Y16 m16 hn hr B1 hold scs scn key", TH, F16)
_sb("sel", 512, F16)
_sb("Kt", RO * TH, F16)
_sb("rot Sg OHT nhm OHs OHf Fo Fn ones irow Kc Vm yvb", TH, BF)
_sb("W1 Ws d0f d0r dl fs Z n32", TH, F32)
_sb("eqo eqn", 2560, BF)
_sb("col", 64, F32)
_sb("rowg rowr tm wy wx", 128, F32)
_sb("Ib nIb I11 I12 I13 I23 BO nBO E8 E8n nRm RTb R12 Dc WG AW", 128, BF)
_sb("Hw", 128, F16)
_sb("Mall M8", 144, BF)
_sb("K8", 64, BF)
_sb("GG GG2 nGG Dg", 16, BF)
_sb("G13 SB nSB Z8", 8, BF)
for _k in range(8):
    SCRATCH["ps%d" % _k] = ("psum", [128, 512], F32)

DMAS = ["d_ob", "d_tv", "d_dr", "d_rec", "d_shp", "d_box", "d_bnd", "d_yh0", "d_yh1", "d_yh2", "d_yh3", "d_yv", "d_yr0", "d_yr1"]
SEMAPHORES = ["cv", "ca", "cp", "cg", "sent"] + ["%s%d%d" % (s, t, k) for s in ("arr", "lst") for t in range(1, RO) for k in range(2)] + DMAS
ENG_SEM = {"v": "cv", "a": "ca", "p": "cp", "g": "cg"}


def lanes(topo, cores, src, dst):
    en = topo.engines(cores[src], cores[dst])
    if src // 2 == dst // 2:
        return en
    m = len(en) // 2
    return en[(dst % 2) * m:(dst % 2 + 1) * m]


def build(g, core, T, topo, rank):
    ops, tally, stage = [], {}, [-1]
    cores = T.cores
    Q = {"v": g.vector, "a": g.scalar, "p": g.tensor, "g": g, "s": g.sync}

    def A(name, lo=None, hi=None, step=1):
        if lo is None:
            return (T[name][:], [(name, 0, 1 << 20)], [])
        return (T[name][:, lo:hi:step] if step != 1 else T[name][:, lo:hi], [(name, lo, hi)], [])

    def AR(name, lo, hi):
        return (T[name][:, hi - 1::-1] if lo == 0 else T[name][:, hi - 1:lo - 1:-1], [(name, lo, hi)], [])

    def M(name, q0, q1, lo, hi, step=1):
        w = SCRATCH[name][1][2]
        pat = T[name][:, q0, lo:hi] if q1 == q0 + 1 else (T[name][:, q0:q1, lo:hi] if step == 1 else T[name][:, q0:q1:step, lo:hi])
        return (pat, [(name, q * w + lo, q * w + hi) for q in range(q0, q1, step)], [])

    def P8(name, lo, hi, step=1):
        return (T[name][0:8, lo:hi:step] if step != 1 else T[name][0:8, lo:hi], [(name, lo, hi)], [])

    def IND(win, off):
        return (win[0].indirect(off[0]), win[1], off[1])

    def op(eng, fn, rd, wr, dur, sem=None, inc=1, lat=0.0):
        r, w = [], []
        for x in rd:
            if isinstance(x, tuple):
                r.extend(x[1] + x[2])
        for x in wr:
            w.extend(x[1])
            r.extend(x[2])
        x = dur - 60.0 if any(isinstance(y, tuple) and y[2] for y in rd + wr) else 0.0
        ops.append({"e": eng, "fn": fn, "r": r, "w": w, "dur": dur, "sem": sem, "inc": inc, "lat": lat, "x": x})
        name = (eng, w[0][0] if eng == "p" else w[0][0].rstrip("0123456789"))
        name = (eng, "E") if name[1] in ("ps2", "ps3") else name
        tally[name] = tally.get(name, 0) + 1
        ops[-1]["like"], ops[-1]["t"] = (name, tally[name], min(stage[0], 1)), stage[0]

    def ap(x):
        return x[0] if isinstance(x, tuple) else x

    def dtype(x):
        return SCRATCH[x[1][0][0]][2]

    def two(x):
        return dtype(x) in (BF, F16, U16)

    def cost(eng, n, out, ins, k=None):
        if out[2]:
            return 50.0 + n * SC * CYC
        if ins[0][2]:
            return (50.0 if eng == "v" else 65.0) + n * GC * CYC
        if k is None:
            k = 0.5 if (eng == "v" and two(out) and all(two(x) for x in ins)) else 1.0
        return max(64.0, n * k) * CYC + (OA if eng == "a" else 0.0)

    def cp(out, in_, n):
        op("v", lambda: g.vector.tensor_copy(out[0], in_[0]), [in_], [out], cost("v", n, out, [in_]))

    def ts(out, in_, n, s1, o0, s2=None, o1=None):
        if o1 is None:
            fn = lambda: g.vector.tensor_scalar(out[0], in_[0], ap(s1), None, o0)
        else:
            fn = lambda: g.vector.tensor_scalar(out[0], in_[0], ap(s1), ap(s2), o0, o1)
        op("v", fn, [in_, s1, s2], [out], cost("v", n, out, [in_]))

    def tt(out, a, b, n, o):
        ps = a[1][0][0].startswith("ps") or b[1][0][0].startswith("ps")
        op("v", lambda: g.vector.tensor_tensor(out[0], a[0], b[0], o), [a, b], [out], cost("v", n, out, [a, b], TTK if out[1][0][0] == "Dab" else 1.0 if ps or (two(out) and two(a) and two(b)) else 2.0))

    def scan(out, d0, d1, n, o0=ALU.add, o1=ALU.min):
        op("v", lambda: g.vector.tensor_tensor_scan(out[0], d0[0], d1[0], 0.0, o0, o1), [d0, d1], [out], cost("v", n, out, [d0, d1]))

    def act(out, in_, n, f, bias=0.0, scale=1.0, extra=0.0):
        op("a", lambda: g.scalar.activation(out[0], in_[0], f, bias=ap(bias), scale=ap(scale)), [in_, scale, bias], [out], cost("a", n, out, [in_]) + extra)

    def silu(out, in_, n, new):
        op("a", lambda: g.scalar.activation(out[0], in_[0], AF.Silu), [in_], [out], cost("a", n, out, [in_]) + (1500.0 if new else 0.0))

    def plus(eng, out, in_, n, add=None):
        if eng == "a":
            if add is None:
                act(out, in_, n, AF.Copy)
            else:
                act(out, in_, n, AF.Identity, bias=add)
        elif add is None:
            cp(out, in_, n)
        else:
            ts(out, in_, n, add, ALU.add)

    def line(eng, out, in_, n, scale, bias):
        if eng == "a":
            act(out, in_, n, AF.Identity, bias=bias, scale=scale)
        else:
            ts(out, in_, n, scale, ALU.mult, bias, ALU.add)

    def iota(out, pat, base, cm, n):
        if dtype(out) == I32:
            fn = lambda: g.iota(out[0], pat, base, cm)
        else:
            fn = lambda: g.iota(out[0], pat, base, cm, allow_small_or_imprecise_dtypes=True)
        op("g", fn, [], [out], 130.0 + 2 * n * CYC)

    def conv(out, in_, n):
        op("g", lambda: g.affine_select(out[0], in_[0], [[0, n]], ALU.is_equal, 0.0, 0, 0), [in_], [out], 170.0 + 2 * n * CYC)

    def mm(lst):
        def fn():
            h = None
            for (o, l, r, n, st, sp) in lst:
                h = g.tensor.matmul(o[0], l[0], r[0], st, sp)
            return h
        dur = sum(n * (4 if dtype(l) == F32 else 1) for (o, l, r, n, st, sp) in lst) * PEC + 20.0
        op("p", fn, [x[1] for x in lst] + [x[2] for x in lst], [x[0] for x in lst], dur)

    def grp(out, terms, n, start=True, stop=True):
        return [(out, l, r, n, start and k == 0, stop and k == len(terms) - 1) for k, (l, r) in enumerate(terms)]

    def dma(eng, sem, out, in_, kb):
        op(eng, lambda: Q[eng].dma_start(out[0], in_[0]), [in_], [out], 60.0, sem=sem, inc=16, lat=DM0 + kb * KB)

    def H(t):
        return (t, [("hbm", 0, 0)], [])

    for eng, sem, dst, src, kb in (("s", "d_ob", A("obi"), T.ob[:], 8), ("a", "d_shp", P8("shpi", 0, V), T.shp[:], 128), ("s", "d_dr", A("drb", 0, 4), T.dr[:], 130),
                                   ("a", "d_tv", A("tvb"), T.tv[:], 190), ("s", "d_rec", A("rect", 0, V), T.rec[:], 1150),
                                   ("s", "d_box", A("boxt", 0, NB), T.box[:], 1900), ("s", "d_bnd", A("bnd"), T.bound[:], 2150)):
        dma(eng, sem, dst, H(src), kb)
        ops[-1]["w"].append(("turn" + eng, 0, 1))

    iota(A("pci", 0, 1), [[1, 1]], 0, 1, 1)
    iota(A("ident", 0, TH), [[1, TH]], 0, 0, TH)
    iota(A("rowg"), [[16, 8], [0, 16]], 0, 0, 128)
    iota(A("wx"), [[0, 16], [16, 8]], 0, 0, 128)
    for k in range(4):
        lo, hi = TH + 448 * k, TH + 448 * (k + 1)
        iota(A("ident", lo, hi), [[1, hi - lo]], lo, 0, hi - lo)
    for k in range(3):
        iota(A("nxt", 512 * k, 512 * k + 512), [[1, 512]], 512 * k + OF, 0, 512)
    C = {n: A("col", 4 * k, 4 * k + 1) for k, n in enumerate("pc rc gc nc pvc dc gm p16 hc r1 h2 p15 wb hk".split())}
    rowm, rowx, row8 = A("ident", 0, 128), A("ident", 0, 144), A("ident", 0, 128, 16)
    ts(A("pci", 4, 5), A("pci", 0, 1), 1, 15, ALU.bitwise_and)
    cp(C["pc"], A("pci", 0, 1), 1)
    cp(C["rc"], A("pci", 4, 5), 1)
    tt(C["gc"], C["pc"], C["rc"], 1, ALU.subtract)
    ts(C["nc"], C["rc"], 1, 15.0, ALU.is_equal, -16.0, ALU.mult)
    ts(C["nc"], C["nc"], 1, C["pc"], ALU.add, 1.0, ALU.add)
    ts(C["pvc"], C["rc"], 1, 0.0, ALU.is_equal, 16.0, ALU.mult)
    ts(C["dc"], C["pvc"], 1, -1.0, ALU.mult, 1.0, ALU.add)
    ts(C["pvc"], C["pvc"], 1, C["pc"], ALU.add, -1.0, ALU.add)
    ts(C["gm"], C["gc"], 1, 15.0, ALU.add)
    ts(C["p16"], C["pc"], 1, 16.0, ALU.mult)
    ts(C["p15"], C["pc"], 1, 16.0, ALU.mult, 15.0, ALU.add)
    ts(C["r1"], C["rc"], 1, 1.0, ALU.add)
    ts(C["hk"], C["rc"], 1, 15.0, ALU.not_equal, 2048.0, ALU.mult)
    ts(C["hc"], C["hk"], 1, -float(OF), ALU.add)
    ts(C["h2"], C["hc"], 1, 2048.0, ALU.add)
    ts(C["wb"], C["rc"], 1, -LR, ALU.mult, L0, ALU.add)
    iota(A("wy"), [[16, 16], [0, 8]], 0, 0, 128)
    act(A("wy"), A("wy"), 128, AF.Exp, bias=C["wb"], scale=-LR, extra=1300.0)
    ops[-1]["w"].append(("turnf", 0, 1))
    ts(A("ndr", 0, RO), A("drb", 0, RO), RO, -1.0, ALU.mult)
    ts(A("Ib"), rowm, 128, C["pc"], ALU.is_equal)
    for n, s in [("nIb", -1.0), ("I11", 2048.0), ("I12", 4096.0), ("I23", -2.0 ** 23), ("Dc", C["dc"])] + ([] if all(SHORT) else [("I13", 8192.0)]):
        act(A(n), A("Ib"), 128, AF.Identity, scale=s)
    ts(A("Hw"), A("Ib"), 128, 0.5 - 2.0 ** -11, ALU.mult)
    ts(A("Mall"), rowx, 144, C["gm"], ALU.is_equal)
    ts(A("M8"), rowx, 144, C["p15"], ALU.is_equal, 2048.0, ALU.mult)
    ts(A("BO"), A("rowg"), 128, C["gc"], ALU.is_equal)
    act(A("nBO"), A("BO"), 128, AF.Identity, scale=-1.0)
    ts(A("E8"), A("rowg"), 128, C["p16"], ALU.is_equal)
    act(A("E8n"), A("E8"), 128, AF.Identity, scale=-4096.0)
    for k in range(4):
        lo, hi = 512 * k, 512 * k + 512
        cp(P8("shph", lo, hi), P8("shpi", lo, hi), 512)
        mm([(A("ps%d" % (k + 2)), P8("E8", 0, 128), P8("shph", lo, hi), 512, True, True)])
        act(A("shpt", lo, hi), A("ps%d" % (k + 2)), 512, AF.Silu, bias=float(OF), extra=0.0 if k else 1500.0)
        ops[-1]["w"].append(("turnf", 0, 1))
    tt(A("rowr"), rowm, A("rowg"), 128, ALU.subtract)
    for n, s in (("GG", 1.0), ("GG2", 2.0), ("nGG", -1.0)):
        ts(A(n, 0, 8), row8, 8, C["gc"], ALU.is_equal, s / 2048, ALU.mult)
        ts(A(n, 8, 16), row8, 8, C["gc"], ALU.is_equal, s, ALU.mult)
    ts(A("G13"), row8, 8, C["gc"], ALU.is_equal, 8192.0, ALU.mult)
    ts(A("SB"), row8, 8, C["pc"], ALU.is_equal, BIG, ALU.mult)
    ts(A("nSB"), row8, 8, C["pc"], ALU.is_equal, -BIG, ALU.mult)
    ts(A("Z8"), row8, 8, 0.0, ALU.mult)
    ts(A("Dg"), A("ident", 0, 16), 16, C["rc"], ALU.is_equal, -2.56, ALU.mult)
    ts(A("K8"), A("rowg", 0, 128, 2), 64, C["gc"], ALU.is_equal)
    nms = sorted(set(x for y in NM for x in y if x))
    assert len(nms) <= 1
    for nm in nms:
        ts(A("Vm", 128, 256), A("rowr"), 128, float(nm), ALU.is_lt)
        tt(A("Vm", 128, 256), A("Vm", 128, 256), A("nBO"), 128, ALU.mult)
        ts(A("Vm", 0, 128), A("Vm", 128, 256), 128, 1.0 / 2048, ALU.mult)
        for t in range(RO):
            ts(A("Kt", TH * t, TH * t + 128), A("Vm", 0, 128), 128, A("drb", t, t + 1), ALU.mult, -1.0 / 128, ALU.add)
            ts(A("Kt", TH * t + 128, TH * t + TH), A("Vm", 128, 256), 128, A("drb", t, t + 1), ALU.mult)
    ts(A("nRm"), rowm, 128, C["nc"], ALU.is_equal)
    tt(A("nRm"), A("Ib"), A("nRm"), 128, ALU.subtract)
    ts(A("RTb"), rowm, 128, C["pvc"], ALU.is_equal)
    tt(A("RTb"), A("RTb"), A("Ib"), 128, ALU.subtract)
    if not all(SHORT):
        act(A("RTI"), A("RTb"), 128, AF.Copy)
    act(A("R12"), A("RTb"), 128, AF.Identity, scale=4096.0)
    iota(A("kf"), [[128, 8]], NB - 2048, 1, 8)
    for j in range(2 * RO):
        ts(A("KF", 8 * j, 8 * j + 8), row8, 8, C["gc"], ALU.is_equal, A("kf", j, j + 1), ALU.mult)
    ts(A("tm"), A("rowr"), 128, C["rc"], ALU.not_equal, 1.0e7, ALU.mult)
    act(A("tm"), A("tm"), 128, AF.Identity, bias=-1.0 + 16 * U)
    ts(A("Y16", 0, 128), A("rowr"), 128, C["rc"], ALU.is_equal, 8192.0, ALU.mult)
    ts(A("m16", 0, 128), A("rowr"), 128, C["r1"], ALU.is_equal, -2048.0, ALU.mult)
    ts(A("il"), A("ident", 0, TH, 16), 16, C["rc"], ALU.add)
    ts(A("spn"), A("il"), 16, C["h2"], ALU.subtract, 1536.0, ALU.add)
    for k in range(RO - 1):
        if not all(EXACT):
            act(A("kc", 16 * k, 16 * k + 16), A("il"), 16, AF.Identity, bias=float(NB - 2048 + TH * k))
    act(A("ones", 0, 128), rowm, 128, AF.Identity, bias=1.0, scale=0.0)
    act(A("irow"), A("ident", 0, TH), TH, AF.Copy)
    ts(A("AW"), A("wx"), 128, C["gc"], ALU.is_equal)
    tt(A("WG"), A("wy"), A("AW"), 128, ALU.mult)
    for h in range(2):
        tt(A("hold", 128 * h, 128 * h + 128), A("Y16", 0, 128), A("m16", 0, 128), 128, ALU.add)
    act(A("d0f"), A("ident", 0, TH), TH, AF.Identity, bias=-U, scale=0.0)
    act(A("d0f", 0, TH, 16), A("il"), 16, AF.Identity, bias=1.0e6, scale=0.0)
    act(A("d0r"), A("ident", 0, TH), TH, AF.Identity, bias=U, scale=0.0)
    act(A("d0r", 15, TH, 16), A("il"), 16, AF.Identity, bias=1.0e6, scale=0.0)
    conv(A("ht", 0, S0), A("bnd"), S0)
    iota(A("nbr"), [[TH, RO], [0, 128]], NB, 0, 128 * RO)

    def pairs(buf, row, keys, cs, blocks, less=None):
        for c in cs:
            lo = 64 * (c // 4) if blocks else 16 * c
            out = A(buf, eoff[c] + lo % 64, eoff[c + 1])
            if less is None:
                ts(out, row(lo), TH - lo, A(keys, c, c + 1), ALU.is_equal)
            else:
                ts(out, row(lo), TH - lo, A(keys, c, c + 1), ALU.subtract, less, ALU.is_equal)

    eoff = [sum(256 - 64 * (k // 4) for k in range(c)) for c in range(17)]

    def sums(lo, buf, wts, cs, last, start=False):
        for c0 in range(0, len(cs), PS):
            lst = []
            for c in cs[c0:c0 + PS]:
                w = A(wts, 8 * c, 8 * c + 8)
                lst.append((P8("ps6", lo + 16 * c, lo + TH), w, A(buf, eoff[c] + 16 * c % 64, eoff[c + 1]), TH - 16 * c, start and c == 0, False))
                lst.append((P8("ps6", lo + 16 * c, lo + 16 * c + 16), w, A("Dg"), 16, False, last and c == cs[-1]))
            mm(lst)

    def places(flags, keys):
        out = A("ps6", 256, 272)
        return [(out, P8("M8", 15 - r, 143 - r), P8(flags, r, TH, 16), 64, r == 0, False) for r in range(16)] + [(out, A("Ib"), keys, 64, False, True)]

    own, par = rank // 2, rank % 2
    horder = [1 - own, own]
    vo, oo, po = 8 * par, 64 + 8 * par, 128 - 124 * par

    def pieces(t, h):
        if h != own:
            return [(128 * h, 128, A("ol%d" % t, 32, 40))]
        return [(64 * rank, 64, A("ol%d" % t, 16 + 12 * par, 20 + 12 * par)), (64 * (rank ^ 1), 64, A("ol%d" % t, 40, 44))]

    def send(t, k, sem, parts, extra):
        def fn():
            trs = []
            for q, src, dst, _here in parts:
                rid, pid, _se = topo.addr(cores[q])
                trs.append(RemoteDMATransfer(dst_ids=[DstId(rid=rid, pnc=pid)], dma_engine_mask=sum(1 << e for e in lanes(topo, cores, rank, q)),
                                             remote_sem=T.sem[sem], src=src[0], dst=dst[0]))
            g.remote_dma_fused(trs, local_sem=T.sem.sent)
            return None
        net = (None, [("net" + sem, 0, 1)], [])
        op("g", fn, [x[1] for x in parts], [net], 300.0, sem="none", lat=extra)
        op("r", None, [net], [x[3] for x in parts], 0.0, sem=sem, inc=sum(len(lanes(topo, cores, x[0], rank)) for x in parts), lat=REM)

    for t in range(RO):
        first, last = t == 0, t == RO - 1
        tally.clear()
        stage[0] = t
        land, nb, ns = "land%d" % t, NB + TH * t, S0 + TH * t
        drc = A("drb", t, t + 1)
        hs = lambda n, h, w=128: A(n, w * h, w * h + w)
        DA = lambda h, a0, a1, lo, hi: M("Dab", 16 * h + a0, 16 * h + a1, lo, hi)
        vv = lambda q0, q1: M("tvb", q0, q1, 0, 64) if first else M(land, 3 + q0, 3 + q1, vo, vo + 64)
        cc = lambda h: M("cpb", 4 * h + 1, 4 * h + 3, 0, 64)
        pp = lambda h: M("cpb", 4 * h, 4 * h + 4, 0, 64, 3)
        for k in range(8 if last else 0):
            conv(A("recf", TH * k, TH * k + TH), A("rect", TH * k, TH * k + TH), TH)
        if first:
            cp(A("ol16"), A("obi"), 16)
            cp(A("olh"), A("obi"), 16)
            cp(A("ol32"), A("obi"), 16)
            cp(A("orow"), IND(A("ident"), A("ol16")), TH)
        for k, h in enumerate(horder):
            h8 = lambda n: hs(n, h, 8)
            if first:
                ts(hs("c32", h), IND(A("rect", 0, V), h8("ol16")), 128, 4095, ALU.bitwise_and)
                cp(hs("cl16", h), hs("c32", h), 128)
                ts(hs("p32", h), IND(A("rect", 0, V), h8("ol16")), 128, 12, ALU.arith_shift_right)
            else:
                conv(h8("ol32"), M(land, 3 + 2 * h, 5 + 2 * h, po, po + 4), 8)
                for j, (lo, n, ol) in enumerate(pieces(t, h)):
                    ts(A("c32", lo, lo + n), IND(A("rect", 0, V), ol), n, 4095, ALU.bitwise_and)
                    plus(ENG["cl16"][k + j], A("cl16", lo, lo + n), A("c32", lo, lo + n), n)
                    ts(A("p32", lo, lo + n), IND(A("rect", 0, V), ol), n, 12, ALU.arith_shift_right)
            if ENG["c16"][k] == "a":
                plus("a", cc(h), hs("c32", h), 128, -2048.0)
            else:
                ts(cc(h), hs("cl16", h), 128, -2048.0, ALU.add)
            conv(pp(h), hs("p32", h), 128)
            plus(ENG["vdr"][k], A("boxt", nb + 128 * h, nb + 128 * h + 128), vv(2 * h, 2 * h + 2), 128, A("ndr", t, t + 1))
            if not first:
                for lo, n, ol in pieces(t, h):
                    plus(ENG["s"], A("s16", lo, lo + n), IND(A("shpt", 0, V), ol), n)
                scan(hs("scs", h), hs("hold", h), hs("s16", h), 128)
                plus(ENG["sl16"][k], h8("sl16"), A("scs", 128 * h + 15, 128 * h + 128, 16), 8, C["hc"])
                plus(ENG["n"], hs("n16", h), IND(A("nxt", 0, 1536), h8("sl16")), 128)
            else:
                plus(ENG["n"], hs("n16", h), IND(A("shpt", 0, V), h8("ol16")), 128)
            scan(hs("scn", h), hs("hold", h), hs("n16", h), 128)
            ts(h8("nl16"), A("scn", 128 * h + 15, 128 * h + 128, 16), 8, C["hc"], ALU.add)
            conv(h8("nl32"), A("scn", 128 * h + 15, 128 * h + 128, 16), 8)
            if not last and ENG["shpt"] == "a":
                conv(hs("n32", h), hs("n16", h), 128)
            plus("v" if first else ENG["hn"], hs("hn", h), IND(A("bnd") if first else A("ht", 0, ns), h8("nl16")), 128, -2048.0)
            S7 = lambda k: A("ps7", 128 * k, 128 * k + 128)
            short = SHORT[horder.index(h)]
            if not first:
                if h == own:
                    plus(ENG["nn"], A("nn16"), IND(A("nxt", 0, 1536), A("nl16")), TH)
                tt(hs("rot", h), hs("n16", h), hs("s16", h), 128, ALU.not_equal)
                tt(hs("hr", h), hs("hn", h), hs("rot", h), 128, ALU.mult)
                if short:
                    tt(M("cp1", 4 * h, 4 * h + 4, 0, 64, 3), pp(h), hs("rot", h), 128, ALU.mult)
                    tt(M("cp1", 4 * h + 1, 4 * h + 3, 0, 64), cc(h), hs("rot", h), 128, ALU.mult)
                mm(grp(S7(0), [(hs("rot", h), A("Dc"))], 128))
                line(ENG["d0"], A("d0f", 128 * h + 1, 128 * h + 128, 16), A("ps7", 1, 128, 16), 8, 16 * U, -U)
                line(ENG["d0"], A("d0r", 128 * h, 128 * h + 128, 16), A("ps7", 1, 128, 16), 8, -16 * U, U)
                line(ENG["dl"], hs("dl", h), S7(0), 128, U, -1.0)
        long = [h for h in horder if not (first or SHORT[horder.index(h)])]
        for h in long:
            mm(grp(S7(1), [(A("I23"), hs("rot", h)), (A("I12"), pp(h)), (A("Ib"), cc(h))], 128))
            act(hs("W1", h), S7(1), 128, AF.Relu, bias=2048.0 - 2.0 ** 23)
        turned = lambda h: [(A("R12"), M("cp1", 4 * h, 4 * h + 4, 0, 64, 3)), (A("RTb"), M("cp1", 4 * h + 1, 4 * h + 3, 0, 64))]
        mm(sum([grp(S7(2 + h), [(A("I12"), pp(h)), (A("Ib"), cc(h))] + ([] if first else [(A("RTI"), hs("W1", h))] if h in long else turned(h)), 128) for h in horder], []))
        act(A("Ws"), A("ps7", 256, 512), TH, AF.Identity, bias=2048.0)
        chunks = list(range(16))
        if first or GROW:
            for h in ([] if first else horder):
                conv(hs("orow", h), M(land, 3 + 2 * h, 5 + 2 * h, oo, oo + 64), 128)
            pairs("eqo", lambda lo: A("orow", lo, TH), "ol32", chunks, False)
        else:
            pairs("eqo", lambda lo: M(land, 3 + lo // 64, 7, oo, oo + 64), "ol32", chunks, True)
        sums(0, "eqo", "WG", chunks, True, True)
        act(P8("Fo", 0, TH), P8("ps6", 0, TH), TH, AF.Sign)
        mm(places("Fo", A("olh") if first else M(land, 3, 7, po, po + 4)))
        tt(A("of32"), A("ps6", 256, 272), A("il"), 16, ALU.min)
        plus(ENG["off"][0], A("offo"), A("of32"), 16, 2048.0)
        if not last:
            if ENG["shpt"] == "a":
                silu(IND(A("shpt"), A("offo")), A("n32"), TH, False)
            else:
                cp(IND(A("shpt"), A("offo")), A("n16"), TH)
        pairs("eqn", lambda lo: A("n16", lo, TH), "nl32", chunks, False, C["hk"])
        out = P8("ps6", TH, 2 * TH)
        if first:
            mm(grp(out, [(A("Z8"), A("irow"))], TH, stop=False))
        else:
            mm(grp(out, [(A("SB"), A("nn16")), (A("nSB"), A("n16"))], TH, stop=False))
        for k, h in enumerate(horder):
            h8 = lambda n: hs(n, h, 8)
            E, cb = "ps%d" % (2 + h), CB[k]
            nm, nd = NM[t][k], ND[t][k]
            flip = par if k else 0
            done = 0
            for eng, n in [("a", n) for n in XC] + [("v", n) for n in XV]:
                n = min(n, (128 - nd if eng == "a" else 128) - done)
                if n > 0:
                    lo = 128 * h + (128 - done - n if flip else done)
                    plus(eng, A("X", 16 * lo, 16 * (lo + n)), IND(A("boxt", 0, nb), A("cl16", lo, lo + n)), 16 * n)
                    if TURN and eng == "a":
                        ops[-1]["w"].append(("turn", 0, 1))
                    done += n
            assert done == 128
            if nm:
                terms = [(hs("ones", 0), A("Kt", TH * t, TH * t + TH)), (A("boxt", nb + 128 * h, nb + 128 * h + 128), A("Vm"))]
            else:
                terms = [(hs("ones", 0), A("Kc"))]
            mm(grp(A(E, 0, 256), terms, 256, stop=False))
            eo = lambda a: A(E, a, 256, 16)
            aa = list(range(nm, 16))
            tiles = [(b ^ flip, aa[j:j + 8]) for b in range(2) for j in range(0, len(aa), 8)]
            for j, (b, part) in enumerate(tiles):
                bank = DB[(len(tiles) * k + j) % len(DB)]
                x0 = 2048 * h + 1024 * b
                for m0 in range(0, len(part), PT):
                    mm(sum([grp(A(bank, 64 * m, 64 * m + 64), [(A("Ib"), A("X", x0 + part[m], x0 + 1024, 16)), (A("nIb"), vv(2 * h + b, 2 * h + b + 1))], 64)
                            for m in range(m0, min(len(part), m0 + PT))], []))
                act(DA(h, part[0], part[-1] + 1, 64 * b, 64 * b + 64), A(bank, 0, 64 * len(part)), 64 * len(part), AF.Abs)
                if TURN:
                    ops[-1]["r"].append(("turn", 0, 1))
            if nm:
                mm([(eo(a), A("X", 2048 * h + a, 2048 * h + 2048, 16), A("nGG"), 64, False, False) for a in range(nm)])
            for lo in list(range(0, 128, MB))[::-1 if flip else 1]:
                x0 = 2048 * h + 16 * lo
                for a in range(nm):
                    tt(DA(h, a, a + 1, lo, lo + MB), A("X", x0 + a, x0 + 16 * MB, 16), vv(2 * h + lo // 64, 2 * h + (lo + MB) // 64), MB, ALU.max)
            he = A(E, 128, 256)
            mm([(he, hs("hn", h), A("nIb"), 128, False, False)] + ([] if first else [(he, hs("hr", h), A("nRm"), 128, False, False)]))
            for j in range(0, nm, 4):
                mm([(eo(a), DA(h, a, a + 1, 0, 128), A("GG2"), 64, False, a == 15) for a in range(j, min(nm, j + 4))])
            for j in range(nm, 16, 8):
                mm([(eo(a), DA(h, a, a + 1, 0, 128), A("GG"), 64, False, a == 15) for a in range(j, min(16, j + 8))])
            act(hs("Sg", h), he, 128, AF.Sign, bias=-2048.5)
            tt(hs("key", h), A(E, 0, 128), hs("Sg", h), 128, ALU.min)
            scan(hs("fs", h), hs("d0f", h), hs("key", h), 128)
            scan(AR(E, 384, 512), AR("d0r", 128 * h, 128 * h + 128), AR("fs", 128 * h, 128 * h + 128), 128)
            rs = A(E, 384, 512)
            short = SHORT[k] or first
            exact = last or EXACT[k]
            fits = hs("OHf", h)
            flags = {"s": lambda: ts(hs("OHs", h), rs, 128, -1.0, ALU.not_equal) if first else tt(hs("OHs", h), rs, hs("dl", h), 128, ALU.not_equal),
                     "t": lambda: None if last and exact else tt(hs("OHT", h), rs, hs("key", h), 128, ALU.is_equal),
                     "f": lambda: ts(fits, rs, 128, -1.0, ALU.is_equal) if exact else None,
                     "n": lambda: tt(hs("nhm", h), rs, A("tm"), 128, ALU.is_ge)}
            for x in ("stfn" if last else FLAGS[k]):
                flags[x]()
            sl = 256 * h
            q0, q1 = (1, 3) if last else (0, 4)

            def change():
                terms = [(A("I12"), pp(h)), (A("Ib"), hs("irow", h))] + ([] if first else [(A("R12"), M("cp1", 4 * h, 4 * h + 4, 0, 64, 3))])
                terms += ([] if last else [(A("Ib"), A("nbr", 128 * t, 128 * t + 128))]) + [(hs("OHs", h), A("I23"))]
                mm(grp(A(cb, 384, 512), terms, 128))
                if last:
                    act(hs("Z", h), A(cb, 384, 512), 128, AF.Identity, bias=float(nb))
                    tt(IND(A("recf"), h8("offo")), hs("Ws", h), hs("Z", h), 128, ALU.max)
                else:
                    tt(hs("Wi", h), A(cb, 384, 512), hs("Ws", h), 128, ALU.max)
                    cp(IND(A("rect"), h8("offo")), hs("Wi", h), 128)
            cb, ob = (ZB if short and ZB else CB[k]), CB[k]
            if short and (SEEN or last):
                change()
            cb = ob
            ab = AB[k] or cb
            ask = [(A(ab, 256, 320), hs("nhm", h), A("K8"), 64, True, True)]
            mm([(A(cb, 64 * q, 64 * q + 64), fits if exact and q in (1, 2) else hs("OHT", h), A("Ib", 64 * (q // 2), 64 * (q // 2) + 64), 64, True, True) for q in range(q0, q1)]
               + ([] if AB[k] else ask))
            tt(A("sel", sl + 64 * q0, sl + 64 * q1), A(cb, 64 * q0, 64 * q1), M("cpb", 4 * h + q0, 4 * h + q1, 0, 64), 64 * (q1 - q0), ALU.mult)
            if AB[k]:
                mm(ask)
            tt(hs("AW", h, 64), A(ab, 256, 320), hs("WG", h, 64), 64, ALU.mult)
            lists = A(E, 128 + 4 * q0, 128 + 4 * q1)
            mm([(lists, A("Mall", 15 - r, 143 - r), A("sel", sl + 64 * q0 + r, sl + 64 * q1, 16), 64, r == 0, False) for r in range(16)]
               + [(A(E, 132, 140), hs("nhm", h), A("KF", 16 * t + 8 * h, 16 * t + 8 * h + 8) if exact else A("G13"), 64, False, True)])
            if exact:
                plus(ENG["xl"][k], h8("xl16"), A(E, 132, 140), 8, 2048.0)
            if not last:
                nol, qs = "ol%d" % (t + 1), [q for q in (2 * h, 2 * h + 1) if q != rank]
                plus(ENG["xl"][k], A(nol, 16 * k, 16 * k + 16), A(E, 128, 144), 16)
                at = lambda q: A(nol, 40 if k else 32 + 4 * (q % 2), 44 if k else 36 + 4 * (q % 2))
                send(t, k, "lst%d%d" % (t + 1, k), [(q, A(nol, 16 * k + 12 * (q % 2), 16 * k + 12 * (q % 2) + 4), at(rank), at(q)) for q in qs],
                     FIRST if first and k == 0 else 0.0)
            if not exact:
                tt(h8("xm"), A(E, 132, 140), A("kc", 16 * t + 8 * h, 16 * t + 8 * h + 8), 8, ALU.min)
                ts(h8("xl16"), h8("xm"), 8, 2048.0, ALU.add)
            if not (short and (SEEN or last)):
                change()
            plus(ENG["Y"][k], hs("Y16", h), IND(A("boxt", 0, nb + TH), h8("xl16")), 128, drc)
            if not last:
                nbx = A("boxt", nb + 128 * h, nb + 128 * h + 128)
                mm(grp(A(cb, 256, 384), [(A("Hw"), hs("Y16", h)), (A("Hw"), nbx)], 128))
                ts(nbx, A(cb, 256, 384), 128, MAG, ALU.add, -MAG, ALU.add)
            ts(hs("m16", h), hs("Y16", h), 128, 256.0, ALU.is_ge, 256.0, ALU.mult)
            if last:
                mm(grp(A(E, 0, 128), [(A("Ib"), hs("Y16", h)), (A("nIb"), hs("m16", h))], 128))
                act(hs("yvb", h), A(E, 0, 128), 128, AF.Copy)
            else:
                nxl = "land%d" % (t + 1)
                lst = []
                for b in range(2):
                    lst += grp(A(E, 64 + 144 * b, 128 + 144 * b), [(A("BO"), A("sel", sl + 192 * b, sl + 192 * b + 64))], 64)
                for b in range(2):
                    x0 = 128 * h + 64 * b
                    lst += grp(A(E, 144 * b, 144 * b + 64), [(A("Ib"), A("Y16", x0, x0 + 64)), (A("nIb"), A("m16", x0, x0 + 64))], 64)
                mm(lst)
                qs = [q for q in (2 * h, 2 * h + 1) if q != rank]
                slot = {q: (3 + q if q == rank else (q % 2 if h != own else (2 if par else 7))) for q in (2 * h, 2 * h + 1)}
                act(M(nxl, slot[2 * h], slot[2 * h + 1] + 1, 0, MW, slot[2 * h + 1] - slot[2 * h]), A(E, 0, 2 * MW), 2 * MW, AF.Copy)
                send(t, k, "arr%d%d" % (t + 1, k), [(q, M(nxl, slot[q], slot[q] + 1, 0, MW), M(nxl, 3 + rank, 4 + rank, 0, MW), M(nxl, 3 + q, 4 + q, 0, MW)) for q in qs], 0.0)
            sums(TH, "eqn", "AW", list(range(8 * h, 8 * h + 8)), k == 1)
            if not first:
                mm(grp(rs, [(hs("key", h), A("I11"))], 128))
                tt(hs("B1", h), rs, hs("rot", h), 128, ALU.mult)
        if last:
            dma("s", "d_yr0", H(T.yr[:, 0:V // 2]), A("recf", 0, V // 2), 1024)
            dma("a", "d_yr1", H(T.yr[:, V // 2:V]), A("recf", V // 2, V), 1024)
            dma("s", "d_yv", H(T.yv[:]), A("yvb"), 64)
        act(P8("Fn", 0, TH), P8("ps6", TH, 2 * TH), TH, AF.Sign, bias=2.0 ** -115)
        if not last:
            mm(places("Fn", A("scn", 15, TH, 16)))
            tt(A("on32"), A("ps6", 256, 272), A("spn"), 16, ALU.min)
            plus(ENG["off"][1], A("offn"), A("on32"), 16, C["h2"])
            if ENG["nxt"] == "a":
                silu(IND(A("nxt"), A("offn")), A("ident", ns + OF, ns + OF + TH), TH, False)
            else:
                cp(IND(A("nxt"), A("offn")), A("ident", ns + OF, ns + OF + TH), TH)
        mm(sum([grp(hs("ps6", h), [(hs("key", h), A("I11")), (P8("E8n", 0, 128), P8("Fn", 128 * h, 128 * h + 128))]
                    + ([] if first else [(A("RTb"), hs("B1", h))]), 128) for h in horder], []))
        act(A("ht", ns, ns + TH), A("ps6", 0, TH), TH, AF.Relu, bias=-2048.0)
        dma("s", "d_yh%d" % t, H(T.yh[:, TH * t:TH * t + TH]), A("ht", ns, ns + TH), 128)
    return ops, Q


def depend(ops):
    hist = {}
    bank = {}
    deps = []
    for i, o in enumerate(ops):
        d = {}
        acc = [(r, False) for r in o["r"]] + [(r, True) for r in o["w"]]
        for (name, lo, hi), wr in acc:
            if name == "hbm":
                continue
            psum = name.startswith("ps")
            if psum and name in bank and bank[name] != i:
                j = bank[name]
                d[j] = d.get(j, False) or ops[j]["e"] != o["e"]
            for (j, l2, h2, w2) in hist.get(name, []):
                same = ops[j]["e"] == o["e"] and ops[j]["sem"] is None
                if name.startswith("turn"):
                    if wr or w2:
                        d[j] = d.get(j, False)
                elif lo < h2 and l2 < hi and (wr or w2) and (same or not psum):
                    d[j] = d.get(j, False) or (not same) or (w2 and o["e"] != "p")
        for (name, lo, hi), wr in acc:
            if name.startswith("ps"):
                if name in bank and ops[bank[name]]["e"] != o["e"]:
                    hist[name] = []
                bank[name] = i
            hist.setdefault(name, []).append((i, lo, hi, wr))
        deps.append(d)
    for i in range(len(ops)):
        d = deps[i]
        for j in sorted(d, reverse=True):
            if j in d and d[j]:
                for k, w in deps[j].items():
                    if k in d and (w or not d[k]):
                        del d[k]
    return deps


def passes(ops, pre, post, prio, back):
    n = len(ops)
    left = [len(p) for p in pre]
    est = [0.0] * n
    start = [0.0] * n
    ready, free, order = {}, {}, []
    for i in range(n):
        ready.setdefault(ops[i]["e"], [])
        if left[i] == 0:
            ready[ops[i]["e"]].append(i)
            est[i] = ops[i]["lat"] if back else 0.0
    while len(order) < n:
        t0, e = min((max(free.get(e, 0.0), min(est[i] for i in lst)), e) for e, lst in ready.items() if lst)
        i = max((k for k in ready[e] if est[k] <= t0 + 1e-6), key=lambda k: prio[k])
        for k in ready[e]:
            if est[k] > t0 and est[k] - t0 < AHEAD * ops[i]["dur"] and prio[k] > prio[i] + ops[i]["dur"]:
                i = k
        ready[e].remove(i)
        start[i] = max(t0, est[i])
        free[e] = start[i] + ops[i]["dur"]
        order.append(i)
        for k, gap in post[i]:
            est[k] = max(est[k], start[i] + gap)
            left[k] -= 1
            if left[k] == 0:
                ready[ops[k]["e"]].append(k)
    fin = [start[i] + ops[i]["dur"] + (0.0 if back else ops[i]["lat"]) for i in range(n)]
    return order, start, fin


def schedule(ops, deps):
    n = len(ops)
    fpre, fpost, bpre, bpost = [[[] for _ in range(n)] for _ in range(4)]
    for i in range(n):
        for j, w in deps[i].items():
            gap = ops[j]["lat"] + LAT if w else 0.0
            fpre[i].append(j)
            fpost[j].append((i, gap + ops[j]["dur"]))
            bpre[j].append(i)
            bpost[i].append((j, gap + ops[i]["dur"]))
    prio = [0.0] * n
    for i in reversed(passes(ops, fpre, fpost, prio, False)[0]):
        prio[i] = max([prio[k] + gap for k, gap in fpost[i]] + [ops[i]["dur"] + ops[i]["lat"]])
    seed = [12345]

    def rnd():
        seed[0] = (seed[0] * 1103515245 + 12345) % 2147483648
        return seed[0] / 2147483648.0
    cases = []
    for lat, f, fx, rem in CASES:
        dur = [f * (o["dur"] + (fx - 1.0) * o["x"]) for o in ops]
        cases.append((dur, [[(j, dur[j] + ((rem if ops[j]["e"][0] == "r" else ops[j]["lat"]) + lat if w else 0.0)) for j, w in deps[i].items()] for i in range(n)]))

    def length(order):
        tot = 0.0
        for dur, pre in cases:
            start, free, end = [0.0] * n, {}, 0.0
            for i in order:
                e = ops[i]["e"]
                t = free.get(e, 0.0)
                for j, gap in pre[i]:
                    if start[j] + gap > t:
                        t = start[j] + gap
                start[i] = t
                free[e] = t + dur[i]
                if t + dur[i] + ops[i]["lat"] > end:
                    end = t + dur[i] + ops[i]["lat"]
            tot += end
        return tot / len(cases)
    best = None
    for it in range(20):
        res = passes(ops, fpre, fpost, prio, False)
        val = length(res[0])
        if best is None or val < low:
            best, base, low = res, prio, val
        prio = passes(ops, bpre, bpost, [x + 300.0 * rnd() for x in res[2]], True)[2]
    kinds = {}
    kind = [kinds.setdefault((o["e"], o["w"][0][0] if o["e"][0] == "p" else o["w"][0][0].rstrip("0123456789"), o["w"][0][1] // 128), len(kinds)) for o in ops]
    shift = [0.0] * len(kinds)
    for it in range(ROUNDS):
        new = list(shift)
        for _ in range(1 + int(4 * rnd())):
            new[int(rnd() * len(kinds))] += NOISE * (2 * rnd() - 1)
        res = passes(ops, fpre, fpost, [base[i] + new[kind[i]] for i in range(n)], False)
        val = length(res[0])
        if val <= low:
            best, shift, low = res, new, val
    order = list(best[0])
    names = sorted(set(o["e"] for o in ops))
    eng = [names.index(o["e"]) for o in ops]
    tail = [o["lat"] for o in ops]

    def run(order, case):
        dur, pre = case
        start, why, free, prev, end, top = [0.0] * n, [-1] * n, [0.0] * len(names), [-1] * len(names), 0.0, 0
        for i in order:
            e = eng[i]
            t, b = free[e], prev[e]
            for j, gap in pre[i]:
                if start[j] + gap >= t:
                    t, b = start[j] + gap, j
            start[i], why[i], prev[e] = t, b, i
            t += dur[i]
            free[e] = t
            if t + tail[i] > end:
                end, top = t + tail[i], i
        swaps = []
        while why[top] >= 0:
            if why[top] not in deps[top]:
                swaps.append((why[top], top))
            top = why[top]
        return end, swaps

    def every(order):
        res = [run(order, c) for c in cases]
        return sum(r[0] for r in res) / len(res), [s for r in res for s in r[1]]
    low, swaps = every(order)
    cur, keep = low, order
    for it in range(SWAPS):
        j, i = swaps[int(rnd() * len(swaps))]
        a, b = order.index(j), order.index(i)
        for _ in range(int(3 * rnd() * rnd())):
            c = a - 1
            while c >= 0 and eng[order[c]] != eng[i]:
                c -= 1
            if c >= 0:
                a = c
        need, engs, up, ok = set(deps[i]), set(), [i], True
        for k in reversed(order[a:b]):
            if k in need or eng[k] in engs:
                if eng[k] == eng[i]:
                    ok = False
                    break
                up.append(k)
                need.update(deps[k])
                engs.add(eng[k])
        if not ok:
            continue
        moved = set(up)
        new = order[:a] + up[::-1] + [k for k in order[a:b] if k not in moved] + order[b + 1:]
        val, sw = every(new)
        if val <= cur + HEAT * (1.0 - it / SWAPS) * rnd():
            order, cur, swaps = new, val, sw
            if val < low:
                low, keep = val, new
    return keep, low


def place(seq, pre, dur, eng, ne, first):
    start = [0.0] * len(dur)
    begs, ends = [[] for _ in range(ne)], [[] for _ in range(ne)]
    for i in seq:
        t = first[i]
        for j, gap in pre[i]:
            gap += start[j]
            if gap > t:
                t = gap
        b, e, d = begs[eng[i]], ends[eng[i]], dur[i]
        lo = hi = len(b)
        while lo and e[lo - 1] > t:
            lo -= 1
        while lo < hi and b[lo] < t + d:
            t = e[lo]
            lo += 1
        b.insert(lo, t)
        e.insert(lo, t + d)
        start[i] = t
    return start


def arrange(ops, deps):
    n = len(ops)
    names = sorted(set(o["e"] for o in ops))
    eng, ne = [names.index(o["e"]) for o in ops], len(names)
    dur = [o["dur"] + 1.0 for o in ops]
    tail, zero = [o["lat"] for o in ops], [0.0] * n
    fpre, bpre = [[] for _ in range(n)], [[] for _ in range(n)]
    for i in range(n):
        for j, w in deps[i].items():
            gap = ops[j]["lat"] + LAT if w else 0.0
            fpre[i].append((j, gap + dur[j]))
            bpre[j].append((i, gap + dur[i]))
    cases = []
    for lat, f, fx, rem, fp, fd in CASES:
        d = [f * (o["dur"] * (fp if o["e"] == "p" else 1.0) + (fx - 1.0) * o["x"]) for o in ops]
        cases.append((d, [[(j, d[j] + ((rem if ops[j]["e"][0] == "r" else fd * ops[j]["lat"]) + lat if w else 0.0)) for j, w in deps[i].items()] for i in range(n)]))

    def length(order, some):
        tot = 0.0
        for d, pre in some:
            start, free = [0.0] * n, [0.0] * ne
            for i in order:
                e = eng[i]
                t = free[e]
                for j, gap in pre[i]:
                    gap += start[j]
                    if gap > t:
                        t = gap
                start[i] = t
                free[e] = t + d[i]
            tot += max(start[i] + d[i] + tail[i] for i in ends)
        return tot
    ends = [i for i in range(n) if not bpre[i]]
    seed = [SEED]

    def rnd():
        seed[0] = (seed[0] * 1103515245 + 12345) % 2147483648
        return seed[0] / 2147483648.0

    def ranked(key, pre):
        k = list(key)
        for i in (todo[::-1] if pre is bpre else todo):
            x = k[i]
            for j, _gap in pre[i]:
                if k[j] >= x:
                    x = k[j] + 1e-3
            k[i] = x
        return [i for _x, i in sorted(zip(k, range(n)))]
    top, left, post = [0] * n, [len(p) for p in fpre], [[] for _ in range(n)]
    for i in range(n):
        for j, _gap in fpre[i]:
            post[j].append(i)
    todo = [i for i in range(n) if not left[i]]
    for m, i in enumerate(todo):
        top[i] = m
        for k in post[i]:
            left[k] -= 1
            if not left[k]:
                todo.append(k)
    kinds = {}
    kind = [kinds.setdefault((o["e"], o["w"][0][0] if o["e"][0] == "p" else o["w"][0][0].rstrip("0123456789"), o["w"][0][1] // 128), len(kinds)) for o in ops]
    cut = [1e9]
    soon = [-SOON if o["t"] < 0 and o["w"][0][0] not in ("recf", "ht", "nxt") else 0.0 for o in ops]

    def both(key):
        back = place(ranked([-x for x in key], bpre), bpre, dur, eng, ne, tail)
        late = [soon[i] - back[i] - dur[i] for i in range(n)]
        return late, place(ranked(late, fpre), fpre, dur, eng, ne, zero)
    def held(order, case):
        d, pre = case
        start, why, free, prev, end, last = [0.0] * n, [-1] * n, [0.0] * ne, [-1] * ne, 0.0, 0
        for i in order:
            t, b = free[eng[i]], prev[eng[i]]
            for j, gap in pre[i]:
                if start[j] + gap >= t:
                    t, b = start[j] + gap, j
            start[i], why[i], prev[eng[i]] = t, b, i
            t += d[i]
            free[eng[i]] = t
            if t + tail[i] > end:
                end, last = t + tail[i], i
        res = []
        while why[last] >= 0:
            if why[last] not in deps[last]:
                res.append((why[last], last))
            last = why[last]
        return res
    like = {}
    for i, o in enumerate(ops):
        like.setdefault(o["like"], []).append(i)
    heads = [like[(("a", "X"), 1, 0)][0]] + like[(("a", "X"), 1, 1)]
    start = place(todo, fpre, dur, eng, ne, zero)
    best, low, cur, pairs = None, 0.0, 0.0, []
    fresh, kept = start, start
    for it in range(ROUNDS):
        if it and it % TRY == 0 and it <= TRY * TRIES:
            start, cur, cut[0] = (fresh, 1e9, 1e9) if it < TRY * TRIES else (kept, low, 1e9)
        way = rnd() if it > 8 else 1.0
        if way < PAIR:
            j, i = pairs[int(rnd() * len(pairs))]
            key = list(start)
            by = start[i] - start[j] + 1.0 + (500.0 * rnd() if rnd() < 0.3 else 0.0)
            m, by = (i, -by) if rnd() < 0.5 else (j, by)
            for x in (like[ops[m]["like"]] if rnd() < 0.6 else [m]):
                key[x] += by
            new = place(ranked(key, fpre), fpre, dur, eng, ne, zero)
        else:
            key = [start[i] + dur[i] for i in range(n)]
            if way < MOVES[0]:
                pick, by = int(rnd() * len(kinds)), NOISE * (2 * rnd() - 1)
                key = [x + by if kind[i] == pick else x for i, x in enumerate(key)]
            elif way < MOVES[1]:
                a, b = 1 + int(2 * rnd()), 1 + int(3 * rnd())
                by = key[heads[b]] - key[heads[a]]
                for grp in like.values():
                    src = [i for i in grp if ops[i]["t"] == a]
                    for i in grp:
                        if src and ops[i]["t"] == b:
                            key[i] = key[src[0]] + by
            elif way < MOVES[2]:
                mid, amp = 20000.0 * rnd() - 5000.0, NOISE * rnd()
                for grp in like.values():
                    by = amp * rnd()
                    for i in grp:
                        if ops[i]["t"] > 0 and abs(key[i] - key[heads[ops[i]["t"]]] - mid) < WIDE:
                            key[i] += by
            elif it > 8:
                mid, amp = rnd() * max(key), NOISE * rnd()
                key = [x + amp * rnd() if abs(x - mid) < WIDE else x for x in key]
            late, new = both(key)
        order = [i for _x, _y, i in sorted(zip(new, top, range(n)))]
        one = length(order, cases[:1])
        if one > cut[0] + 1000.0:
            continue
        val = (one + length(order, cases[1:])) / len(cases)
        if best is None or val <= cur + HEAT * (1.0 - it / ROUNDS) * rnd():
            start, cur, cut[0] = new, val, one
            if PAIR:
                pairs = held(order, cases[1]) + held(order, cases[int(rnd() * len(cases))])
            if best is None or val < low:
                best, low, kept = order, val, new
    after = [set(j for j, _gap in p) for p in bpre]

    def swap(order, j, i, ahead):
        a, b = order.index(j), order.index(i)
        if a > b:
            return order
        part = order[a:b + 1] if ahead else order[a:b + 1][::-1]
        tie = deps if ahead else after
        need, engs, up = set(tie[part[-1]]), set(), [part[-1]]
        for k in reversed(part[:-1]):
            if k in need or eng[k] in engs:
                if eng[k] == eng[i]:
                    return order
                up.append(k)
                need.update(tie[k])
                engs.add(eng[k])
        moved = set(up)
        part = up[::-1] + [k for k in part if k not in moved]
        return order[:a] + (part if ahead else part[::-1]) + order[b + 1:]
    order, cur, one = best, low, length(best, cases[:1])
    pairs = held(order, cases[0]) + held(order, cases[2])
    for it in range(SWAPS):
        j, i = pairs[int(rnd() * len(pairs))]
        ahead, new = rnd() < 0.5, order
        twins = [(x, y) for x in like[ops[j]["like"]] for y in like[ops[i]["like"]] if ops[x]["t"] - ops[y]["t"] == ops[j]["t"] - ops[i]["t"]]
        for x, y in (twins if rnd() < 0.5 else [(j, i)]):
            new = swap(new, x, y, ahead)
        if new is order:
            continue
        two = length(new, cases[:1])
        if two > one + 500.0:
            continue
        val = (two + length(new, cases[1:])) / len(cases)
        if val <= cur + WARM * (1.0 - it / SWAPS) * rnd():
            order, cur, one = new, val, two
            pairs = held(order, cases[0]) + held(order, cases[1 + int(rnd() * (len(cases) - 1))])
            if val < low:
                best, low = order, val
    return best, low


ORDERS = {}


def orders(g, core, T, topo):
    if not ORDERS:
        parts = [build(g, core, T, topo, rank)[0] for rank in range(len(T.cores))]
        ops = [dict(x[0], dur=max(o["dur"] for o in x)) for x in zip(*parts)]
        deps = [{j: any(d.get(j, False) for d in x) for j in set().union(*x)} for x in zip(*[depend(p) for p in parts])]
        ORDERS["all"] = (ops, deps, arrange(ops, deps))
    return ORDERS["all"][2][0]


def rank_program(g, core, T, topo):
    rank = T.rank_of(core)
    if rank is None:
        return
    ops, Q = build(g, core, T, topo, rank)
    deps = depend(ops)
    order = orders(g, core, T, topo)
    count = {}
    mark = {}
    seen = {}
    for i in order:
        o = ops[i]
        e = o["e"]
        sem = o["sem"] or ENG_SEM[e]
        if e != "r":
            need = {}
            for j, w in deps[i].items():
                if w and mark[j][0] != "none":
                    need[mark[j][0]] = max(need.get(mark[j][0], 0), mark[j][1])
            for s, c in need.items():
                if seen.get((e, s), 0) < c:
                    Q[e].wait_ge(T.sem[s], c)
                    seen[(e, s)] = c
            h = o["fn"]()
            if sem != "none":
                h.then_inc(T.sem[sem], o["inc"])
        count[sem] = count.get(sem, 0) + o["inc"]
        mark[i] = (sem, count[sem])
    count["sent"] = 2 * (RO - 1) * sum(len(lanes(topo, T.cores, rank, q)) for q in range(4) if q != rank)
    for s, c in count.items():
        if s != "none":
            g.wait_ge(T.sem[s], c)
